import numpy as np, ml_dtypes
CORES = [35,38,43,46]
N = 4
BF = ml_dtypes.bfloat16
def gentries(a):
    return np.ascontiguousarray(a.reshape(8, 16, -1).transpose(0, 2, 1)).reshape(8, -1)
def gtable(e):
    e = np.asarray(e); return np.ascontiguousarray(e.reshape(8, -1, 16).transpose(0, 2, 1)).reshape(128, -1).astype(np.int32)
W, F, FC, LM, CAP, TS, LB, RO = 3456, 256, 512, 32, 64, 2048, 2, 3
WT = 255 - 14 * np.arange(16)
M = 8
def pick(t, ix):
    return np.take_along_axis(t, ix[:, :, None, :], 3)
def letters(rng, uneven):
    C = W // M; A = C // 4; hc = (A // 2) * 4; hw = hc * M
    if uneven:
        v = (np.floor(np.exp2(8 * rng.random((N, 8, 1, C))) * rng.random((N, 8, 16, C))) * (rng.random((N, 8, 1, C)) > 0.0625)).astype(np.int64)
        q = (np.floor(np.exp2(8 * rng.random((N, 8, 1, W))) * rng.random((N, 8, 16, W))) * (rng.random((N, 8, 1, W)) > 0.0625)).astype(np.int64)
    else:
        v = rng.integers(0, 256, (N, 8, 16, C)); q = rng.integers(0, 256, (N, 8, 16, W))
    base = rng.integers(0, C, (N, 8, A, 16)); base[:, :, :A // 2] %= hc
    alt = rng.integers(0, C, (N, 8, C, 16)); alt[:, :, :hc] %= hc
    seq = np.repeat(base, 4, axis=2); seq = np.where(rng.random(seq.shape) < 0.08, alt, seq)
    blk = np.repeat(np.add.accumulate((rng.random((N, 8, A, 16)) < 0.6).astype(np.int64), axis=3), 4 * M, axis=2)
    loose = np.take_along_axis(rng.random((N, 8, W, 17)), blk, 3) < rng.choice(np.array([0.15, 0.3, 0.5]), (N, 8, 1, 1))
    order = np.argsort(blk + np.where(loose, rng.random(blk.shape), 0.0625 * np.arange(16)), axis=3)
    mem = np.repeat(rng.integers(0, M, (N, 8, A, 16)), 4 * M, axis=2)
    mem = np.where(rng.random(mem.shape) < rng.choice(np.array([0.02, 0.06, 0.15, 0.4]), (N, 8, 1, 1)), rng.integers(0, M, mem.shape), mem)
    kid = np.take_along_axis(np.repeat(seq, M, axis=2) * M + mem, order, 3)
    v[:, :, :, :hc] = v[:1, :, :, :hc].copy(); q[:, :, :, :hw] = q[:1, :, :, :hw].copy(); kid[:, :, :hw] = kid[:1, :, :hw].copy()
    return np.repeat(v, M, axis=3), q, kid
def front(rng, skew):
    A = W // (4 * M)
    st = rng.random((N, 8, F)) < rng.choice(np.array([0.3, 0.5, 0.8]), (N, 8, 1)); st[:, :, 0] = True
    st = st.astype(np.int64); sid = np.add.accumulate(st, axis=2) - 1
    fam = (A * rng.random((N, 8, F)) ** (3 if skew else 1)).astype(np.int64)
    fam = np.take_along_axis(np.where(rng.random(fam.shape) < 0.7, fam % (A // 2), fam), sid, 2)
    c = fam * 4 + rng.integers(0, 4, fam.shape); m = rng.integers(0, M, fam.shape)
    o = np.argsort(sid + 0.99 * rng.random(fam.shape), axis=2)
    mv = np.where(rng.random(fam.shape) < 0.3, np.take_along_axis(m, o, 2), rng.integers(0, M, fam.shape))
    fv = np.take_along_axis(c, o, 2) * M + mv
    return c * M + m, np.where(rng.random(fam.shape) < 0.04, rng.integers(0, W, fam.shape), fv), st
def mix(rng, v, q, kid, fu, fv):
    pm = np.argsort(rng.random((N, 8, W)), axis=2); inv = np.argsort(pm, axis=2)
    k = np.take_along_axis(pm, kid.reshape(N, 8, 16 * W), 2).reshape(N, 8, W, 16)
    k = np.ascontiguousarray(np.take_along_axis(k, inv[:, :, :, None], 2).transpose(0, 1, 3, 2))
    return pick(v, inv), pick(q, inv), k, np.take_along_axis(pm, fu, 2), np.take_along_axis(pm, fv, 2)
def pack(v, q, k, fu, fv, st):
    return {"vec": v.reshape(N, 128, W).astype(np.float32).astype(BF), "mark": q.reshape(N, 128, W).astype(np.float32).astype(BF), "kids": np.ascontiguousarray(k.reshape(N, 128, W)).astype(np.int32),
            "fu": np.stack([gtable(a) for a in fu]), "fv": np.stack([gtable(a) for a in fv]), "fs": np.ascontiguousarray(st).astype(np.int32)}
def setup_inputs(rng):
    v, q, kid = letters(rng, False); fu, fv, st = front(rng, False)
    return pack(*mix(rng, v, q, kid, fu, fv), st)
def setup_inputs_room(rng):
    v = np.zeros((N, 8, 16, W), np.int64); q = np.zeros((N, 8, 16, W), np.int64); k = np.zeros((N, 8, 16, W), np.int64)
    fu = np.zeros((N, 8, F), np.int64); fv = np.zeros((N, 8, F), np.int64); st = np.zeros((N, 8, F), np.int64); st[:, :, 0] = 1
    for r in range(N):
        for g in range(8):
            o = rng.permutation(W); z0 = o[2 * F]; rest = o[2 * F + 1:]
            b = rng.integers(0, 2, W); b[z0] = 0; i = int(rng.integers(0, 16))
            v[r, g] = rng.integers(0, 128, (16, 1)); v[r, g, i] += b * int(rng.integers(1, 128))
            own = rng.integers(0, N, W); w = rng.integers(0, 256, (16, W)); w[0] -= w[0] % N; w[0] += (WT @ w - own) % N; w[:, z0] = 0; q[r, g] = w
            pool = [rest[(own[rest] == a) & (b[rest] == 0)] for a in range(N)]; zero = rest[b[rest] == 0]; ones = rest[b[rest] == 1]
            pu = rng.choice(rest, 16 * F); pv = pu.copy(); mode = g if g in (2, 3) else (0, 1, 0, 4)[(r + g) % 4]
            if mode in (0, 1):
                if mode == 0:
                    n = rng.choice(np.array([0, 1, CAP - 1, CAP, CAP + 1, CAP + 8]), N)
                    if r == 0: n[1] = CAP
                    x = rng.permutation(np.concatenate([np.resize(rng.permutation(pool[a]), int(n[a])) for a in range(N)]))
                else:
                    a = rng.permutation(N)
                    x = np.concatenate([np.resize(rng.permutation(pool[a[0]]), FC - 2), np.resize(rng.permutation(pool[a[1]]), 5)])
                t = np.sort(rng.permutation(16 * F)[:len(x)])
                pu[t] = x; pv[t] = z0
            elif mode in (2, 3):
                t = int(rng.integers(0, 8))
                for n in ([LM + 1] + [LM] * (F // LM) + [1] if mode == 2 else [LM] * (F // LM - 1) + [LM - 1, 2, 1, 1]):
                    if n == 1:
                        pu[t] = rng.choice(zero); pv[t] = z0
                    else:
                        pu[t] = rng.choice(zero); pv[t] = rng.choice(ones); pu[t + n - 1] = rng.choice(ones); pv[t + n - 1] = rng.choice(zero)
                    t += n + int(rng.integers(0, 4))
            else:
                lu, lv, lx, ly = int(o[0]), int(o[F]), int(rest[0]), int(rest[1])
                j = 13 if r == 0 else 0 if r == 1 else int(rng.integers(0, 14))
                for c in (lv, lx, ly): v[r, g, :, c] = v[r, g, :, lu]
                q[r, g, j:j + 3, lu] = np.minimum(np.maximum(q[r, g, j:j + 3, lu], 2), 254)
                q[r, g, :, lx] = q[r, g, :, lu]; q[r, g, j:j + 3, lx] += np.array([1, -2, 1])
                q[r, g, :, lv] = 0; q[r, g, :, ly] = 0
                pu[0] = lu; pv[0] = lv; pu[1] = lx; pv[1] = ly
            kk = rng.choice(rest, (16, W)); kk[:, o[:F]] = pu.reshape(F, 16).T; kk[:, o[F:2 * F]] = pv.reshape(F, 16).T
            k[r, g] = kk; fu[r, g] = o[:F]; fv[r, g] = o[F:2 * F]
    return pack(v, q, k, fu, fv, st)
def swing(rng, pu, pv, t, n, low, high):
    x, y = (pu, pv) if rng.random() < 0.5 else (pv, pu)
    x[t] = rng.choice(low); y[t] = rng.choice(high); x[t + n - 1] = rng.choice(high); y[t + n - 1] = rng.choice(low)
def setup_inputs_deep(rng):
    v = np.zeros((N, 8, 16, W), np.int64); q = np.zeros((N, 8, 16, W), np.int64); k = np.zeros((N, 8, 16, W), np.int64)
    fu = np.zeros((N, 8, F), np.int64); fv = np.zeros((N, 8, F), np.int64); st = np.zeros((N, 8, F), np.int64); st[:, :, 0] = 1
    P = 16 * F; C = (LM + 15) // 16
    for r in range(N):
        for g in range(8):
            mode = (r + g) % 4; o = rng.permutation(W); z0 = int(o[2 * F]); rest = o[2 * F + 1:]
            b = rng.integers(0, 3, W) if mode > 1 else rng.integers(0, 2, W) * mode
            b[z0] = 0
            half = 8 * int(rng.integers(0, 2)); m = rng.random((16, 1)) < 0.4; m[np.arange(16) // 8 * 8 != half] = False; m[half + int(rng.integers(0, 8))] = True
            j = 8 - half + int(rng.integers(0, 6)); tri = np.zeros((16, 1), np.int64); tri[j:j + 3, 0] = int(rng.integers(1, 33)) * np.array([1, -2, 1])
            two = m.astype(np.int64) if mode == 2 else tri
            v[r, g] = np.where(m, 0, rng.integers(64, 128, (16, 1))) + 255 * m.astype(np.int64) * (b == 1) + two * (b == 2)
            own = rng.integers(0, N, W); w = rng.integers(0, 256, (16, W)); w[0] -= w[0] % N; w[0] += (WT @ w - own) % N; w[:, z0] = 0; q[r, g] = w
            pool = [rest[(own[rest] == a) & (b[rest] == 0)] for a in range(N)]; kind = [rest[b[rest] == c] for c in range(3)]
            pu = rng.choice(rest, P); pv = pu.copy(); kk = rng.choice(rest, (16, W)); a = rng.permutation(N); a0 = int(a[0]); a1 = int(a[1])
            if mode == 0:
                heads = rest[:64]; t = np.sort(rng.permutation(P)[:64]); pu[t] = heads; pv[t] = z0
                n0 = FC // 16 + (16 if g < 4 else 0)
                kk[:, z0] = z0; kk[:, heads[:n0]] = rng.choice(pool[a0], (16, n0)); kk[:, heads[n0:]] = rng.choice(pool[a1], (16, 64 - n0))
            elif mode == 1:
                t = int(rng.integers(0, 4))
                for n in range(8):
                    swing(rng, pu, pv, t, LM + 1, kind[0], kind[1]); t += LM + 1 + int(rng.integers(0, 4))
                x = np.concatenate([np.resize(rng.permutation(pool[a0]), FC - 16), np.resize(rng.permutation(pool[a1]), 20)])
                i = t + np.sort(rng.permutation(P - t)[:len(x)]); pu[i] = x; pv[i] = z0
            elif mode == 2:
                x, y = (pu, pv) if r % 2 == 0 else (pv, pu)
                t = int(rng.integers(0, 8))
                x[t:t + 257] = rng.choice(kind[1], 257); x[t + 257] = rng.choice(kind[2]); y[t:t + 258] = rng.choice(kind[0], 258); t += 258
                i = t + np.sort(rng.permutation(800)[:24]); pu[i] = rng.choice(kind[0], 24); pv[i] = z0; t += 800
                y[t:t + 257] = rng.choice(kind[1], 257); y[t + 257] = rng.choice(kind[2]); x[t:t + 258] = rng.choice(kind[0], 258); t += 258
                while t + LM + 16 < P:
                    t += int(rng.integers(0, 16)); n = int(rng.integers(2, LM + 1))
                    swing(rng, pu, pv, t, n, kind[0], kind[int(rng.integers(1, 3))]); t += n
            else:
                s = int(rng.integers(1, 6)); e = F - 4 * C
                st[r, g, s] = 1; st[r, g, e + C * np.arange(4)] = 1
                i = int(rng.integers(0, 16 * s)); pu[i] = rng.choice(kind[0]); pv[i] = rng.choice(kind[1])
                t = 16 * s
                while t + LM + 48 < 16 * e:
                    t += int(rng.integers(0, 48))
                    if rng.random() < 0.5:
                        pu[t] = rng.choice(kind[0]); pv[t] = z0; t += 1
                    else:
                        n = int(rng.integers(2, LM + 1)); swing(rng, pu, pv, t, n, kind[0], kind[2]); t += n
                for c in range(4):
                    i = 16 * (e + C * (c + 1)); x, y = (pv, pu) if c < 3 else (pu, pv)
                    x[i - LM:i] = rng.choice(kind[1], LM); y[i - LM:i] = rng.choice(kind[0], LM)
            kk[:, o[:F]] = pu.reshape(F, 16).T; kk[:, o[F:2 * F]] = pv.reshape(F, 16).T
            k[r, g] = kk; fu[r, g] = o[:F]; fv[r, g] = o[F:2 * F]
    return pack(v, q, k, fu, fv, st)
def setup_inputs_ends(rng):
    v, q, kid = letters(rng, False); fu, fv, st = front(rng, False)
    v, q, k, fu, fv = mix(rng, v, q, kid, fu, fv)
    st[:, 0] = 1; st[:, 1] = 0
    two = np.array([0, W - 1]); few = np.array([0, 1, W - 1])
    fu[:, 2] = rng.choice(two, (N, F)); fv[:, 2] = rng.choice(two, (N, F)); k[:, 2, :, 0] = rng.choice(few, (N, 16)); k[:, 2, :, W - 1] = rng.choice(few, (N, 16))
    for r in range(N):
        i = int(rng.integers(0, 16)); x = v[r, 3, i].copy(); v[r, 3] = 7; v[r, 3, i] = x
    v[:, 4] = 255 * (np.arange(W) >= W // 2); k[:, 4] = rng.integers(0, W // 2, (N, 16, W)) + (W // 2) * (np.arange(W) % 2 == 0)
    even = 2 * rng.integers(0, W // 2, (N, F)); odd = 2 * rng.integers(0, W // 2, (N, F)) + 1
    fu[:, 4] = even; fv[:, 4] = odd; fu[1::2, 4] = odd[1::2]; fv[1::2, 4] = even[1::2]; st[:, 4] = 0; st[:, 4, F - 4:] = 1
    fv[:, 5] = rng.integers(0, W, (N, F)); st[:, 5] = np.arange(F) % 3 != 1
    fv[:, 6] = fu[:, 6]; fv[:, 6, F - 1] = (fu[:, 6, F - 1] + 1 + rng.integers(0, W - 1, N)) % W
    q[:, 7] = 0; q[1::2, 7] = 255
    st[:, :, 0] = 1
    return pack(v, q, k, fu, fv, st)
def setup_inputs_alike(rng):
    v, q, kid = letters(rng, False); fu, fv, st = front(rng, False)
    v[:] = v[:1].copy(); q[:] = q[:1].copy(); kid[:] = kid[:1].copy()
    for x in (fu, fv, st):
        for r in range(1, N):
            x[r, ::2] = x[0, ::2]; x[r, 1::2] = np.roll(x[0, 1::2], r * (F // N), axis=1)
    st[:, :, 0] = 1
    return pack(*mix(rng, v, q, kid, fu, fv), st)
def setup_inputs_spread(rng):
    v, q, kid = letters(rng, True); fu, fv, st = front(rng, True)
    return pack(*mix(rng, v, q, kid, fu, fv), st)
def check_inputs(d):
    bad = []
    for k, hi in (("vec", 255), ("mark", 255), ("kids", W - 1), ("fu", W - 1), ("fv", W - 1), ("fs", 1)):
        a = np.asarray(d[k]).astype(np.float32)
        if not np.all((a >= 0) & (a <= hi) & (a == np.floor(a))): bad.append("range of " + k)
    if not np.all(np.asarray(d["fs"])[:, :, 0] == 1): bad.append("first place of fs")
    return bad
def reference(vec, mark, kids, fu, fv, fs):
    vt = vec.astype(np.float32).astype(np.int64).reshape(N, 8, 16, W); qt = mark.astype(np.float32).astype(np.int64).reshape(N, 8, 16, W); kt = kids.astype(np.int64).reshape(N, 8, 16, W)
    u = np.stack([gentries(a) for a in fu]).astype(np.int64); v = np.stack([gentries(a) for a in fv]).astype(np.int64); st = fs.astype(np.int64)
    store = np.full((N, 8, 16, TS), -1, np.int64)
    for rnd in range(RO):
        a = pick(kt, u).transpose(0, 1, 3, 2).reshape(N, 8, 16 * F); b = pick(kt, v).transpose(0, 1, 3, 2).reshape(N, 8, 16 * F)
        d = np.add.accumulate(pick(vt, a) - pick(vt, b), axis=3)
        s0 = 16 * np.repeat(np.maximum.accumulate(np.where(st == 1, np.arange(F), 0), axis=2), 16, axis=2)
        d = d - np.where((s0 > 0)[:, :, None, :], pick(d, np.maximum(s0 - 1, 0)), 0)
        last = np.zeros((N, 8, F, 16), bool); last[:, :, F - 1, 15] = True; last[:, :, :F - 1, 15] = st[:, :, 1:] == 1
        cut = np.all(d == 0, axis=2) | last.reshape(N, 8, 16 * F)
        e = np.maximum(pick(qt, a), pick(qt, b)) + d; run = np.add.accumulate(e, axis=3)
        fac = {}
        for r in range(N):
            for g in range(8):
                t1 = np.flatnonzero(cut[r, g]); t0 = np.concatenate([np.zeros(1, np.int64), t1[:-1] + 1]); ln = t1 - t0 + 1
                c = np.flatnonzero((ln <= LM) & ~((ln == 1) & (a[r, g, t0] == b[r, g, t0])))[:FC]
                t0 = t0[c]; t1 = t1[c]; ln = ln[c]
                z = (run[r, g][:, t1] - run[r, g][:, t0] + e[r, g][:, t0]) & 255
                h = (WT @ z) & (N * TS - 1)
                fac[r, g] = (t0, ln, z, h & (N - 1), h >> LB, np.zeros(len(c), bool))
        for o in range(N):
            for g in range(8):
                ix = [np.flatnonzero(fac[r, g][3] == o)[:CAP] for r in range(N)]
                zz = np.concatenate([fac[r, g][2][:, ix[r]] for r in range(N)], axis=1); pp = np.concatenate([fac[r, g][4][ix[r]] for r in range(N)])
                i = np.flatnonzero(np.any(store[o, g][:, pp] != zz, axis=0))
                win = i[np.unique(pp[i], return_index=True)[1]]
                store[o, g][:, pp[win]] = zz[:, win]
                new = np.zeros(len(pp), bool); new[win] = True; n = 0
                for r in range(N):
                    fac[r, g][5][ix[r]] = new[n:n + len(ix[r])]; n += len(ix[r])
        u = np.zeros((N, 8, F), np.int64); v = np.zeros((N, 8, F), np.int64); st = np.ones((N, 8, F), np.int64)
        for r in range(N):
            for g in range(8):
                t0, ln, z, o, p, new = fac[r, g]
                n = np.flatnonzero(new); to = np.add.accumulate(ln[n]); n = n[to <= F]; j = 0
                for x in n:
                    L = int(ln[x]); t = int(t0[x])
                    u[r, g, j:j + L] = a[r, g, t:t + L]; v[r, g, j:j + L] = b[r, g, t:t + L]; st[r, g, j + 1:j + L] = 0; j += L
    return {"yt": store.reshape(N, 128, TS).astype(np.float32).astype(BF), "yu": u.astype(np.float32), "yv": v.astype(np.float32), "ys": st.astype(np.float32)}

@@ -1,0 +1,591 @@
+import math
+from concourse.bass import DstId, RemoteDMATransfer
+from concourse.mybir import AluOpType, AxisListType, ActivationFunctionType
+
+A = AluOpType
+AF = ActivationFunctionType
+W, F, FC, CAP, TS, RO = 3456, 256, 512, 64, 2048, 3
+P = 16 * F
+MAG = float(2 ** 27)
+RND = float(2 ** 23)
+CH = [(0, 512), (512, 512), (1024, 1024), (2048, 1024), (3072, 512), (3584, 512)]
+ORDER = "BABABABABABAABAAABAB"
+TW = 288
+SD = 2064
+SW = SD + 256
+
+
+def shapes(kind, dtype, text):
+    return {w.split(":")[0]: (kind, [128, int(w.split(":")[1])], dtype) for w in text.split()}
+
+
+SCRATCH = {}
+SCRATCH.update(shapes("sbuf", "int32", "KID:3456 FUI:32 FSI:256 ZI:512 Z8:512 HI:32 OW:32 HT:16 HP:16 HR:256 RI:256 CI:1280"))
+SCRATCH.update(shapes("sbuf", "uint16", "FUV:32 KU:512 OPU:16 JT:32 T1:32 OFF:32 PU:16 R1:256 SU:16 OF2:32 CT:16 EXL:16"))
+SCRATCH.update(shapes("sbuf", "bfloat16", "VEC:3456 MRK:3456 FSB:256 NF:264 LASTF:256 EQ:256 KH:576 KL:576 MF:4096 VV:4096 DF:4096 AB:4096 "
+                      "NS:4112 QV:4096 MQ:4096 CU:264 CV:256 CB:256 CD:264 XL:256 L2B:8 JW:768 JK:512 OO:512 LL:512 ZB:512 OHB:132 "
+                      "STO:2320 NQ:256 ED:256 EO:1920 NK:512 NL:40 KB:32 H:256 M2:256 YH:512 YL:512 CM:4096 JR:256 "
+                      "SND:2304 ARR:768 NEW:768 RPL:2304"))
+SCRATCH.update(shapes("sbuf", "float32", "KF:512 D:4096 EM:4096 LG:256 XLI:256 SC:256 XC:256 T0:512 SN:132 RA:132 RB:132 R2:66 RQ:40 "
+                      "RM:256 UH:256 NXT:768 NFX:256 FM:256 FL:256 PP:256 MD:256 OUTF:768 CF:1280 CR:1792 SM:976"))
+VIEW = {}
+for _w in ("L2:16 LT:8 PN:16 OP1:16 OP2:16 OP3:16 LEN:32 INV:32 OV:32 D2:32 O1:32 O2:32 O3:32 O4:32 IV:16 PF:16 P1:16 PM1:16 S1:16 "
+           "S2:16 S3:16 NP:32 NP2:32 SF:32 ST:32 EN:32 PE1:32 X1:32 X2:32 KP:32 W0:32 VT:32 TOT:8 TOB:8 X3:32").split():
+    _n, _k = _w.split(":")
+    VIEW[_n] = ("SM", sum(x[2] for x in VIEW.values()), int(_k))
+BANKS = ("BA", "BB", "BC", "BD", "BE", "BF", "BG", "BH")
+SCRATCH.update({b: ("psum", [128, 512], "float32") for b in BANKS})
+SEMAPHORES = ["qv", "qs", "qt", "qg"] + ["ld%d" % k for k in range(9)] + ["st%d" % k for k in range(4)] + ["ac%d" % k for k in range(len(CH))] + \
+             ["%s%d" % (s, r) for s in ("ka", "ra", "lk", "lr") for r in range(RO)]
+
+
+def rank_program(g, core, T, topo):
+    me = T.rank_of(core)
+    if me is None:
+        return
+    cores = list(T.cores)
+    N = len(cores)
+
+    def masks(src):
+        s = cores[src]
+        out = [d for d in range(N) if d != src and topo.chip(cores[d]) != topo.chip(s)]
+        on = [d for d in range(N) if d != src and topo.chip(cores[d]) == topo.chip(s)]
+        res = {}
+        used = []
+        for ds in (out, on):
+            if ds:
+                lst = [e for e in topo.engines(s, cores[ds[0]]) if e not in used]
+                n = 1
+                while n * 2 * len(ds) <= len(lst):
+                    n *= 2
+                for x, d in enumerate(ds):
+                    res[d] = lst[x * n:(x + 1) * n]
+                    used = used + res[d]
+        return res
+
+    queues = {"v": g.vector, "s": g.scalar, "t": g.tensor, "g": g, "y": g.sync}
+    count = {}
+    known = {q: {} for q in queues}
+    waited = {}
+    recs = {}
+    finals = {}
+
+    def dowaits(q, reads, writes):
+        best = {}
+        for regs, wr in ((reads, False), (writes, True)):
+            for (b, lo, hi) in regs:
+                for rec in recs.get(b, []):
+                    if rec[0] < hi and lo < rec[1] and (wr or rec[2]):
+                        s, v = rec[3]
+                        if known[q].get(s, 0) < v and best.get(s, (0, None))[0] < v:
+                            best[s] = (v, rec[4])
+        for s in sorted(best, key=lambda s: -sum(best[s][1].values())):
+            v, clk = best[s]
+            if known[q].get(s, 0) >= v:
+                continue
+            queues[q].wait_ge(T.sem[s], v)
+            waited[s] = max(waited.get(s, 0), v)
+            known[q][s] = v
+            for a, b in clk.items():
+                known[q][a] = max(known[q].get(a, 0), b)
+
+    def note(q, tok, reads, writes):
+        clk = dict(known[q])
+        clk[tok[0]] = max(clk.get(tok[0], 0), tok[1])
+        for (b, lo, hi) in writes:
+            recs[b] = [r for r in recs.get(b, []) if not (lo <= r[0] and r[1] <= hi)] + [(lo, hi, True, tok, clk)]
+        for (b, lo, hi) in reads:
+            recs[b] = [r for r in recs.get(b, []) if not (r[0] == lo and r[1] == hi and not r[2] and r[3][0] == tok[0])] + [(lo, hi, False, tok, clk)]
+        finals[tok[0]] = max(finals.get(tok[0], 0), tok[1])
+
+    def bankfix(reads, writes):
+        w = [(x[0], 0, 512) if x[0] in BANKS else x for x in writes] + [(x[0], 0, 512) for x in reads if x[0] in BANKS]
+        return [x for x in reads if x[0] not in BANKS], w
+
+    def op(q, fn, reads, writes):
+        reads, writes = bankfix(reads, writes)
+        dowaits(q, reads, writes)
+        s = "q" + q
+        fn().then_inc(T.sem[s], 1)
+        count[s] = count.get(s, 0) + 1
+        note(q, (s, count[s]), reads, writes)
+
+    def dma(q, sem, out, in_):
+        dowaits(q, in_[1], out[1])
+        queues[q].dma_start(out=out[0], in_=in_[0]).then_inc(T.sem[sem], 16)
+        note(q, (sem, 16), in_[1], out[1])
+
+    def addto(out, in_, sem):
+        dowaits("g", in_[1], out[1])
+        g.dma_start(out=out[0], in_=in_[0], accum_op=A.add).then_inc(T.sem[sem], 16)
+        count[sem] = count.get(sem, 0) + 16
+        note("g", (sem, count[sem]), in_[1], out[1])
+
+    def R(name, lo=None, hi=None, step=None, p=None):
+        if name in VIEW:
+            name, at, n = VIEW[name]
+            lo, hi = (at, at + n) if lo is None else (at + lo, at + hi)
+        t = T[name]
+        if lo is None:
+            lo, hi = 0, t.shape[1]
+        if p is not None:
+            ap = t[p[0]:p[1], lo:hi]
+        else:
+            ap = t[:, lo:hi] if step is None else t[:, lo:hi:step]
+        return (ap, [(name, lo, hi)])
+
+    def I(win, off):
+        return (win[0].indirect(off[0]), win[1] + off[1])
+
+    def rg(*xs):
+        return [r for x in xs if isinstance(x, tuple) for r in x[1]]
+
+    def va(x):
+        return x[0] if isinstance(x, tuple) else x
+
+    def copy(out, in_):
+        op("v", lambda: g.vector.tensor_copy(out=out[0], in_=in_[0]), rg(in_) + out[1][1:], out[1][:1])
+
+    def tt(out, a, b, o):
+        op("v", lambda: g.vector.tensor_tensor(out=out[0], in0=a[0], in1=b[0], op=o), rg(a, b), out[1])
+
+    def ts(out, a, s1, o1, s2=None, o2=None):
+        if o2 is None:
+            op("v", lambda: g.vector.tensor_scalar(out=out[0], in0=a[0], scalar1=va(s1), scalar2=None, op0=o1), rg(a, s1), out[1])
+        else:
+            op("v", lambda: g.vector.tensor_scalar(out=out[0], in0=a[0], scalar1=va(s1), scalar2=va(s2), op0=o1, op1=o2), rg(a, s1, s2), out[1])
+
+    def scan(out, d0, d1, init, o1, o2):
+        op("v", lambda: g.vector.tensor_tensor_scan(out=out[0], data0=d0[0], data1=d1[0], initial=va(init), op0=o1, op1=o2), rg(d0, d1, init), out[1])
+
+    def reduce(out, in_):
+        op("v", lambda: g.vector.tensor_reduce(out=out[0], in_=in_[0], axis=AxisListType.X, op=A.add), in_[1], out[1])
+
+    def fill(out, c):
+        op("v", lambda: g.vector.memset(out[0], c), [], out[1])
+
+    def act(out, in_, f, bias=0.0, scale=1.0):
+        op("s", lambda: g.scalar.activation(out=out[0], in_=in_[0], func=f, bias=va(bias), scale=va(scale)), rg(in_, bias, scale), out[1])
+
+    def mm(out, prs):
+        rd, wr = bankfix(rg(*[x for p in prs for x in p[:2]]), out[1])
+        ins = None
+        for k, p in enumerate(prs):
+            dowaits("t", rg(p[0], p[1]), wr)
+            o = p[2] if len(p) > 2 else out
+            ins = g.tensor.matmul(out=o[0], lhsT=p[0][0], rhs=p[1][0], start=(k == 0), stop=(k == len(prs) - 1))
+        ins.then_inc(T.sem.qt, 1)
+        count["qt"] = count.get("qt", 0) + 1
+        note("t", ("qt", count["qt"]), rd, wr)
+
+    def iota(out, pat, base, cm, flag=False):
+        if flag:
+            op("g", lambda: g.iota(out[0], pat, base, cm, allow_small_or_imprecise_dtypes=True), [], out[1])
+        else:
+            op("g", lambda: g.iota(out[0], pat, base, cm), [], out[1])
+
+    def gfill(out, c):
+        iota(out, [[0, out[1][0][2] - out[1][0][1]]], c, 0, True)
+
+    dma("y", "ld0", R("FUI", 0, 16), (T.fu[:], []))
+    dma("s", "ld1", R("FUI", 16, 32), (T.fv[:], []))
+    dma("s", "ld2", R("FSI", 0, 256, p=(0, 8)), (T.fs[:], []))
+    for k, (b, x) in enumerate((("KID", T.kids), ("VEC", T.vec), ("MRK", T.mark))):
+        s0, s1 = "ld%d" % (3 + 2 * k), "ld%d" % (4 + 2 * k)
+        g.sync.dma_start(out=T[b][0:64, :], in_=x[0:64, :]).then_inc(T.sem[s0], 16)
+        g.scalar.dma_start(out=T[b][64:128, :], in_=x[64:128, :]).then_inc(T.sem[s1], 16)
+        recs[b] = [(0, W, True, (s0, 16), {s0: 16}), (0, W, True, (s1, 16), {s1: 16})]
+        finals[s0] = finals[s1] = 16
+
+    free = {"CI": 0, "CF": 0, "CM": 0, "CR": 0}
+
+    def new(buf, n):
+        lo = free[buf]
+        free[buf] = lo + (n + 15) // 16 * 16
+        return R(buf, lo, lo + n)
+
+    def part(m, a, b):
+        return R(m[1][0][0], m[1][0][1] + a, m[1][0][1] + b)
+
+    def win(m, i):
+        return part(m, 15 - i, 143 - i)
+
+    pI = new("CI", 1); cI = new("CI", 144); ktI = new("CI", 32); kdI = new("CI", 16); ksI = new("CI", 16); aI = new("CI", 256); exI = new("CI", 16)
+    iota(pI, [[0, 1]], 0, 1)
+    iota(cI, [[1, 144]], 0, 0)
+    iota(ktI, [[16, 32]], 256, 0)
+    iota(kdI, [[1, 16]], 512, 0)
+    iota(ksI, [[16, 16]], SD, 0)
+    iota(aI, [[1, 256]], 0, 0)
+    iota(exI, [[1, 16]], 0, 0)
+    gfill(R("MF"), 1)
+    K1 = new("CR", 512); IQ = new("CR", 256)
+    iota(K1, [[1, 512]], -4096, 0, True)
+    iota(IQ, [[1, 256]], 0, 0, True)
+    iota(R("JR"), [[1, 16], [16, 16]], 0, 0, True)
+    gfill(R("STO"), -1)
+    gfill(R("SND", 0, 256), -1)
+    gfill(R("KH"), 0)
+    gfill(R("KL"), 0)
+    gfill(R("RPL", 256, 768), 0)
+    for r in range(1, RO):
+        gfill(R("SND", 768 * r, 768 * r + 256), -1)
+        gfill(R("RPL", 768 * r + 256, 768 * r + 768), 0)
+    pmI = new("CI", 1); pgI = new("CI", 1); cgI = new("CI", 144); cmI = new("CI", 144); amI = new("CI", 256)
+    ts(pmI, pI, 15, A.bitwise_and)
+    ts(pgI, pI, 4, A.arith_shift_right)
+    ts(cgI, cI, 4, A.arith_shift_right)
+    ts(cmI, cI, 15, A.bitwise_and)
+    PM = new("CF", 1); PG = new("CF", 1); CG = new("CF", 144); CMF = new("CF", 144); PX = new("CF", 1)
+    copy(PM, pmI); copy(PG, pgI); copy(CG, cgI); copy(CMF, cmI); copy(PX, pI)
+    BLK = new("CM", 144); C15 = new("CM", 144); MST = new("CM", 144); G8 = new("CM", 8); R8 = new("CM", 128)
+    ts(BLK, CG, PG, A.is_equal)
+    ts(C15, CMF, 15.0, A.is_equal)
+    tt(MST, BLK, C15, A.mult)
+    ts(G8, part(cI, 0, 8), PG, A.is_equal)
+    ts(R8, part(CG, 0, 128), PX, A.is_equal)
+    ts(R("FSB", 0, 256, p=(0, 8)), R("FSI", 0, 256, p=(0, 8)), -1.0, A.mult, 1.0, A.add)
+    r0 = R8[1][0][1]
+    mm(R("BA", 0, 256), [((T.CM[0:8, r0:r0 + 128], R8[1]), R("FSB", 0, 256, p=(0, 8)))])
+    fill(R("NF"), 0.0)
+    copy(R("NF", 0, 256), R("BA", 0, 256))
+    copy(R("FUV"), R("FUI"))
+    WC = new("CF", 1)
+    ts(WC, PM, -14.0, A.mult, 255.0, A.add)
+
+    def scaled(src, by, n=144):
+        m = new("CM", n)
+        act(m, part(src, 0, n), AF.Identity, 0.0, by)
+        return m
+    MSL = scaled(MST, -float(2 ** 36)); MS = scaled(MST, 0.0625); MSC = scaled(MST, 2.0 ** -8); MSW = scaled(MST, WC)
+    MS4 = scaled(MST, 4096.0); MSI = scaled(MST, PM)
+    BW = scaled(BLK, WC, 128); BN = scaled(BLK, -1.0, 128); BI = scaled(BLK, PM, 128); G8S = scaled(G8, 0.0625, 8)
+    B1 = part(BLK, 0, 128)
+    DK = new("CF", 128); TMP = new("CF", 128); TM2 = new("CF", 128); CM1 = part(CMF, 0, 128)
+    ts(DK, CM1, PM, A.subtract)
+
+    def masked(o, c):
+        m = new("CM", 128)
+        ts(TMP, DK, c, o)
+        tt(m, TMP, B1, A.mult)
+        return m
+    TRS = masked(A.is_gt, 0.0); TRI = masked(A.is_ge, 0.0); TGE = masked(A.is_le, 0.0); IDN = masked(A.is_equal, 0.0)
+    S0 = masked(A.is_equal, 1.0); S1 = masked(A.is_equal, -15.0)
+    TRN = new("CM", 128)
+    ts(TMP, IDN, 65.0, A.mult)
+    tt(TRN, TMP, TRI, A.subtract)
+    TRX = new("CM", 128)
+    ts(TMP, IDN, -4096.0, A.mult)
+    tt(TRX, TRS, TMP, A.add)
+    DA = new("CF", 128); DB = new("CF", 128)
+    R4 = new("CR", 128); R4P = new("CR", 128); C4 = new("CR", 1)
+    ts(DB, CM1, 0.0, A.is_equal)
+    ts(DA, CM1, 0.0, A.is_gt, 0.25, A.mult)
+    scan(R4, DA, DB, 0.0, A.mult, A.add)
+    ts(TMP, CM1, 0.0, A.is_gt, 4.0, A.mult)
+    scan(R4P, TMP, DB, 0.0, A.mult, A.add)
+    tt(TM2, IDN, R4P, A.mult)
+    reduce(C4, TM2)
+    A1 = new("CM", 128); A0 = new("CM", 128); A2 = new("CM", 128)
+    ts(TMP, R4, C4, A.mult, float(4 ** 16), A.mult)
+    tt(A1, TMP, B1, A.mult)
+    ts(TM2, TMP, float(4 ** 16), A.mult)
+    tt(A0, TM2, TRS, A.mult)
+    ts(TM2, TMP, float(4.0 ** -16), A.mult)
+    tt(A2, TM2, TGE, A.mult)
+    KT = new("CR", 32); KD = new("CR", 16); KS = new("CR", 16); PM16 = new("CF", 1); PM85 = new("CF", 1); ZR = new("CR", 256)
+    MK = new("CR", 256); RS = new("CR", 132); QT = new("CR", 16)
+    ts(KT, ktI, PM, A.add)
+    ts(QT, part(KT, 0, 16), -256.0, A.add)
+    ts(PM16, PM, 16.0, A.mult)
+    ts(KD, kdI, PM16, A.add)
+    ts(KS, ksI, PM, A.add)
+    ts(PM85, PM, 8.5, A.add)
+    ts(amI, aI, 15, A.bitwise_and)
+    ts(MK, amI, PM, A.is_le, 4096.0, A.mult)
+    ts(MK, MK, 1.0, A.add)
+    copy(R("EXL"), exI)
+    fill(ZR, 0.0)
+    fill(RS, 1.0)
+    for o in range(N):
+        fill(part(RS, 33 * o, 33 * o + 1), 0.0)
+    fill(R("OHB"), 0.0); fill(R("CD"), 0.0); fill(R("CU"), 0.0); fill(R("NL"), 0.0); fill(R("NS", 0, 16), 0.0)
+    ts(R("CU", 1, 2), PM, 15.0, A.is_equal)
+
+    def relay(outb, n, *parts):
+        mm(R(outb, 0, n), [(win(m, i), R(b, lo + i, lo + 16 * n, 16)) for m, b, lo in parts for i in range(16)])
+
+    def gv(c):
+        a, n = CH[c]
+        act(R("VV", a, a + n), I(R("VEC"), R("KU", 256 + a // 16, 256 + (a + n) // 16)), AF.Copy)
+
+    def gq(c):
+        a, n = CH[c]
+        act(R("QV", a, a + n), I(R("MRK"), R("KU", 256 + a // 16, 256 + (a + n) // 16)), AF.Copy)
+
+    def vphase():
+        copy(R("KU", 256, 512), I(R("KID"), R("FUV", 16, 32)))
+        copy(R("KU", 0, 256), I(R("KID"), R("FUV", 0, 16)))
+        gv(0)
+        gv(1)
+        act(R("LASTF"), R("NF", 1, 257), AF.Identity, 1.0, -1.0)
+        gfill(R("JW", 0, 512), 0)
+        copy(R("MF", 0, P, 16), R("NF", 0, 256))
+        for c, (a, n) in enumerate(CH):
+            tt(R("DF", a, a + n), I(R("VEC"), R("KU", a // 16, (a + n) // 16)), R("VV", a, a + n), A.subtract)
+            scan(R("D", a, a + n), R("MF", a, a + n), R("DF", a, a + n), R("D", a - 1, a) if a else 0.0, A.mult, A.add)
+            if c + 2 < len(CH):
+                gv(c + 2)
+            elif c + 2 == len(CH):
+                gq(0)
+            act(R("AB", a, a + n), R("D", a, a + n), AF.Abs)
+            j0, j1 = a // 16, (a + n) // 16
+            mm(R("BC", j0, j1), [(win(MST, i), R("AB", a + i, a + n, 16)) for i in range(16)] + [(win(MSL, 15), R("LASTF", j0, j1))])
+
+    def comp():
+        copy(R("KF", 256, 512), R("KU", 256, 512))
+        tt(R("EQ"), I(R("KID"), R("FUV", 0, 16)), R("KF", 256, 512), A.is_equal)
+        ts(R("CU", 2, 258), R("BC", 0, 256), 0.0, A.is_le)
+        mm(R("BD", 0, 256), [(A0, R("CU", 2, 258)), (A1, R("CU", 1, 257)), (A2, R("CU", 0, 256))])
+        mm(R("BE", 0, 256), [(S0, R("CU", 2, 258)), (S1, R("CU", 1, 257))])
+        yield
+        tt(R("CV"), R("BD", 0, 256), R("CU", 2, 258), A.min)
+        act(R("LG"), R("BD", 0, 256), AF.Ln, 0.25)
+        act(R("XLI"), R("LG"), AF.Identity, 32.1 + RND, -1.0 / math.log(4.0))
+        tt(R("CB"), R("BE", 0, 256), R("EQ"), A.mult)
+        yield
+        tt(R("CD", 1, 257), R("CV"), R("CB"), A.is_gt)
+        mm(R("BH", 0, 16), [(win(MST, a), R("CD", 1 + 16 * a, 17 + 16 * a)) for a in range(16)])
+        mm(R("BF", 0, 256), [(TRX, R("CD", 1, 257))])
+        mm(R("BG", 0, 256), [(B1, R("CD", 0, 256))])
+        yield
+        scan(R("L2"), R("BH", 0, 16), part(ZR, 0, 16), 0.0, A.add, A.add)
+        ts(R("PN"), R("BH", 0, 16), 0.0, A.is_equal, 8192.0, A.mult)
+        copy(R("L2B", 0, 1), R("L2", 15, 16))
+        tt(R("OP1"), R("BH", 0, 16), R("PN"), A.subtract)
+        mm(R("BD", 0, 1), [(TRS, R("L2B", 0, 1))])
+        yield
+        tt(R("OP2"), R("L2"), R("OP1"), A.subtract)
+        copy(R("LT", 0, 1), R("BD", 0, 1))
+        yield
+        ts(R("OP1"), R("OP2"), R("LT", 0, 1), A.add)
+        ts(R("OP2"), R("OP1"), 512.0, A.is_ge, 8192.0, A.mult)
+        tt(R("OP3"), R("OP1"), R("OP2"), A.max)
+        tt(R("OP1"), R("OP3"), KD, A.min)
+        copy(R("OPU"), R("OP1"))
+        copy(I(R("JW"), R("OPU")), R("JR"))
+        yield
+        scan(R("JK"), R("JW", 0, 512), R("JW", 0, 512), 0.0, A.max, A.max)
+        relay("BD", 32, (MS, "JK", 0))
+        scan(R("SC"), R("BG", 0, 256), ZR, 0.0, A.add, A.add)
+        yield
+        act(R("XL"), R("XLI"), AF.Identity, -RND)
+        copy(R("JT"), R("BD", 0, 32))
+        yield
+        tt(R("XC"), R("BF", 0, 256), R("SC"), A.add)
+        yield
+        tt(R("OO"), I(R("XC"), R("JT")), K1, A.is_equal)
+        tt(R("LL"), I(R("XL"), R("JT")), R("OO"), A.mult)
+        relay("BE", 32, (MST, "JK", 0), (MSI, "OO", 0))
+        relay("BF", 32, (MST, "LL", 0))
+        mm(R("BG", 0, 512), [(B1, R("JK")), (BI, R("OO")), (BN, R("LL"))])
+        yield
+        copy(R("T1"), R("BE", 0, 32))
+        copy(R("LEN"), R("BF", 0, 32))
+        ts(R("INV"), R("BF", 0, 32), 0.0, A.is_equal, 8.0, A.mult)
+        act(R("T0"), R("BG", 0, 512), AF.Identity, 9.5)
+        yield
+
+    def qphase():
+        for c in range(1, len(CH)):
+            gq(c)
+        banks = ("BA", "BB", "BC")
+        rc = 0
+        for c, (a, n) in enumerate(CH):
+            tt(R("MQ", a, a + n), I(R("MRK"), R("KU", a // 16, (a + n) // 16)), R("QV", a, a + n), A.max)
+            addto(R("D", a, a + n), R("MQ", a, a + n), "ac%d" % c)
+            for _ in range(2 if c >= 2 else 0):
+                b = banks[rc % 3]
+                mm(R(b, 0, 512), [(B1, R("AB", 512 * rc, 512 * rc + 512))])
+                act(R("NS", 512 * rc + 1, 512 * rc + 513), R(b, 0, 512), AF.Sign)
+                rc += 1
+            yield
+        tt(R("NS", 0, P, 16), R("NS", 0, P, 16), R("NF", 0, 256), A.mult)
+        yield
+        for a in range(0, P, 2048):
+            scan(R("EM", a, a + 2048), R("NS", a, a + 2048), R("D", a, a + 2048), R("EM", a - 1, a) if a else 0.0, A.mult, A.add)
+            yield
+
+    def fused(src, dst, lsem, rsem):
+        m = masks(me)
+        tr, rd, tot = [], [], 0
+        for d in range(N):
+            if d != me:
+                rid, pid = topo.addr(cores[d])[:2]
+                x = src(d)
+                rd += x[1]
+                tot += len(m[d])
+                tr.append(RemoteDMATransfer(dst_ids=[DstId(rid=rid, pnc=pid)], dma_engine_mask=sum(1 << e for e in m[d]), remote_sem=T.sem[rsem], src=x[0], dst=dst[0]))
+        dowaits("g", rd, [])
+        g.remote_dma_fused(tr, local_sem=T.sem[lsem])
+        note("g", (lsem, tot), rd, [])
+
+    def landed(sem, buf, base):
+        tot = sum(len(masks(s)[me]) for s in range(N) if s != me)
+        for s in range(N):
+            if s != me:
+                recs.setdefault(buf, []).append((base + CAP * s, base + CAP * (s + 1), True, (sem, tot), {sem: tot}))
+        finals[sem] = tot
+
+    def keys(r):
+        copy(R("ZI"), I(R("EM"), R("T1")))
+        ts(R("Z8"), R("ZI"), 255, A.bitwise_and)
+        copy(R("ZB"), R("Z8"))
+        relay("BD", 32, (MSW, "ZB", 0))
+        copy(R("HI"), R("BD", 0, 32))
+        ts(R("OW"), R("HI"), 3, A.bitwise_and)
+        tt(R("OV"), R("OW"), R("INV"), A.add)
+        for o in range(N):
+            ts(R("OHB", 33 * o + 1, 33 * o + 33), R("OV"), float(o), A.is_equal)
+        mm(R("BE", 0, 132), [(BN, R("OHB"))])
+        mm(R("BF", 0, 132), [(TRN, R("OHB"))])
+        ts(R("D2"), R("OV"), 64.0, A.mult, 64.0, A.add)
+        scan(R("SN"), RS, R("BE", 0, 132), 0.0, A.mult, A.add)
+        tt(R("RA", 1, 132), R("BF", 1, 132), R("SN", 0, 131), A.add)
+        tt(R("RB", 1, 132), R("RA", 1, 132), R("OHB", 1, 132), A.mult)
+        tt(R("R2", 1, 66), R("RB", 1, 66), R("RB", 67, 132), A.add)
+        tt(R("RQ", 1, 33), R("R2", 1, 33), R("R2", 34, 66), A.add)
+        ts(R("O1"), R("RQ", 1, 33), 0.0, A.is_le, 4096.0, A.mult)
+        tt(R("O2"), R("D2"), R("RQ", 1, 33), A.subtract)
+        tt(R("O3"), R("O2"), R("O1"), A.max)
+        tt(R("O4"), R("O3"), KT, A.min)
+        copy(R("OFF"), R("O4"))
+        b, c = 768 * r, 256 * r + CAP * me
+        copy(I(R("SND", b, b + 768), R("OFF")), R("ZB"))
+        fused(lambda d: R("SND", b + CAP * d, b + CAP * d + CAP), R("ARR", c, c + CAP), "lk%d" % r, "ka%d" % r)
+        act(R("ARR", c, c + CAP), R("SND", b + CAP * me, b + CAP * me + CAP), AF.Copy)
+        fill(R("NXT", 0, 256), 1.0)
+        copy(R("KF", 0, 256), R("KU", 0, 256))
+        for k in range(2):
+            ts(R("KH", TW * k, TW * k + 256), R("KU", 256 * k, 256 * k + 256), MAG, A.add, MAG, A.subtract)
+            tt(R("KL", TW * k, TW * k + 256), R("KF", 256 * k, 256 * k + 256), R("KH", TW * k, TW * k + 256), A.subtract)
+        landed("ka%d" % r, "ARR", 256 * r)
+
+    def owner(r):
+        b = 256 * r
+        arr = R("ARR", b, b + 256)
+        mm(R("BH", 0, 256), [(BW, arr)])
+        relay("BG", 16, (MSW, "ARR", b))
+        copy(R("HR"), R("BH", 0, 256))
+        ts(R("RI"), R("HR"), 2, A.arith_shift_right, TS - 1, A.bitwise_and)
+        copy(R("HT"), R("BG", 0, 16))
+        ts(R("HP"), R("HT"), 2, A.arith_shift_right, TS - 1, A.bitwise_and)
+        ts(R("IV"), R("HT"), 0.0, A.is_lt, float(TS), A.mult)
+        tt(R("PF"), R("HP"), R("IV"), A.max)
+        copy(R("PU"), R("PF"))
+        tt(R("NQ"), I(R("STO"), R("PU")), arr, A.not_equal)
+        relay("BD", 16, (MS4, "NQ", 0))
+        mm(R("BE", 0, 256), [(B1, R("NQ"))])
+        ts(R("R1"), R("RI"), 1.0, A.add)
+        tt(R("RM"), R("RI"), MK, A.add)
+        ts(R("P1"), R("PF"), 1.0, A.add)
+        tt(R("PM1"), R("BD", 0, 16), R("P1"), A.min)
+        tt(R("ED"), I(R("PM1"), R("EXL")), R("RM"), A.is_equal)
+        eo = [(B1, R("ED"))]
+        lo = 0
+        for m in range(15):
+            n = 240 - 16 * m
+            ts(R("EO", lo, lo + n), R("R1", 16 * m + 16, 256), R("PM1", m, m + 1), A.is_equal)
+            eo.append((B1, R("EO", lo, lo + n), R("BF", 16 * m + 16, 256)))
+            lo += n
+        ts(R("UH"), R("BE", 0, 256), 1.0, A.min, 0.5, A.mult)
+        mm(R("BF", 0, 256), eo)
+        tt(R("NEW", b, b + 256), R("UH"), R("BF", 0, 256), A.is_gt)
+        rb = 768 * r + CAP * me
+        fused(lambda d: R("NEW", b + CAP * d, b + CAP * d + CAP), R("RPL", rb, rb + CAP), "lr%d" % r, "ra%d" % r)
+        act(R("RPL", rb, rb + CAP), R("NEW", b + CAP * me, b + CAP * me + CAP), AF.Copy)
+        landed("ra%d" % r, "RPL", 768 * r)
+        relay("BG", 16, (MS, "NEW", b))
+        ts(R("S1"), R("BG", 0, 16), 0.0, A.is_equal, 8192.0, A.mult)
+        tt(R("S2"), R("S1"), R("PF"), A.max)
+        tt(R("S3"), R("S2"), KS, A.min)
+        copy(R("SU"), R("S3"))
+        copy(I(R("STO"), R("SU")), arr)
+        if r == RO - 1:
+            dma("y", "st0", (T.yt[:], []), R("STO", 0, TS))
+
+    def nextfront(r):
+        b = 768 * r
+        last = r == RO - 1
+        act(R("NK", 0, 224), I(R("RPL", b, b + 768), part(R("OFF"), 0, 14)), AF.Copy)
+        copy(R("NK", 224, 512), I(R("RPL", b, b + 768), part(R("OFF"), 14, 32)))
+        relay("BH", 32, (MS, "NK", 0))
+        tt(R("NL", 1, 33), R("BH", 0, 32), R("LEN"), A.mult)
+        mm(R("BD", 0, 32), [(B1, R("NL", 0, 32))])
+        mm(R("BE", 0, 32), [(TRS, R("NL", 1, 33))])
+        ts(R("NP"), R("NL", 1, 33), 0.0, A.is_equal, 2048.0, A.mult)
+        scan(R("SF"), R("BD", 0, 32), part(ZR, 0, 32), 0.0, A.add, A.add)
+        tt(R("NP2"), R("NP"), R("NL", 1, 33), A.add)
+        tt(R("ST"), R("BE", 0, 32), R("SF"), A.add)
+        tt(R("EN"), R("ST"), R("NP2"), A.add)
+        ts(R("PE1"), R("EN"), 256.0, A.is_gt, 32768.0, A.mult)
+        ts(R("KP"), R("EN"), 256.0, A.is_le)
+        tt(R("X1"), R("ST"), R("PE1"), A.max)
+        tt(R("KB"), R("KP"), R("NL", 1, 33), A.mult)
+        tt(R("X2"), R("X1"), KT, A.min)
+        mm(R("BC", 0, 32), [(B1, R("KB"))])
+        copy(R("OF2"), R("X2"))
+        op("s", lambda: g.scalar.activation(out=R("X3")[0], in_=T.BC[:, 0:32], func=AF.Copy, accum_out=R("TOT", 0, 1)[0]),
+           [("BC", 0, 32)], R("X3")[1] + R("TOT", 0, 1)[1])
+        if not last:
+            act(R("TOB", 0, 1), R("TOT", 0, 1), AF.Identity, 0.5, -1.0)
+            for k in range(2):
+                act(R("VT", 16 * k, 16 * k + 16), QT, AF.Sign, R("TOB", 0, 1))
+            act(R("VT"), R("VT"), AF.Relu, 0.0, -1.0)
+        else:
+            act(R("TOB", 0, 1), R("TOT", 0, 1), AF.Identity, 16384.0, -32768.0)
+            act(R("FM"), IQ, AF.Relu, R("TOB", 0, 1), 32768.0)
+        copy(I(R("NXT"), R("OF2")), R("T0"))
+        ts(R("NFX"), R("NXT", 0, 256), 1.0, A.is_equal)
+        scan(R("PP"), R("NFX"), R("NXT", 0, 256), 0.0, A.mult, A.add)
+        ts(R("H"), R("PP"), MAG, A.add, MAG + 16.0, A.subtract)
+        relay("BF", 16, (MSC, "H", 0))
+        if last:
+            tt(R("PP"), R("PP"), R("FM"), A.max)
+        tt(R("MD"), R("PP"), R("H"), A.subtract)
+        ts(R("M2"), R("MD"), PM85, A.is_equal)
+        copy(R("CT"), R("BF", 0, 16))
+        for y, k0 in (("YH", "KH"), ("YL", "KL")):
+            for k in range(2):
+                tt(R(y, 256 * k, 256 * k + 256), I(R(k0, TW * k, TW * k + TW), R("CT")), R("M2"), A.mult)
+        if not last:
+            relay("BG", 32, (MST, "YH", 0), (MST, "YL", 0))
+        else:
+            mm((T.BG[0:8, 0:512], [("BG", 0, 512)]), [(G8, R("YH")), (G8, R("YL"))])
+        ts(R("FL"), IQ, R("TOT", 0, 1), A.is_lt)
+        tt(R("NF", 0, 256), R("FL"), R("NFX"), A.mult)
+        if not last:
+            tt(R("W0"), R("BG", 0, 32), R("VT"), A.mult)
+            copy(R("FUV"), R("W0"))
+        else:
+            mm((T.BH[0:8, 0:256], [("BH", 0, 512)]), [(G8S, R("NF", 0, 256))])
+            copy(R("OUTF", 0, 512, p=(0, 8)), (T.BG[0:8, 0:512], [("BG", 0, 512)]))
+            dma("y", "st1", (T.yu[:], []), R("OUTF", 0, 256, p=(0, 8)))
+            dma("s", "st2", (T.yv[:], []), R("OUTF", 256, 512, p=(0, 8)))
+            ts(R("OUTF", 512, 768, p=(0, 8)), (T.BH[0:8, 0:256], [("BH", 0, 512)]), -1.0, A.mult, 1.0, A.add)
+            dma("s", "st3", (T.ys[:], []), R("OUTF", 512, 768, p=(0, 8)))
+
+    for r in range(RO):
+        vphase()
+        two = {"B": qphase(), "A": comp()}
+        for x in ORDER:
+            next(two[x], None)
+        for x in two.values():
+            for _ in x:
+                pass
+        keys(r)
+        owner(r)
+        nextfront(r)
+    for s in sorted(finals):
+        if waited.get(s, 0) < finals[s]:
+            g.wait_ge(T.sem[s], finals[s])

@@ -1,18 +1,21 @@
-import math
 from concourse.bass import DstId, RemoteDMATransfer
-from concourse.mybir import AluOpType, AxisListType, ActivationFunctionType
+from concourse.mybir import AluOpType, ActivationFunctionType
 
 A = AluOpType
 AF = ActivationFunctionType
 W, F, FC, CAP, TS, RO = 3456, 256, 512, 64, 2048, 3
 P = 16 * F
-MAG = float(2 ** 27)
-RND = float(2 ** 23)
+RND = 1.5 * 2 ** 23
+M11 = 1.5 * 2 ** 34
+CL = 393216
+HALF = W // 2
 CH = [(0, 512), (512, 512), (1024, 1024), (2048, 1024), (3072, 512), (3584, 512)]
-ORDER = "BABABABABABAABAAABAB"
-TW = 288
-SD = 2064
-SW = SD + 256
+QH = [(512 * c, 512) for c in range(8)]
+AH = [(0, 1024), (1024, 1024), (2048, 1024), (3072, 512), (3584, 512)]
+EH = [(1024 * c, 1024) for c in range(4)]
+DUMP = 4128
+SNW = 2560
+ZC = P + 1
 
 
 def shapes(kind, dtype, text):
@@ -20,23 +23,26 @@ def shapes(kind, dtype, text):
 
 
 SCRATCH = {}
-SCRATCH.update(shapes("sbuf", "int32", "KID:3456 FUI:32 FSI:256 ZI:512 Z8:512 HI:32 OW:32 HT:16 HP:16 HR:256 RI:256 CI:1280"))
-SCRATCH.update(shapes("sbuf", "uint16", "FUV:32 KU:512 OPU:16 JT:32 T1:32 OFF:32 PU:16 R1:256 SU:16 OF2:32 CT:16 EXL:16"))
-SCRATCH.update(shapes("sbuf", "bfloat16", "VEC:3456 MRK:3456 FSB:256 NF:264 LASTF:256 EQ:256 KH:576 KL:576 MF:4096 VV:4096 DF:4096 AB:4096 "
-                      "NS:4112 QV:4096 MQ:4096 CU:264 CV:256 CB:256 CD:264 XL:256 L2B:8 JW:768 JK:512 OO:512 LL:512 ZB:512 OHB:132 "
-                      "STO:2320 NQ:256 ED:256 EO:1920 NK:512 NL:40 KB:32 H:256 M2:256 YH:512 YL:512 CM:4096 JR:256 "
-                      "SND:2304 ARR:768 NEW:768 RPL:2304"))
-SCRATCH.update(shapes("sbuf", "float32", "KF:512 D:4096 EM:4096 LG:256 XLI:256 SC:256 XC:256 T0:512 SN:132 RA:132 RB:132 R2:66 RQ:40 "
-                      "RM:256 UH:256 NXT:768 NFX:256 FM:256 FL:256 PP:256 MD:256 OUTF:768 CF:1280 CR:1792 SM:976"))
+SCRATCH.update(shapes("sbuf", "int32", "KID:3456 FUI:32 FSI:256 ZI:512 Z8:512 HI:32 OW:32 WI:16 UI:32 CI:1024"))
+SCRATCH.update(shapes("sbuf", "uint16", "FUV:32 KU:512 OPU:16 JT:32 T1:32 OFF:32 PU:16 R1:256 SU:16 OF2:32 CT:16"))
+SCRATCH.update(shapes("sbuf", "float16", "KF:512 SEL:4096"))
+SCRATCH.update(shapes("sbuf", "bfloat16", "VEC:3456 FSB:256 LASTF:256 EQ:256 MF:4112 VV:4096 NS:4112 CU:264 AP:256 CD:264 "
+                      "JW:4384 JK:512 YJ:512 JB:32 OO:512 LR:512 ZB:512 OHB:144 INV:40 STO:2320 NQ:256 NEG:256 ED:256 EO:1920 YN:256 "
+                      "NK:512 YK:512 NL:40 LN:40 SL:32 KB:32 CM:6400 RL:512 SND:2560 ARR:768 NEW:768 RPL:7680 ONE:256 J1:256 FF:256 FA:256"))
+SCRATCH.update(shapes("sbuf", "float32", "MRK:3456 QV:4096 D:4640 UV:4112 SC:264 XX:256 YX:256 XC:256 LA:512 T0:512 "
+                      "RK:136 R2:72 RR:256 P1:256 NP1:256 YP:256 PMR:256 YM:256 PP:256 YQ:256 GU:256 YU:256 F0:256 OUTF:768 "
+                      "CF:768 CR:1280 SM:512"))
 VIEW = {}
-for _w in ("L2:16 LT:8 PN:16 OP1:16 OP2:16 OP3:16 LEN:32 INV:32 OV:32 D2:32 O1:32 O2:32 O3:32 O4:32 IV:16 PF:16 P1:16 PM1:16 S1:16 "
-           "S2:16 S3:16 NP:32 NP2:32 SF:32 ST:32 EN:32 PE1:32 X1:32 X2:32 KP:32 W0:32 VT:32 TOT:8 TOB:8 X3:32").split():
+for _w in "RQ:32 S1:16 S2:16 S3:16 PF:16 SE:64 DU:32 X1:32 NR:32 GF:32 X3:32 TOT:8 TOB:8".split():
     _n, _k = _w.split(":")
     VIEW[_n] = ("SM", sum(x[2] for x in VIEW.values()), int(_k))
+SAME = {"DF": "VV", "AB": "VV", "EM": "QV", "NXT": "D"}
 BANKS = ("BA", "BB", "BC", "BD", "BE", "BF", "BG", "BH")
 SCRATCH.update({b: ("psum", [128, 512], "float32") for b in BANKS})
-SEMAPHORES = ["qv", "qs", "qt", "qg"] + ["ld%d" % k for k in range(9)] + ["st%d" % k for k in range(4)] + ["ac%d" % k for k in range(len(CH))] + \
+SEMAPHORES = ["qv", "qs", "qt", "qg"] + ["ld%d" % k for k in range(9)] + ["st%d" % k for k in range(4)] + ["ac%d" % k for k in range(len(AH))] + \
              ["%s%d" % (s, r) for s in ("ka", "ra", "lk", "lr") for r in range(RO)]
+SIZE = {"int32": 4, "float32": 4, "uint16": 2, "float16": 2, "bfloat16": 2}
+CY, PC, GA, SCA, WAKE, NET, DMA0, DMAB = 0.92, 0.46, 1.56, 3.5, 80.0, 3000.0, 2000.0, 0.6
 
 
 def rank_program(g, core, T, topo):
@@ -63,65 +69,15 @@ def rank_program(g, core, T, topo):
                     used = used + res[d]
         return res
 
-    queues = {"v": g.vector, "s": g.scalar, "t": g.tensor, "g": g, "y": g.sync}
-    count = {}
-    known = {q: {} for q in queues}
-    waited = {}
-    recs = {}
-    finals = {}
+    ops = []
 
-    def dowaits(q, reads, writes):
-        best = {}
-        for regs, wr in ((reads, False), (writes, True)):
-            for (b, lo, hi) in regs:
-                for rec in recs.get(b, []):
-                    if rec[0] < hi and lo < rec[1] and (wr or rec[2]):
-                        s, v = rec[3]
-                        if known[q].get(s, 0) < v and best.get(s, (0, None))[0] < v:
-                            best[s] = (v, rec[4])
-        for s in sorted(best, key=lambda s: -sum(best[s][1].values())):
-            v, clk = best[s]
-            if known[q].get(s, 0) >= v:
-                continue
-            queues[q].wait_ge(T.sem[s], v)
-            waited[s] = max(waited.get(s, 0), v)
-            known[q][s] = v
-            for a, b in clk.items():
-                known[q][a] = max(known[q].get(a, 0), b)
-
-    def note(q, tok, reads, writes):
-        clk = dict(known[q])
-        clk[tok[0]] = max(clk.get(tok[0], 0), tok[1])
-        for (b, lo, hi) in writes:
-            recs[b] = [r for r in recs.get(b, []) if not (lo <= r[0] and r[1] <= hi)] + [(lo, hi, True, tok, clk)]
-        for (b, lo, hi) in reads:
-            recs[b] = [r for r in recs.get(b, []) if not (r[0] == lo and r[1] == hi and not r[2] and r[3][0] == tok[0])] + [(lo, hi, False, tok, clk)]
-        finals[tok[0]] = max(finals.get(tok[0], 0), tok[1])
-
-    def bankfix(reads, writes):
+    def put(q, fn, reads, writes, hold, lat=0.0, sem=None, inc=1, chained=False):
         w = [(x[0], 0, 512) if x[0] in BANKS else x for x in writes] + [(x[0], 0, 512) for x in reads if x[0] in BANKS]
-        return [x for x in reads if x[0] not in BANKS], w
-
-    def op(q, fn, reads, writes):
-        reads, writes = bankfix(reads, writes)
-        dowaits(q, reads, writes)
-        s = "q" + q
-        fn().then_inc(T.sem[s], 1)
-        count[s] = count.get(s, 0) + 1
-        note(q, (s, count[s]), reads, writes)
-
-    def dma(q, sem, out, in_):
-        dowaits(q, in_[1], out[1])
-        queues[q].dma_start(out=out[0], in_=in_[0]).then_inc(T.sem[sem], 16)
-        note(q, (sem, 16), in_[1], out[1])
-
-    def addto(out, in_, sem):
-        dowaits("g", in_[1], out[1])
-        g.dma_start(out=out[0], in_=in_[0], accum_op=A.add).then_inc(T.sem[sem], 16)
-        count[sem] = count.get(sem, 0) + 16
-        note("g", (sem, count[sem]), in_[1], out[1])
+        r = [x for x in reads if x[0] not in BANKS]
+        ops.append({"q": q, "fn": fn, "r": r, "w": w, "hold": hold, "lat": lat, "sem": sem or "q" + q, "inc": inc, "ch": chained})
 
     def R(name, lo=None, hi=None, step=None, p=None):
+        name = SAME.get(name, name)
         if name in VIEW:
             name, at, n = VIEW[name]
             lo, hi = (at, at + n) if lo is None else (at + lo, at + hi)
@@ -129,13 +85,16 @@ def rank_program(g, core, T, topo):
         if lo is None:
             lo, hi = 0, t.shape[1]
         if p is not None:
-            ap = t[p[0]:p[1], lo:hi]
+            ap = t[p[0]:p[1]:p[2], lo:hi] if len(p) > 2 else t[p[0]:p[1], lo:hi]
         else:
             ap = t[:, lo:hi] if step is None else t[:, lo:hi:step]
-        return (ap, [(name, lo, hi)])
+        return (ap, [(name, lo, hi)], len(range(lo, hi, step or 1)), SIZE[SCRATCH[name][2]], name in BANKS, False)
 
     def I(win, off):
-        return (win[0].indirect(off[0]), win[1] + off[1])
+        return (win[0].indirect(off[0]), win[1] + off[1], 16 * off[2], win[3], False, True)
+
+    def H(t):
+        return (t, [], 0, 4, False, False)
 
     def rg(*xs):
         return [r for x in xs if isinstance(x, tuple) for r in x[1]]
@@ -143,59 +102,83 @@ def rank_program(g, core, T, topo):
     def va(x):
         return x[0] if isinstance(x, tuple) else x
 
+    def cost(out, *ins, both=False):
+        if out[5]:
+            return 50 + out[2] * SCA * CY
+        if ins and ins[0][5]:
+            return 50 + out[2] * GA * CY
+        f = 0.5 if all(x[3] == 2 for x in (out,) + ins) else 1.0
+        if both and not any(x[4] for x in ins):
+            f *= 2
+        return max(64, out[2] * f) * CY
+
     def copy(out, in_):
-        op("v", lambda: g.vector.tensor_copy(out=out[0], in_=in_[0]), rg(in_) + out[1][1:], out[1][:1])
+        put("v", lambda: g.vector.tensor_copy(out=out[0], in_=in_[0]), rg(in_) + out[1][1:], out[1][:1], cost(out, in_))
 
     def tt(out, a, b, o):
-        op("v", lambda: g.vector.tensor_tensor(out=out[0], in0=a[0], in1=b[0], op=o), rg(a, b), out[1])
+        put("v", lambda: g.vector.tensor_tensor(out=out[0], in0=a[0], in1=b[0], op=o), rg(a, b), out[1], cost(out, a, b, both=True))
 
     def ts(out, a, s1, o1, s2=None, o2=None):
         if o2 is None:
-            op("v", lambda: g.vector.tensor_scalar(out=out[0], in0=a[0], scalar1=va(s1), scalar2=None, op0=o1), rg(a, s1), out[1])
+            put("v", lambda: g.vector.tensor_scalar(out=out[0], in0=a[0], scalar1=va(s1), scalar2=None, op0=o1), rg(a, s1), out[1], cost(out, a))
         else:
-            op("v", lambda: g.vector.tensor_scalar(out=out[0], in0=a[0], scalar1=va(s1), scalar2=va(s2), op0=o1, op1=o2), rg(a, s1, s2), out[1])
+            put("v", lambda: g.vector.tensor_scalar(out=out[0], in0=a[0], scalar1=va(s1), scalar2=va(s2), op0=o1, op1=o2), rg(a, s1, s2), out[1], cost(out, a))
 
     def scan(out, d0, d1, init, o1, o2):
-        op("v", lambda: g.vector.tensor_tensor_scan(out=out[0], data0=d0[0], data1=d1[0], initial=va(init), op0=o1, op1=o2), rg(d0, d1, init), out[1])
-
-    def reduce(out, in_):
-        op("v", lambda: g.vector.tensor_reduce(out=out[0], in_=in_[0], axis=AxisListType.X, op=A.add), in_[1], out[1])
+        put("v", lambda: g.vector.tensor_tensor_scan(out=out[0], data0=d0[0], data1=d1[0], initial=va(init), op0=o1, op1=o2), rg(d0, d1, init), out[1], cost(out, d0, d1))
 
     def fill(out, c):
-        op("v", lambda: g.vector.memset(out[0], c), [], out[1])
+        put("v", lambda: g.vector.memset(out[0], c), [], out[1], cost(out))
 
-    def act(out, in_, f, bias=0.0, scale=1.0):
-        op("s", lambda: g.scalar.activation(out=out[0], in_=in_[0], func=f, bias=va(bias), scale=va(scale)), rg(in_, bias, scale), out[1])
-
-    def mm(out, prs):
-        rd, wr = bankfix(rg(*[x for p in prs for x in p[:2]]), out[1])
-        ins = None
-        for k, p in enumerate(prs):
-            dowaits("t", rg(p[0], p[1]), wr)
-            o = p[2] if len(p) > 2 else out
-            ins = g.tensor.matmul(out=o[0], lhsT=p[0][0], rhs=p[1][0], start=(k == 0), stop=(k == len(prs) - 1))
-        ins.then_inc(T.sem.qt, 1)
-        count["qt"] = count.get("qt", 0) + 1
-        note("t", ("qt", count["qt"]), rd, wr)
-
-    def iota(out, pat, base, cm, flag=False):
-        if flag:
-            op("g", lambda: g.iota(out[0], pat, base, cm, allow_small_or_imprecise_dtypes=True), [], out[1])
+    def act(out, in_, f, bias=0.0, scale=1.0, acc=None):
+        c = 65 + out[2] * GA * CY if in_[5] else max(64, out[2]) * CY
+        if acc is None:
+            put("s", lambda: g.scalar.activation(out=out[0], in_=in_[0], func=f, bias=va(bias), scale=va(scale)), rg(in_, bias, scale), out[1], c)
         else:
-            op("g", lambda: g.iota(out[0], pat, base, cm), [], out[1])
+            put("s", lambda: g.scalar.activation(out=out[0], in_=in_[0], func=f, accum_out=acc[0]), rg(in_), out[1] + acc[1], c + 20)
+
+    def mm(*parts):
+        for x, part in enumerate(parts):
+            def fn(part=part, first=(x == 0), last=(x == len(parts) - 1)):
+                ins = None
+                for k, (o, l, r) in enumerate(part):
+                    ins = g.tensor.matmul(out=o[0], lhsT=l[0], rhs=r[0], start=(first and k == 0), stop=(last and k == len(part) - 1))
+                return ins
+            put("t", fn, rg(*[y for p in part for y in p[1:]]), part[0][0][1], sum(max(64, p[0][2]) for p in part) * PC, chained=(x > 0))
+
+    def iota(out, pat, base, cm, flag=True):
+        if flag:
+            put("g", lambda: g.iota(out[0], pat, base, cm, allow_small_or_imprecise_dtypes=True), [], out[1], 130 + 2 * out[2] * CY)
+        else:
+            put("g", lambda: g.iota(out[0], pat, base, cm), [], out[1], 130 + 2 * out[2] * CY)
 
     def gfill(out, c):
-        iota(out, [[0, out[1][0][2] - out[1][0][1]]], c, 0, True)
+        iota(out, [[0, out[2]]], c, 0)
 
-    dma("y", "ld0", R("FUI", 0, 16), (T.fu[:], []))
-    dma("s", "ld1", R("FUI", 16, 32), (T.fv[:], []))
-    dma("s", "ld2", R("FSI", 0, 256, p=(0, 8)), (T.fs[:], []))
-    for k, (b, x) in enumerate((("KID", T.kids), ("VEC", T.vec), ("MRK", T.mark))):
-        s0, s1 = "ld%d" % (3 + 2 * k), "ld%d" % (4 + 2 * k)
-        g.sync.dma_start(out=T[b][0:64, :], in_=x[0:64, :]).then_inc(T.sem[s0], 16)
-        g.scalar.dma_start(out=T[b][64:128, :], in_=x[64:128, :]).then_inc(T.sem[s1], 16)
-        recs[b] = [(0, W, True, (s0, 16), {s0: 16}), (0, W, True, (s1, 16), {s1: 16})]
-        finals[s0] = finals[s1] = 16
+    queues = {"v": g.vector, "s": g.scalar, "t": g.tensor, "g": g, "y": g.sync}
+
+    def dma(q, sem, out, in_, lat, after=()):
+        put(q, lambda: queues[q].dma_start(out=out[0], in_=in_[0]), in_[1] + list(after), out[1], 60.0, lat, sem, 16)
+
+    def addto(out, in_, sem, after=()):
+        put("g", lambda: g.dma_start(out=out[0], in_=in_[0], accum_op=A.add), in_[1] + list(after), out[1], 600.0, DMA0 + 4 * out[2] * DMAB, sem, 16)
+
+    dma("y", "ld0", R("FUI", 0, 16), H(T.fu[:]), DMA0)
+    dma("s", "ld1", R("FUI", 16, 32), H(T.fv[:]), DMA0)
+    dma("s", "ld2", R("FSI", 0, 256, p=(0, 8)), H(T.fs[:]), DMA0)
+    lat = DMA0
+    for k, (b, x) in enumerate((("KID", T.kids), ("VEC", T.vec))):
+        lat += SIZE[SCRATCH[b][2]] * W * DMAB
+        for q, lo in (("y", 0), ("s", 64)):
+            dma(q, "ld%d" % (3 + 2 * k + lo // 64), (T[b][lo:lo + 64, :], [(b, W + lo // 64, W + lo // 64 + 1)]), H(x[lo:lo + 64, :]), lat)
+    NLOAD = len(ops)
+
+    def L(name):
+        x = R(name)
+        return (x[0], [(name, 0, W + 2)]) + x[2:]
+    fill(R("MRK"), float(CL))
+    for k in range(2):
+        addto(R("MRK", HALF * k, HALF * k + HALF), H(T.mark[:, HALF * k:HALF * k + HALF]), "ld%d" % (7 + k), L("VEC")[1])
 
     free = {"CI": 0, "CF": 0, "CM": 0, "CR": 0}
 
@@ -204,64 +187,49 @@ def rank_program(g, core, T, topo):
         free[buf] = lo + (n + 15) // 16 * 16
         return R(buf, lo, lo + n)
 
-    def part(m, a, b):
-        return R(m[1][0][0], m[1][0][1] + a, m[1][0][1] + b)
+    def part(m, a, b, step=None):
+        return R(m[1][0][0], m[1][0][1] + a, m[1][0][1] + b, step)
 
     def win(m, i):
         return part(m, 15 - i, 143 - i)
 
-    pI = new("CI", 1); cI = new("CI", 144); ktI = new("CI", 32); kdI = new("CI", 16); ksI = new("CI", 16); aI = new("CI", 256); exI = new("CI", 16)
-    iota(pI, [[0, 1]], 0, 1)
-    iota(cI, [[1, 144]], 0, 0)
-    iota(ktI, [[16, 32]], 256, 0)
-    iota(kdI, [[1, 16]], 512, 0)
-    iota(ksI, [[16, 16]], SD, 0)
-    iota(aI, [[1, 256]], 0, 0)
-    iota(exI, [[1, 16]], 0, 0)
-    gfill(R("MF"), 1)
-    K1 = new("CR", 512); IQ = new("CR", 256)
-    iota(K1, [[1, 512]], -4096, 0, True)
-    iota(IQ, [[1, 256]], 0, 0, True)
-    iota(R("JR"), [[1, 16], [16, 16]], 0, 0, True)
-    gfill(R("STO"), -1)
-    gfill(R("SND", 0, 256), -1)
-    gfill(R("KH"), 0)
-    gfill(R("KL"), 0)
-    gfill(R("RPL", 256, 768), 0)
-    for r in range(1, RO):
-        gfill(R("SND", 768 * r, 768 * r + 256), -1)
-        gfill(R("RPL", 768 * r + 256, 768 * r + 768), 0)
-    pmI = new("CI", 1); pgI = new("CI", 1); cgI = new("CI", 144); cmI = new("CI", 144); amI = new("CI", 256)
+    pI = new("CI", 1); cI = new("CI", 144); ktI = new("CI", 32)
+    iota(pI, [[0, 1]], 0, 1, False)
+    iota(cI, [[1, 144]], 0, 0, False)
+    iota(ktI, [[16, 32]], 0, 0, False)
+    pmI = new("CI", 1); pgI = new("CI", 1); cgI = new("CI", 144); cmI = new("CI", 144)
     ts(pmI, pI, 15, A.bitwise_and)
     ts(pgI, pI, 4, A.arith_shift_right)
     ts(cgI, cI, 4, A.arith_shift_right)
     ts(cmI, cI, 15, A.bitwise_and)
     PM = new("CF", 1); PG = new("CF", 1); CG = new("CF", 144); CMF = new("CF", 144); PX = new("CF", 1)
     copy(PM, pmI); copy(PG, pgI); copy(CG, cgI); copy(CMF, cmI); copy(PX, pI)
-    BLK = new("CM", 144); C15 = new("CM", 144); MST = new("CM", 144); G8 = new("CM", 8); R8 = new("CM", 128)
+    BLK = new("CM", 144); C15 = new("CM", 144); MST = new("CM", 144); R8 = new("CM", 128)
     ts(BLK, CG, PG, A.is_equal)
     ts(C15, CMF, 15.0, A.is_equal)
     tt(MST, BLK, C15, A.mult)
-    ts(G8, part(cI, 0, 8), PG, A.is_equal)
     ts(R8, part(CG, 0, 128), PX, A.is_equal)
+    gfill(R("MF"), 1)
+    fill(R("MF", P, P + 16), 0.0)
     ts(R("FSB", 0, 256, p=(0, 8)), R("FSI", 0, 256, p=(0, 8)), -1.0, A.mult, 1.0, A.add)
     r0 = R8[1][0][1]
-    mm(R("BA", 0, 256), [((T.CM[0:8, r0:r0 + 128], R8[1]), R("FSB", 0, 256, p=(0, 8)))])
-    fill(R("NF"), 0.0)
-    copy(R("NF", 0, 256), R("BA", 0, 256))
+    mm([(R("BA", 0, 256), R("CM", r0, r0 + 128, p=(0, 8)), R("FSB", 0, 256, p=(0, 8)))])
+    copy(R("MF", 0, P, 16), R("BA", 0, 256))
     copy(R("FUV"), R("FUI"))
-    WC = new("CF", 1)
+    WC = new("CF", 1); W4 = new("CF", 1); SGN = new("CF", 1); SG16 = new("CF", 1); SGH = new("CF", 1); NSG = new("CF", 1)
     ts(WC, PM, -14.0, A.mult, 255.0, A.add)
+    ts(W4, WC, 0.25, A.mult)
+    ts(SGH, PM, 15.0, A.is_equal, -0.5, A.add)
+    ts(SGN, SGH, 2.0, A.mult)
+    ts(SG16, SGH, 32.0, A.mult)
+    ts(NSG, SGH, -2.0, A.mult)
 
-    def scaled(src, by, n=144):
+    def scaled(src, by, n=128):
         m = new("CM", n)
         act(m, part(src, 0, n), AF.Identity, 0.0, by)
         return m
-    MSL = scaled(MST, -float(2 ** 36)); MS = scaled(MST, 0.0625); MSC = scaled(MST, 2.0 ** -8); MSW = scaled(MST, WC)
-    MS4 = scaled(MST, 4096.0); MSI = scaled(MST, PM)
-    BW = scaled(BLK, WC, 128); BN = scaled(BLK, -1.0, 128); BI = scaled(BLK, PM, 128); G8S = scaled(G8, 0.0625, 8)
     B1 = part(BLK, 0, 128)
-    DK = new("CF", 128); TMP = new("CF", 128); TM2 = new("CF", 128); CM1 = part(CMF, 0, 128)
+    DK = new("CF", 128); TMP = new("CF", 128); CM1 = part(CMF, 0, 128)
     ts(DK, CM1, PM, A.subtract)
 
     def masked(o, c):
@@ -269,156 +237,139 @@ def rank_program(g, core, T, topo):
         ts(TMP, DK, c, o)
         tt(m, TMP, B1, A.mult)
         return m
+
+    def comb(a, b, by):
+        m = new("CM", 128)
+        ts(TMP, b, by, A.mult)
+        tt(m, a, TMP, A.add)
+        return m
     TRS = masked(A.is_gt, 0.0); TRI = masked(A.is_ge, 0.0); TGE = masked(A.is_le, 0.0); IDN = masked(A.is_equal, 0.0)
-    S0 = masked(A.is_equal, 1.0); S1 = masked(A.is_equal, -15.0)
-    TRN = new("CM", 128)
-    ts(TMP, IDN, 65.0, A.mult)
-    tt(TRN, TMP, TRI, A.subtract)
-    TRX = new("CM", 128)
-    ts(TMP, IDN, -4096.0, A.mult)
-    tt(TRX, TRS, TMP, A.add)
-    DA = new("CF", 128); DB = new("CF", 128)
-    R4 = new("CR", 128); R4P = new("CR", 128); C4 = new("CR", 1)
-    ts(DB, CM1, 0.0, A.is_equal)
-    ts(DA, CM1, 0.0, A.is_gt, 0.25, A.mult)
-    scan(R4, DA, DB, 0.0, A.mult, A.add)
-    ts(TMP, CM1, 0.0, A.is_gt, 4.0, A.mult)
-    scan(R4P, TMP, DB, 0.0, A.mult, A.add)
-    tt(TM2, IDN, R4P, A.mult)
-    reduce(C4, TM2)
-    A1 = new("CM", 128); A0 = new("CM", 128); A2 = new("CM", 128)
-    ts(TMP, R4, C4, A.mult, float(4 ** 16), A.mult)
-    tt(A1, TMP, B1, A.mult)
-    ts(TM2, TMP, float(4 ** 16), A.mult)
-    tt(A0, TM2, TRS, A.mult)
-    ts(TM2, TMP, float(4.0 ** -16), A.mult)
-    tt(A2, TM2, TGE, A.mult)
-    KT = new("CR", 32); KD = new("CR", 16); KS = new("CR", 16); PM16 = new("CF", 1); PM85 = new("CF", 1); ZR = new("CR", 256)
-    MK = new("CR", 256); RS = new("CR", 132); QT = new("CR", 16)
-    ts(KT, ktI, PM, A.add)
-    ts(QT, part(KT, 0, 16), -256.0, A.add)
-    ts(PM16, PM, 16.0, A.mult)
-    ts(KD, kdI, PM16, A.add)
-    ts(KS, ksI, PM, A.add)
-    ts(PM85, PM, 8.5, A.add)
-    ts(amI, aI, 15, A.bitwise_and)
-    ts(MK, amI, PM, A.is_le, 4096.0, A.mult)
-    ts(MK, MK, 1.0, A.add)
-    copy(R("EXL"), exI)
-    fill(ZR, 0.0)
-    fill(RS, 1.0)
+    TGT = masked(A.is_lt, 0.0); S0 = masked(A.is_equal, 1.0); S1 = masked(A.is_equal, -15.0)
+    A0 = comb(TRS, S0, 63.0); A1 = comb(B1, S1, 63.0); A0C = comb(A0, IDN, -128.0)
+    TRX = comb(TRS, IDN, -4096.0); TRB = comb(TRS, IDN, 4096.0)
+    MSL = scaled(MST, -float(2 ** 36), 144); MS = scaled(MST, 0.0625, 144); MSW = scaled(MST, WC, 144); MSI = scaled(MST, PM, 144)
+    BW4 = scaled(BLK, W4); BI = scaled(BLK, PM); BL = scaled(BLK, -0.0625); BN8 = scaled(BLK, -8192.0); BN4 = scaled(BLK, -4096.0)
+    BP8 = scaled(BLK, 8192.0); BP17 = scaled(BLK, float(2 ** 17))
+    NTRS = scaled(TRS, -1.0); NTGE = scaled(TGE, -1.0); NTRI = scaled(TRI, -1.0); NTGT = scaled(TGT, -1.0)
+    ID = {}
+    for c in (94.0, 128.0, float(DUMP), float(2 ** 20), 512.0, -512.0, -4096.0, 4096.0, 8192.0, -8192.0, -1024.0, 0.5 - me / 4, 1.0 - me / 4):
+        if c not in ID:
+            ID[c] = scaled(IDN, c)
+    K1 = new("CR", 512); IQ = new("CR", 256); KT1 = new("CR", 32); KD = new("CR", 32); KS = new("CR", 16); ZR = new("CR", 264)
+    RS = new("CM", 136); PADC = new("CM", 136); RS2 = new("CM", 64)
+    iota(K1, [[1, 512]], 1 - 4096, 0)
+    iota(IQ, [[1, 256]], 0, 0)
+    iota(R("J1"), [[1, 256]], 1, 0)
+    gfill(R("ONE"), 1)
+    gfill(R("STO"), -1)
+    gfill(ZR, 0)
+    for r in range(RO):
+        fill(R("RPL", SNW * r, SNW * r + SNW), 1.0)
+    ts(KT1, ktI, PM, A.add, 1.0, A.add)
+    ts(KD, KT1, float(DUMP - 1), A.add)
+    ts(KS, part(KT1, 0, 16), float(TS + 16), A.add)
+    fill(RS, 1.0); fill(PADC, 0.0); fill(RS2, 1.0)
     for o in range(N):
-        fill(part(RS, 33 * o, 33 * o + 1), 0.0)
-    fill(R("OHB"), 0.0); fill(R("CD"), 0.0); fill(R("CU"), 0.0); fill(R("NL"), 0.0); fill(R("NS", 0, 16), 0.0)
-    ts(R("CU", 1, 2), PM, 15.0, A.is_equal)
+        fill(part(RS, 34 * o + 1, 34 * o + 2), 0.0)
+        fill(part(PADC, 34 * o + 1, 34 * o + 2), 512.0 * o - 4096.0)
+    fill(part(RS2, 32, 33), 0.0)
+    fill(R("OHB"), 0.0); fill(R("CD"), 0.0); fill(R("CU"), -1.0); fill(R("NL"), 0.0); fill(R("LN"), 0.0); fill(R("INV"), 0.0)
+    fill(R("NS", 0, 16), 0.0)
+    fill(R("UV", 0, 8), 1.0); fill(R("UV", P, P + 16), 1.0)
+    copy(R("CU", 1, 2), SGN)
+    aI = new("CI", 512)
+    iota(aI, [[0, 32], [1, 16]], 0, 0, False)
+    PN = new("CF", 1)
+    ts(PN, PM, 1.0, A.add, 16.0, A.is_lt)
+    ts(PN, PM, 1.0, A.add, PN, A.mult)
+    ts(R("LA"), aI, PM, A.is_equal, -float(2 ** 40), A.mult)
+    ts(R("T0"), aI, PN, A.is_equal, -2.0, A.mult)
+    tt(R("LA"), R("LA"), R("T0"), A.add)
+    ts(R("RL"), R("LA"), 1.0, A.add)
+    for i in range(16):
+        c = new("CF", 1) if i < 2 else (cs[i % 2])
+        if i == 0:
+            cs = [c]
+        elif i == 1:
+            cs.append(c)
+        ts(c, PM, float(i), A.is_equal)
+        ts(R("SEL", 256 * i, 256 * i + 128), B1, c, A.mult, 4096.0, A.mult)
+        ts(R("SEL", 256 * i + 128, 256 * i + 256), B1, c, A.mult)
 
-    def relay(outb, n, *parts):
-        mm(R(outb, 0, n), [(win(m, i), R(b, lo + i, lo + 16 * n, 16)) for m, b, lo in parts for i in range(16)])
+    def sums(out, m, b, lo):
+        return [(out, win(m, i), R(b, lo + i, lo + 16 * out[2], 16)) for i in range(16)]
 
-    def gv(c):
-        a, n = CH[c]
-        act(R("VV", a, a + n), I(R("VEC"), R("KU", 256 + a // 16, 256 + (a + n) // 16)), AF.Copy)
-
-    def gq(c):
-        a, n = CH[c]
-        act(R("QV", a, a + n), I(R("MRK"), R("KU", 256 + a // 16, 256 + (a + n) // 16)), AF.Copy)
+    def relay(out, in_):
+        scan(out, R("RL", 0, out[2]), in_, SGH, A.mult, A.min)
+        return part(out, 15, out[2], 16)
 
     def vphase():
-        copy(R("KU", 256, 512), I(R("KID"), R("FUV", 16, 32)))
-        copy(R("KU", 0, 256), I(R("KID"), R("FUV", 0, 16)))
-        gv(0)
-        gv(1)
-        act(R("LASTF"), R("NF", 1, 257), AF.Identity, 1.0, -1.0)
+        copy(R("KU", 256, 512), I(L("KID"), R("FUV", 16, 32)))
+        copy(R("KU", 0, 256), I(L("KID"), R("FUV", 0, 16)))
+        act(R("LASTF"), R("MF", 16, P + 16, 16), AF.Identity, 1.0, -1.0)
         gfill(R("JW", 0, 512), 0)
-        copy(R("MF", 0, P, 16), R("NF", 0, 256))
+        for o in range(N):
+            gfill(R("SND", 512 * o, 512 * o + CAP), -1)
         for c, (a, n) in enumerate(CH):
-            tt(R("DF", a, a + n), I(R("VEC"), R("KU", a // 16, (a + n) // 16)), R("VV", a, a + n), A.subtract)
+            act(R("VV", a, a + n), I(L("VEC"), R("KU", 256 + a // 16, 256 + (a + n) // 16)), AF.Copy)
+            tt(R("DF", a, a + n), I(L("VEC"), R("KU", a // 16, (a + n) // 16)), R("VV", a, a + n), A.subtract)
             scan(R("D", a, a + n), R("MF", a, a + n), R("DF", a, a + n), R("D", a - 1, a) if a else 0.0, A.mult, A.add)
-            if c + 2 < len(CH):
-                gv(c + 2)
-            elif c + 2 == len(CH):
-                gq(0)
             act(R("AB", a, a + n), R("D", a, a + n), AF.Abs)
             j0, j1 = a // 16, (a + n) // 16
-            mm(R("BC", j0, j1), [(win(MST, i), R("AB", a + i, a + n, 16)) for i in range(16)] + [(win(MSL, 15), R("LASTF", j0, j1))])
+            mm([(R("BA", j0, j1), win(MSL, 15), R("LASTF", j0, j1))] + sums(R("BA", j0, j1), MST, "AB", a))
 
     def comp():
-        copy(R("KF", 256, 512), R("KU", 256, 512))
-        tt(R("EQ"), I(R("KID"), R("FUV", 0, 16)), R("KF", 256, 512), A.is_equal)
-        ts(R("CU", 2, 258), R("BC", 0, 256), 0.0, A.is_le)
-        mm(R("BD", 0, 256), [(A0, R("CU", 2, 258)), (A1, R("CU", 1, 257)), (A2, R("CU", 0, 256))])
-        mm(R("BE", 0, 256), [(S0, R("CU", 2, 258)), (S1, R("CU", 1, 257))])
-        yield
-        tt(R("CV"), R("BD", 0, 256), R("CU", 2, 258), A.min)
-        act(R("LG"), R("BD", 0, 256), AF.Ln, 0.25)
-        act(R("XLI"), R("LG"), AF.Identity, 32.1 + RND, -1.0 / math.log(4.0))
-        tt(R("CB"), R("BE", 0, 256), R("EQ"), A.mult)
-        yield
-        tt(R("CD", 1, 257), R("CV"), R("CB"), A.is_gt)
-        mm(R("BH", 0, 16), [(win(MST, a), R("CD", 1 + 16 * a, 17 + 16 * a)) for a in range(16)])
-        mm(R("BF", 0, 256), [(TRX, R("CD", 1, 257))])
-        mm(R("BG", 0, 256), [(B1, R("CD", 0, 256))])
-        yield
-        scan(R("L2"), R("BH", 0, 16), part(ZR, 0, 16), 0.0, A.add, A.add)
-        ts(R("PN"), R("BH", 0, 16), 0.0, A.is_equal, 8192.0, A.mult)
-        copy(R("L2B", 0, 1), R("L2", 15, 16))
-        tt(R("OP1"), R("BH", 0, 16), R("PN"), A.subtract)
-        mm(R("BD", 0, 1), [(TRS, R("L2B", 0, 1))])
-        yield
-        tt(R("OP2"), R("L2"), R("OP1"), A.subtract)
-        copy(R("LT", 0, 1), R("BD", 0, 1))
-        yield
-        ts(R("OP1"), R("OP2"), R("LT", 0, 1), A.add)
-        ts(R("OP2"), R("OP1"), 512.0, A.is_ge, 8192.0, A.mult)
-        tt(R("OP3"), R("OP1"), R("OP2"), A.max)
-        tt(R("OP1"), R("OP3"), KD, A.min)
-        copy(R("OPU"), R("OP1"))
-        copy(I(R("JW"), R("OPU")), R("JR"))
-        yield
-        scan(R("JK"), R("JW", 0, 512), R("JW", 0, 512), 0.0, A.max, A.max)
-        relay("BD", 32, (MS, "JK", 0))
-        scan(R("SC"), R("BG", 0, 256), ZR, 0.0, A.add, A.add)
-        yield
-        act(R("XL"), R("XLI"), AF.Identity, -RND)
-        copy(R("JT"), R("BD", 0, 32))
-        yield
-        tt(R("XC"), R("BF", 0, 256), R("SC"), A.add)
-        yield
+        ts(R("KF"), R("KU"), -float(HALF), A.add)
+        tt(R("EQ"), R("KF", 0, 256), R("KF", 256, 512), A.is_equal)
+        act(R("CU", 2, 258), R("BA", 0, 256), AF.Sign, 0.5, -1.0)
+        z, b = R("BD", 0, 256), R("BE", 0, 256)
+        mm([(b, ID[128.0], R("EQ"))], [(b, A0C, R("CU", 2, 258)), (b, A1, R("CU", 1, 257)), (b, TGE, R("CU", 0, 256))])
+        mm([(z, ID[94.0], R("ONE"))], [(z, A0, R("CU", 2, 258)), (z, A1, R("CU", 1, 257)), (z, TGE, R("CU", 0, 256))])
+        act(R("AP"), b, AF.Relu, -8192.0, 256.0)
+        tt(R("CD", 1, 257), z, R("AP"), A.is_gt)
+        mm([(R("BF", 0, 257), B1, R("CD", 0, 257))])
+        x = R("BG", 0, 256)
+        mm([(x, IDN, R("J1")), (x, ID[float(DUMP)], R("ONE"))], [(x, BN8, R("CD", 1, 257))])
+        mm([(R("BH", 0, 256), TRX, R("CD", 1, 257))])
+        scan(R("SC", 0, 257), R("BF", 0, 257), part(ZR, 0, 257), 1.0, A.add, A.add)
+        tt(R("XX"), x, R("SC", 0, 256), A.max)
+        ts(R("OPU"), relay(R("YX"), R("XX")), SGN, A.mult, -1.0, A.add)
+        copy(I(R("JW", 0, DUMP + 256), R("OPU")), R("J1"))
+        scan(R("JK"), R("JW", 0, 512), R("JW", 0, 512), 1.0, A.max, A.max)
+        y = relay(R("YJ"), R("JK"))
+        ts(R("JT"), y, SGN, A.mult, -1.0, A.add)
+        act(R("JB"), y, AF.Identity, 0.0, SG16)
+        tt(R("XC"), R("BH", 0, 256), R("SC", 0, 256), A.add)
+        ts(R("INV", 1, 33), KT1, R("SC", 256, 257), A.is_ge)
         tt(R("OO"), I(R("XC"), R("JT")), K1, A.is_equal)
-        tt(R("LL"), I(R("XL"), R("JT")), R("OO"), A.mult)
-        relay("BE", 32, (MST, "JK", 0), (MSI, "OO", 0))
-        relay("BF", 32, (MST, "LL", 0))
-        mm(R("BG", 0, 512), [(B1, R("JK")), (BI, R("OO")), (BN, R("LL"))])
-        yield
-        copy(R("T1"), R("BE", 0, 32))
-        copy(R("LEN"), R("BF", 0, 32))
-        ts(R("INV"), R("BF", 0, 32), 0.0, A.is_equal, 8.0, A.mult)
-        act(R("T0"), R("BG", 0, 512), AF.Identity, 9.5)
-        yield
+        t = R("BD", 0, 32)
+        mm([(t, IDN, R("JB"))], sums(t, MSI, "OO", 0))
+        ts(R("T1"), t, -16.0, A.add)
 
     def qphase():
-        for c in range(1, len(CH)):
-            gq(c)
-        banks = ("BA", "BB", "BC")
-        rc = 0
-        for c, (a, n) in enumerate(CH):
-            tt(R("MQ", a, a + n), I(R("MRK"), R("KU", a // 16, (a + n) // 16)), R("QV", a, a + n), A.max)
-            addto(R("D", a, a + n), R("MQ", a, a + n), "ac%d" % c)
-            for _ in range(2 if c >= 2 else 0):
-                b = banks[rc % 3]
-                mm(R(b, 0, 512), [(B1, R("AB", 512 * rc, 512 * rc + 512))])
-                act(R("NS", 512 * rc + 1, 512 * rc + 513), R(b, 0, 512), AF.Sign)
-                rc += 1
-            yield
-        tt(R("NS", 0, P, 16), R("NS", 0, P, 16), R("NF", 0, 256), A.mult)
-        yield
-        for a in range(0, P, 2048):
-            scan(R("EM", a, a + 2048), R("NS", a, a + 2048), R("D", a, a + 2048), R("EM", a - 1, a) if a else 0.0, A.mult, A.add)
-            yield
+        for a, n in QH:
+            act(R("QV", a, a + n), I(R("MRK"), R("KU", 256 + a // 16, 256 + (a + n) // 16)), AF.Copy)
+            tt(R("QV", a, a + n), I(R("MRK"), R("KU", a // 16, (a + n) // 16)), R("QV", a, a + n), A.max)
+        for c, (a, n) in enumerate(AH):
+            addto(R("D", a, a + n), R("QV", a, a + n), "ac%d" % c)
+        for c in range(8):
+            b = R(("BB", "BC")[c % 2])
+            mm([(b, B1, R("AB", 512 * c, 512 * c + 512))])
+            act(R("NS", 512 * c + 1, 512 * c + 513), b, AF.Sign)
+        for a, n in EH:
+            tt(R("NS", a, a + n, 16), R("NS", a, a + n, 16), R("MF", a, a + n, 16), A.mult)
+            scan(R("EM", a, a + n), R("NS", a, a + n), R("D", a, a + n), R("EM", a - 1, a) if a else 0.0, A.mult, A.add)
 
-    def fused(src, dst, lsem, rsem):
+    def pairs():
+        for i in range(16):
+            b = R(("BB", "BC")[i % 2], 0, 256)
+            mm([(b, R("SEL", 256 * i, 256 * i + 128), R("KF", 0, 256)), (b, R("SEL", 256 * i + 128, 256 * i + 256), R("KF", 256, 512))])
+            act(R("UV", 1 + i, 1 + P, 16), b, AF.Identity, float(4097 * HALF + 1))
+
+    def fused(src, buf, base, step, lsem, rsem):
         m = masks(me)
         tr, rd, tot = [], [], 0
+        dst = R(buf, base + step * me, base + step * me + CAP)
         for d in range(N):
             if d != me:
                 rid, pid = topo.addr(cores[d])[:2]
@@ -426,166 +377,208 @@ def rank_program(g, core, T, topo):
                 rd += x[1]
                 tot += len(m[d])
                 tr.append(RemoteDMATransfer(dst_ids=[DstId(rid=rid, pnc=pid)], dma_engine_mask=sum(1 << e for e in m[d]), remote_sem=T.sem[rsem], src=x[0], dst=dst[0]))
-        dowaits("g", rd, [])
-        g.remote_dma_fused(tr, local_sem=T.sem[lsem])
-        note("g", (lsem, tot), rd, [])
-
-    def landed(sem, buf, base):
+        put("g", lambda: g.remote_dma_fused(tr, local_sem=T.sem[lsem]), rd, [(lsem, 0, 1)], 500.0, 1000.0, lsem, -tot)
+        act(dst, src(me), AF.Copy)
         tot = sum(len(masks(s)[me]) for s in range(N) if s != me)
-        for s in range(N):
-            if s != me:
-                recs.setdefault(buf, []).append((base + CAP * s, base + CAP * (s + 1), True, (sem, tot), {sem: tot}))
-        finals[sem] = tot
+        put("n", None, [(lsem, 0, 1)], [(buf, base + step * s, base + step * s + CAP) for s in range(N) if s != me], 1.0, NET - 1500.0, rsem, tot)
 
     def keys(r):
-        copy(R("ZI"), I(R("EM"), R("T1")))
+        ts(R("ZI"), I(R("EM"), R("T1")), float(2 ** 30), A.min, -float(2 ** 30), A.max)
         ts(R("Z8"), R("ZI"), 255, A.bitwise_and)
         copy(R("ZB"), R("Z8"))
-        relay("BD", 32, (MSW, "ZB", 0))
-        copy(R("HI"), R("BD", 0, 32))
-        ts(R("OW"), R("HI"), 3, A.bitwise_and)
-        tt(R("OV"), R("OW"), R("INV"), A.add)
+        h = R("BD", 0, 32)
+        mm([(h, ID[float(2 ** 20)], R("INV", 1, 33))], sums(h, MSW, "ZB", 0))
+        copy(R("HI"), h)
+        ts(R("OW"), R("HI"), 3 + 2 ** 20, A.bitwise_and)
         for o in range(N):
-            ts(R("OHB", 33 * o + 1, 33 * o + 33), R("OV"), float(o), A.is_equal)
-        mm(R("BE", 0, 132), [(BN, R("OHB"))])
-        mm(R("BF", 0, 132), [(TRN, R("OHB"))])
-        ts(R("D2"), R("OV"), 64.0, A.mult, 64.0, A.add)
-        scan(R("SN"), RS, R("BE", 0, 132), 0.0, A.mult, A.add)
-        tt(R("RA", 1, 132), R("BF", 1, 132), R("SN", 0, 131), A.add)
-        tt(R("RB", 1, 132), R("RA", 1, 132), R("OHB", 1, 132), A.mult)
-        tt(R("R2", 1, 66), R("RB", 1, 66), R("RB", 67, 132), A.add)
-        tt(R("RQ", 1, 33), R("R2", 1, 33), R("R2", 34, 66), A.add)
-        ts(R("O1"), R("RQ", 1, 33), 0.0, A.is_le, 4096.0, A.mult)
-        tt(R("O2"), R("D2"), R("RQ", 1, 33), A.subtract)
-        tt(R("O3"), R("O2"), R("O1"), A.max)
-        tt(R("O4"), R("O3"), KT, A.min)
-        copy(R("OFF"), R("O4"))
-        b, c = 768 * r, 256 * r + CAP * me
-        copy(I(R("SND", b, b + 768), R("OFF")), R("ZB"))
-        fused(lambda d: R("SND", b + CAP * d, b + CAP * d + CAP), R("ARR", c, c + CAP), "lk%d" % r, "ka%d" % r)
-        act(R("ARR", c, c + CAP), R("SND", b + CAP * me, b + CAP * me + CAP), AF.Copy)
-        fill(R("NXT", 0, 256), 1.0)
-        copy(R("KF", 0, 256), R("KU", 0, 256))
-        for k in range(2):
-            ts(R("KH", TW * k, TW * k + 256), R("KU", 256 * k, 256 * k + 256), MAG, A.add, MAG, A.subtract)
-            tt(R("KL", TW * k, TW * k + 256), R("KF", 256 * k, 256 * k + 256), R("KH", TW * k, TW * k + 256), A.subtract)
-        landed("ka%d" % r, "ARR", 256 * r)
+            ts(R("OHB", 34 * o + 3, 34 * o + 35), R("OW"), float(o), A.is_equal if o < N - 1 else A.is_ge)
+        k = R("BF", 0, 136)
+        k3 = R("BF", 104, 136)
+        mm([(k, IDN, PADC), (k3, ID[512.0], R("INV", 1, 33)), (k3, ID[-512.0], R("INV", 0, 32))],
+           [(k, TRB, R("OHB", 1, 137)), (k, TGE, R("OHB", 0, 136)), (k, ID[-4096.0], R("OHB", 0, 136))])
+        scan(R("RK"), RS, k, 0.0, A.mult, A.add)
+        tt(R("R2", 0, 66), R("RK", 2, 68), R("RK", 70, 136), A.max)
+        tt(R("RQ"), R("R2", 0, 32), R("R2", 34, 66), A.max)
+        copy(R("OFF"), R("RQ"))
+        copy(I(R("SND"), R("OFF")), R("ZB"))
+        fused(lambda d: R("SND", 512 * d, 512 * d + CAP), "ARR", 256 * r, CAP, "lk%d" % r, "ka%d" % r)
+        gfill(R("NXT", 0, 256), 0)
+        act(R("LA"), I(R("EM"), R("T1")), AF.Identity, RND, 1.0 / CL)
+        act(R("LR"), R("LA"), AF.Identity, -RND)
+        t = R("BE")
+        mm([(t, B1, R("JK")), (t, BI, R("OO")), (t, BL, R("LR"))])
+        act(R("T0"), t, AF.Identity, -14.0)
+        t = R("BG", 0, 32)
+        mm(sums(t, MS, "LR", 0))
+        act(R("LN", 1, 33), t, AF.Copy)
+        act(R("SL"), t, AF.Identity, 0.0, SGN)
 
     def owner(r):
         b = 256 * r
         arr = R("ARR", b, b + 256)
-        mm(R("BH", 0, 256), [(BW, arr)])
-        relay("BG", 16, (MSW, "ARR", b))
-        copy(R("HR"), R("BH", 0, 256))
-        ts(R("RI"), R("HR"), 2, A.arith_shift_right, TS - 1, A.bitwise_and)
-        copy(R("HT"), R("BG", 0, 16))
-        ts(R("HP"), R("HT"), 2, A.arith_shift_right, TS - 1, A.bitwise_and)
-        ts(R("IV"), R("HT"), 0.0, A.is_lt, float(TS), A.mult)
-        tt(R("PF"), R("HP"), R("IV"), A.max)
-        copy(R("PU"), R("PF"))
+        pa, pb = R("BH", 0, 256), R("BH", 256, 512)
+        mm([(pa, ID[-1024.0], R("ONE")), (pa, ID[0.5 - me / 4], R("ONE")), (pb, ID[1.0 - me / 4], R("ONE"))], [(pa, BW4, arr), (pb, BW4, arr)])
+        act(R("NEG"), arr, AF.Relu, 0.0, -1.0)
+        ts(R("RR"), pa, M11, A.add, M11, A.subtract)
+        tt(R("P1"), pb, R("RR"), A.subtract)
+        yp = relay(R("YP"), R("P1"))
+        ts(R("PU"), yp, SGN, A.mult, -1.0, A.add)
         tt(R("NQ"), I(R("STO"), R("PU")), arr, A.not_equal)
-        relay("BD", 16, (MS4, "NQ", 0))
-        mm(R("BE", 0, 256), [(B1, R("NQ"))])
-        ts(R("R1"), R("RI"), 1.0, A.add)
-        tt(R("RM"), R("RI"), MK, A.add)
-        ts(R("P1"), R("PF"), 1.0, A.add)
-        tt(R("PM1"), R("BD", 0, 16), R("P1"), A.min)
-        tt(R("ED"), I(R("PM1"), R("EXL")), R("RM"), A.is_equal)
-        eo = [(B1, R("ED"))]
+        s, n = R("BA", 0, 256), R("BD", 0, 256)
+        mm([(s, ID[4096.0], R("ONE")), (s, BP8, R("NEG"))], [(s, BN4, R("NQ"))])
+        copy(R("R1"), R("P1"))
+        act(R("NP1"), R("P1"), AF.Identity, 0.0, -1.0)
+        tt(R("PMR"), s, R("P1"), A.max)
+        relay(R("YM"), R("PMR"))
+        tt(R("ED"), R("YM"), R("NP1"), A.is_equal)
+        eo = [[(n, ID[4096.0], R("ONE")), (n, BP8, R("NEG")), (n, BN4, R("NQ"))]]
         lo = 0
         for m in range(15):
-            n = 240 - 16 * m
-            ts(R("EO", lo, lo + n), R("R1", 16 * m + 16, 256), R("PM1", m, m + 1), A.is_equal)
-            eo.append((B1, R("EO", lo, lo + n), R("BF", 16 * m + 16, 256)))
-            lo += n
-        ts(R("UH"), R("BE", 0, 256), 1.0, A.min, 0.5, A.mult)
-        mm(R("BF", 0, 256), eo)
-        tt(R("NEW", b, b + 256), R("UH"), R("BF", 0, 256), A.is_gt)
-        rb = 768 * r + CAP * me
-        fused(lambda d: R("NEW", b + CAP * d, b + CAP * d + CAP), R("RPL", rb, rb + CAP), "lr%d" % r, "ra%d" % r)
-        act(R("RPL", rb, rb + CAP), R("NEW", b + CAP * me, b + CAP * me + CAP), AF.Copy)
-        landed("ra%d" % r, "RPL", 768 * r)
-        relay("BG", 16, (MS, "NEW", b))
-        ts(R("S1"), R("BG", 0, 16), 0.0, A.is_equal, 8192.0, A.mult)
-        tt(R("S2"), R("S1"), R("PF"), A.max)
-        tt(R("S3"), R("S2"), KS, A.min)
-        copy(R("SU"), R("S3"))
+            k = 240 - 16 * m
+            ts(R("EO", lo, lo + k), R("R1", 16 * m + 16, 256), SGN, A.mult, R("YM", 16 * m + 15, 16 * m + 16), A.is_equal)
+            eo.append([(R("BD", 16 * m + 16, 256), BP17, R("EO", lo, lo + k))])
+            lo += k
+        eo.insert(8, [(n, BP17, R("ED"))])
+        mm(*eo)
+        ts(R("NEW", b, b + 256), n, 0.0, A.is_le, 1.0, A.add)
+        fused(lambda d: R("NEW", b + CAP * d, b + CAP * d + CAP), "RPL", SNW * r, 512, "lr%d" % r, "ra%d" % r)
+        act(R("PF"), yp, AF.Abs)
+        ts(R("S1"), relay(R("YN"), R("NEW", b, b + 256)), NSG, A.mult, 2.0, A.add)
+        tt(R("S2"), R("S1"), KS, A.mult)
+        tt(R("S3"), R("S2"), R("PF"), A.max)
+        ts(R("SU"), R("S3"), -1.0, A.add)
         copy(I(R("STO"), R("SU")), arr)
         if r == RO - 1:
-            dma("y", "st0", (T.yt[:], []), R("STO", 0, TS))
+            dma("y", "st0", H(T.yt[:]), R("STO", 0, TS), DMA0 + 2 * TS * DMAB)
 
     def nextfront(r):
-        b = 768 * r
-        last = r == RO - 1
-        act(R("NK", 0, 224), I(R("RPL", b, b + 768), part(R("OFF"), 0, 14)), AF.Copy)
-        copy(R("NK", 224, 512), I(R("RPL", b, b + 768), part(R("OFF"), 14, 32)))
-        relay("BH", 32, (MS, "NK", 0))
-        tt(R("NL", 1, 33), R("BH", 0, 32), R("LEN"), A.mult)
-        mm(R("BD", 0, 32), [(B1, R("NL", 0, 32))])
-        mm(R("BE", 0, 32), [(TRS, R("NL", 1, 33))])
-        ts(R("NP"), R("NL", 1, 33), 0.0, A.is_equal, 2048.0, A.mult)
-        scan(R("SF"), R("BD", 0, 32), part(ZR, 0, 32), 0.0, A.add, A.add)
-        tt(R("NP2"), R("NP"), R("NL", 1, 33), A.add)
-        tt(R("ST"), R("BE", 0, 32), R("SF"), A.add)
-        tt(R("EN"), R("ST"), R("NP2"), A.add)
-        ts(R("PE1"), R("EN"), 256.0, A.is_gt, 32768.0, A.mult)
-        ts(R("KP"), R("EN"), 256.0, A.is_le)
-        tt(R("X1"), R("ST"), R("PE1"), A.max)
-        tt(R("KB"), R("KP"), R("NL", 1, 33), A.mult)
-        tt(R("X2"), R("X1"), KT, A.min)
-        mm(R("BC", 0, 32), [(B1, R("KB"))])
-        copy(R("OF2"), R("X2"))
-        op("s", lambda: g.scalar.activation(out=R("X3")[0], in_=T.BC[:, 0:32], func=AF.Copy, accum_out=R("TOT", 0, 1)[0]),
-           [("BC", 0, 32)], R("X3")[1] + R("TOT", 0, 1)[1])
-        if not last:
-            act(R("TOB", 0, 1), R("TOT", 0, 1), AF.Identity, 0.5, -1.0)
-            for k in range(2):
-                act(R("VT", 16 * k, 16 * k + 16), QT, AF.Sign, R("TOB", 0, 1))
-            act(R("VT"), R("VT"), AF.Relu, 0.0, -1.0)
-        else:
-            act(R("TOB", 0, 1), R("TOT", 0, 1), AF.Identity, 16384.0, -32768.0)
-            act(R("FM"), IQ, AF.Relu, R("TOB", 0, 1), 32768.0)
+        rp = R("RPL", SNW * r, SNW * r + SNW)
+        act(R("NK", 0, 224), I(rp, R("OFF", 0, 14)), AF.Copy)
+        copy(R("NK", 224, 512), I(rp, R("OFF", 14, 32)))
+        tt(R("NL", 1, 33), relay(R("YK"), R("NK")), R("SL"), A.mult)
+        st, en, du = R("BF", 0, 32), R("BF", 32, 64), R("BF", 64, 96)
+        l1, l0, n1, n0 = R("LN", 1, 33), R("LN", 0, 32), R("NL", 1, 33), R("NL", 0, 32)
+        mm([(st, NTRS, l1), (st, NTGE, l0), (en, NTRI, l1), (en, NTGT, l0), (du, ID[8192.0], l1)],
+           [(st, TRS, n1), (st, TGE, n0), (en, TRI, n1), (en, TGT, n0), (du, ID[-8192.0], n1)])
+        scan(R("SE"), RS2, R("BF", 0, 64), 0.0, A.mult, A.add)
+        tt(R("DU"), du, KD, A.add)
+        tt(R("X1"), R("SE", 0, 32), R("DU"), A.max)
+        copy(R("OF2"), R("X1"))
+        act(R("NR"), du, AF.Identity, 0.0, -1.0 / 8192)
+        act(R("GF"), R("SE", 32, 64), AF.Relu, 64.0 * 257, -64.0)
+        tt(R("KB"), R("NR"), R("GF"), A.min)
+        mm([(R("BG", 0, 32), B1, R("KB"))])
+        act(R("X3"), R("BG", 0, 32), AF.Copy, acc=R("TOT", 0, 1))
+        act(R("TOB", 0, 1), R("TOT", 0, 1), AF.Identity, 8192.0, -16384.0)
+        act(R("F0"), IQ, AF.Relu, R("TOB", 0, 1), 16384.0)
+        act(R("FF"), R("F0"), AF.Identity, 1.0)
+        act(R("FA"), R("F0"), AF.Relu, 0.5, -1.0)
         copy(I(R("NXT"), R("OF2")), R("T0"))
-        ts(R("NFX"), R("NXT", 0, 256), 1.0, A.is_equal)
-        scan(R("PP"), R("NFX"), R("NXT", 0, 256), 0.0, A.mult, A.add)
-        ts(R("H"), R("PP"), MAG, A.add, MAG + 16.0, A.subtract)
-        relay("BF", 16, (MSC, "H", 0))
-        if last:
-            tt(R("PP"), R("PP"), R("FM"), A.max)
-        tt(R("MD"), R("PP"), R("H"), A.subtract)
-        ts(R("M2"), R("MD"), PM85, A.is_equal)
-        copy(R("CT"), R("BF", 0, 16))
-        for y, k0 in (("YH", "KH"), ("YL", "KL")):
-            for k in range(2):
-                tt(R(y, 256 * k, 256 * k + 256), I(R(k0, TW * k, TW * k + TW), R("CT")), R("M2"), A.mult)
-        if not last:
-            relay("BG", 32, (MST, "YH", 0), (MST, "YL", 0))
+        scan(R("PP"), R("FF"), R("NXT", 0, 256), 0.0, A.add, A.max)
+        ts(R("CT"), relay(R("YQ"), R("PP")), SGN, A.mult, float(ZC), A.min)
+        tt(R("MF", 0, P, 16), R("FA"), R("NXT", 0, 256), A.is_gt)
+        if r < RO - 1:
+            copy(R("GU"), I(R("UV"), R("CT")))
+            ts(R("WI"), relay(R("YU"), R("GU")), SGN, A.mult, -1.0, A.add)
+            ts(R("UI", 16, 32), R("WI"), 4095, A.bitwise_and)
+            ts(R("UI", 0, 16), R("WI"), 12, A.arith_shift_right)
+            copy(R("FUV", 16, 32), R("UI", 16, 32))
+            copy(R("FUV", 0, 16), R("UI", 0, 16))
         else:
-            mm((T.BG[0:8, 0:512], [("BG", 0, 512)]), [(G8, R("YH")), (G8, R("YL"))])
-        ts(R("FL"), IQ, R("TOT", 0, 1), A.is_lt)
-        tt(R("NF", 0, 256), R("FL"), R("NFX"), A.mult)
-        if not last:
-            tt(R("W0"), R("BG", 0, 32), R("VT"), A.mult)
-            copy(R("FUV"), R("W0"))
-        else:
-            mm((T.BH[0:8, 0:256], [("BH", 0, 512)]), [(G8S, R("NF", 0, 256))])
-            copy(R("OUTF", 0, 512, p=(0, 8)), (T.BG[0:8, 0:512], [("BG", 0, 512)]))
-            dma("y", "st1", (T.yu[:], []), R("OUTF", 0, 256, p=(0, 8)))
-            dma("s", "st2", (T.yv[:], []), R("OUTF", 256, 512, p=(0, 8)))
-            ts(R("OUTF", 512, 768, p=(0, 8)), (T.BH[0:8, 0:256], [("BH", 0, 512)]), -1.0, A.mult, 1.0, A.add)
-            dma("s", "st3", (T.ys[:], []), R("OUTF", 512, 768, p=(0, 8)))
+            ts(R("ZI", 0, 256), I(R("UV"), R("CT")), -1.0, A.add)
+            ts(R("Z8", 0, 256), R("ZI", 0, 256), 12, A.arith_shift_right)
+            ts(R("Z8", 256, 512), R("ZI", 0, 256), 4095, A.bitwise_and)
+            copy(R("OUTF", 0, 256), R("Z8", 0, 256))
+            copy(R("OUTF", 256, 512), R("Z8", 256, 512))
+            act(R("OUTF", 512, 768), R("MF", 0, P, 16), AF.Identity, 1.0, -1.0)
+            for k, (q, y) in enumerate((("y", T.yu), ("s", T.yv), ("y", T.ys))):
+                dma(q, "st%d" % (k + 1), H(y[:]), R("OUTF", 256 * k, 256 * k + 256, p=(0, 128, 16)), DMA0)
 
     for r in range(RO):
         vphase()
-        two = {"B": qphase(), "A": comp()}
-        for x in ORDER:
-            next(two[x], None)
-        for x in two.values():
-            for _ in x:
-                pass
+        comp()
+        qphase()
+        pairs()
         keys(r)
         owner(r)
         nextfront(r)
-    for s in sorted(finals):
-        if waited.get(s, 0) < finals[s]:
-            g.wait_ge(T.sem[s], finals[s])
+
+    n = len(ops)
+    recs = {}
+    pred = []
+    for x, o in enumerate(ops):
+        ps = set()
+        for regs, wr in ((o["r"], False), (o["w"], True)):
+            for (b, lo, hi) in regs:
+                for rec in recs.get(b, []):
+                    if rec[0] < hi and lo < rec[1] and (wr or rec[2]):
+                        ps.add(rec[3])
+        if x < NLOAD:
+            ps.update(y for y in range(x) if ops[y]["q"] == o["q"])
+        pred.append(ps)
+        for (b, lo, hi) in o["w"]:
+            recs[b] = [r for r in recs.get(b, []) if not (lo <= r[0] and r[1] <= hi)] + [(lo, hi, True, x)]
+        for (b, lo, hi) in o["r"]:
+            recs.setdefault(b, []).append((lo, hi, False, x))
+
+    def gap(y, x):
+        if x < NLOAD:
+            return ops[y]["hold"]
+        return ops[y]["hold"] + ops[y]["lat"] + (0.0 if ops[x]["ch"] and ops[y]["q"] == "t" else WAKE)
+    rank = [0.0] * n
+    for x in range(n - 1, -1, -1):
+        rank[x] = max(rank[x], ops[x]["hold"] + ops[x]["lat"]) + (1e9 if x < NLOAD else 0.0)
+        for y in pred[x]:
+            rank[y] = max(rank[y], rank[x] + gap(y, x))
+    start = [0.0] * n
+    busy = {}
+    for x in sorted(range(n), key=lambda x: (-rank[x], x)):
+        t = max([start[y] + gap(y, x) for y in pred[x]] + [0.0])
+        lst = busy.setdefault(ops[x]["q"], [])
+        k = 0
+        while k < len(lst):
+            if lst[k][1] > t:
+                if lst[k][0] >= t + ops[x]["hold"]:
+                    break
+                t = lst[k][1]
+            k += 1
+        lst.insert(k, (t, t + ops[x]["hold"]))
+        start[x] = t
+
+    count = {}
+    known = {q: {} for q in queues}
+    waited = {}
+    token = {}
+    for x in sorted(range(n), key=lambda x: (start[x], x)):
+        o = ops[x]
+        q = o["q"]
+        s = o["sem"]
+        count[s] = count.get(s, 0) + abs(o["inc"])
+        if q == "n":
+            token[x] = (s, count[s], {s: count[s]})
+            continue
+        best = {}
+        for y in pred[x]:
+            if x < NLOAD or (o["ch"] and ops[y]["q"] == "t" and ops[y]["w"] == o["w"]):
+                continue
+            a, v, clk = token[y]
+            if known[q].get(a, 0) < v and best.get(a, (0, None))[0] < v:
+                best[a] = (v, clk)
+        for a in sorted(best, key=lambda a: -sum(best[a][1].values())):
+            v, clk = best[a]
+            if known[q].get(a, 0) >= v:
+                continue
+            queues[q].wait_ge(T.sem[a], v)
+            waited[a] = max(waited.get(a, 0), v)
+            known[q][a] = v
+            for b, u in clk.items():
+                known[q][b] = max(known[q].get(b, 0), u)
+        ins = o["fn"]()
+        if o["inc"] > 0:
+            ins.then_inc(T.sem[s], o["inc"])
+        clk = dict(known[q])
+        clk[s] = count[s]
+        token[x] = (s, count[s], clk)
+    for s in sorted(count):
+        if waited.get(s, 0) < count[s]:
+            g.wait_ge(T.sem[s], count[s])

@@ -9,10 +9,11 @@ RND = 1.5 * 2 ** 23
 M11 = 1.5 * 2 ** 34
 CL = 393216
 HALF = W // 2
-CH = [(0, 512), (512, 512), (1024, 1024), (2048, 1024), (3072, 512), (3584, 512)]
+CH = [(0, 256), (256, 256)] + [(512 * c, 512) for c in range(1, 8)]
 QH = [(512 * c, 512) for c in range(8)]
 AH = [(0, 1024), (1024, 1024), (2048, 1024), (3072, 512), (3584, 512)]
 EH = [(1024 * c, 1024) for c in range(4)]
+RW = 272
 DUMP = 4128
 SNW = 2560
 ZC = P + 1
@@ -24,16 +25,18 @@ def shapes(kind, dtype, text):
 
 SCRATCH = {}
 SCRATCH.update(shapes("sbuf", "int32", "KID:3456 FUI:32 FSI:256 ZI:512 Z8:512 HI:32 OW:32 WI:16 UI:32 CI:1024"))
-SCRATCH.update(shapes("sbuf", "uint16", "FUV:32 KU:512 OPU:16 JT:32 T1:32 OFF:32 PU:16 R1:256 SU:16 OF2:32 CT:16"))
+SCRATCH.update(shapes("sbuf", "uint16", "FUV:32 KU:512 OPU:16 JT:32 T1:32 OFF:32 PU:16 R1:256 SU:16 OF2:16 CT:16 OP2:2 JT2:16 KS2:16 OFS:16"))
 SCRATCH.update(shapes("sbuf", "float16", "KF:512 SEL:4096"))
-SCRATCH.update(shapes("sbuf", "bfloat16", "VEC:3456 FSB:256 LASTF:256 EQ:256 MF:4112 VV:4096 NS:4112 CU:264 AP:256 CD:264 "
+SCRATCH.update(shapes("sbuf", "bfloat16", "VEC:3456 FSB:256 LASTF:256 EQ:256 MF:4112 VV:4096 CU:264 NS:4112 AP:256 CD:264 "
                       "JW:4384 JK:512 YJ:512 JB:32 OO:512 LR:512 ZB:512 OHB:144 INV:40 STO:2320 NQ:256 NEG:256 ED:256 EO:1920 YN:256 "
-                      "NK:512 YK:512 NL:40 LN:40 SL:32 KB:32 CM:6400 RL:512 SND:2560 ARR:768 NEW:768 RPL:7680 ONE:256 J1:256 FF:256 FA:256"))
+                      "NK:256 YK:256 NL:24 LN:24 SL:16 KB:16 SNT:40 JW2:320 JK2:256 YJ2:256 JB2:16 OO2:256 SG:256 PR:256 LR2:256 "
+                      "CM:6656 RL:512 SND:2560 ARR:768 NEW:768 RPL:816 ONE:256 J1:256 FF:256 FA:256"))
 SCRATCH.update(shapes("sbuf", "float32", "MRK:3456 QV:4096 D:4640 UV:4112 SC:264 XX:256 YX:256 XC:256 LA:512 T0:512 "
-                      "RK:136 R2:72 RR:256 P1:256 NP1:256 YP:256 PMR:256 YM:256 PP:256 YQ:256 GU:256 YU:256 F0:256 OUTF:768 "
-                      "CF:768 CR:1280 SM:512"))
+                      "RK:136 R2:72 RR:256 P1:256 T2:256 YP:256 PMR:256 YM:256 PP:256 YQ:256 GU:256 YU:256 F0:256 OUTF:768 "
+                      "CF:768 CR:1280 SM:576"))
 VIEW = {}
-for _w in "RQ:32 S1:16 S2:16 S3:16 PF:16 SE:64 DU:32 X1:32 NR:32 GF:32 X3:32 TOT:8 TOB:8".split():
+for _w in ("RQ:32 S1:16 S2:16 S3:16 PF:16 SE:32 DU:16 X1:16 NR:16 GF:16 X3:16 O3:32 TH:32 O4:32 SLT:32 SC2:40 X2:32 Y2:32 XC2:32 "
+           "TOB:8").split():
     _n, _k = _w.split(":")
     VIEW[_n] = ("SM", sum(x[2] for x in VIEW.values()), int(_k))
 SAME = {"DF": "VV", "AB": "VV", "EM": "QV", "NXT": "D"}
@@ -42,7 +45,8 @@ SCRATCH.update({b: ("psum", [128, 512], "float32") for b in BANKS})
 SEMAPHORES = ["qv", "qs", "qt", "qg"] + ["ld%d" % k for k in range(9)] + ["st%d" % k for k in range(4)] + ["ac%d" % k for k in range(len(AH))] + \
              ["%s%d" % (s, r) for s in ("ka", "ra", "lk", "lr") for r in range(RO)]
 SIZE = {"int32": 4, "float32": 4, "uint16": 2, "float16": 2, "bfloat16": 2}
-CY, PC, GA, SCA, WAKE, NET, DMA0, DMAB = 0.92, 0.46, 1.56, 3.5, 80.0, 3000.0, 2000.0, 0.6
+PASSES = 8
+CY, PC, GA, SCA, WAKE, NET, DMA0, DMAB, FIX = 0.92, 0.65, 1.56, 3.5, 100.0, 2200.0, 2000.0, 0.6, 30.0
 
 
 def rank_program(g, core, T, topo):
@@ -74,7 +78,7 @@ def rank_program(g, core, T, topo):
     def put(q, fn, reads, writes, hold, lat=0.0, sem=None, inc=1, chained=False):
         w = [(x[0], 0, 512) if x[0] in BANKS else x for x in writes] + [(x[0], 0, 512) for x in reads if x[0] in BANKS]
         r = [x for x in reads if x[0] not in BANKS]
-        ops.append({"q": q, "fn": fn, "r": r, "w": w, "hold": hold, "lat": lat, "sem": sem or "q" + q, "inc": inc, "ch": chained})
+        ops.append({"q": q, "fn": fn, "r": r, "w": w, "hold": hold + (FIX if q in "vs" else 0.0), "lat": lat, "sem": sem or "q" + q, "inc": inc, "ch": chained})
 
     def R(name, lo=None, hi=None, step=None, p=None):
         name = SAME.get(name, name)
@@ -135,7 +139,7 @@ def rank_program(g, core, T, topo):
         if acc is None:
             put("s", lambda: g.scalar.activation(out=out[0], in_=in_[0], func=f, bias=va(bias), scale=va(scale)), rg(in_, bias, scale), out[1], c)
         else:
-            put("s", lambda: g.scalar.activation(out=out[0], in_=in_[0], func=f, accum_out=acc[0]), rg(in_), out[1] + acc[1], c + 20)
+            put("s", lambda: g.scalar.activation(out=out[0], in_=in_[0], func=f, bias=bias, scale=scale, accum_out=acc[0]), rg(in_), out[1] + acc[1], c + 20)
 
     def mm(*parts):
         for x, part in enumerate(parts):
@@ -171,15 +175,6 @@ def rank_program(g, core, T, topo):
         lat += SIZE[SCRATCH[b][2]] * W * DMAB
         for q, lo in (("y", 0), ("s", 64)):
             dma(q, "ld%d" % (3 + 2 * k + lo // 64), (T[b][lo:lo + 64, :], [(b, W + lo // 64, W + lo // 64 + 1)]), H(x[lo:lo + 64, :]), lat)
-    NLOAD = len(ops)
-
-    def L(name):
-        x = R(name)
-        return (x[0], [(name, 0, W + 2)]) + x[2:]
-    fill(R("MRK"), float(CL))
-    for k in range(2):
-        addto(R("MRK", HALF * k, HALF * k + HALF), H(T.mark[:, HALF * k:HALF * k + HALF]), "ld%d" % (7 + k), L("VEC")[1])
-
     free = {"CI": 0, "CF": 0, "CM": 0, "CR": 0}
 
     def new(buf, n):
@@ -193,10 +188,19 @@ def rank_program(g, core, T, topo):
     def win(m, i):
         return part(m, 15 - i, 143 - i)
 
+    def L(name):
+        x = R(name)
+        return (x[0], [(name, 0, W + 2)]) + x[2:]
     pI = new("CI", 1); cI = new("CI", 144); ktI = new("CI", 32)
     iota(pI, [[0, 1]], 0, 1, False)
     iota(cI, [[1, 144]], 0, 0, False)
     iota(ktI, [[16, 32]], 0, 0, False)
+    NLOAD = len(ops)
+    gfill(R("MRK"), CL)
+    for k in range(2):
+        addto(R("MRK", HALF * k, HALF * k + HALF), H(T.mark[:, HALF * k:HALF * k + HALF]), "ld%d" % (7 + k), L("KID")[1])
+        ops[-1]["lat"] = DMA0 + (2 * W + 4 * HALF * (k + 1)) * DMAB
+
     pmI = new("CI", 1); pgI = new("CI", 1); cgI = new("CI", 144); cmI = new("CI", 144)
     ts(pmI, pI, 15, A.bitwise_and)
     ts(pgI, pI, 4, A.arith_shift_right)
@@ -209,7 +213,7 @@ def rank_program(g, core, T, topo):
     ts(C15, CMF, 15.0, A.is_equal)
     tt(MST, BLK, C15, A.mult)
     ts(R8, part(CG, 0, 128), PX, A.is_equal)
-    gfill(R("MF"), 1)
+    fill(R("MF", 0, P), 1.0)
     fill(R("MF", P, P + 16), 0.0)
     ts(R("FSB", 0, 256, p=(0, 8)), R("FSI", 0, 256, p=(0, 8)), -1.0, A.mult, 1.0, A.add)
     r0 = R8[1][0][1]
@@ -229,19 +233,19 @@ def rank_program(g, core, T, topo):
         act(m, part(src, 0, n), AF.Identity, 0.0, by)
         return m
     B1 = part(BLK, 0, 128)
-    DK = new("CF", 128); TMP = new("CF", 128); CM1 = part(CMF, 0, 128)
+    DK = new("CF", 128); CM1 = part(CMF, 0, 128)
     ts(DK, CM1, PM, A.subtract)
 
     def masked(o, c):
         m = new("CM", 128)
-        ts(TMP, DK, c, o)
-        tt(m, TMP, B1, A.mult)
+        ts(m, DK, c, o)
+        tt(m, m, B1, A.mult)
         return m
 
     def comb(a, b, by):
         m = new("CM", 128)
-        ts(TMP, b, by, A.mult)
-        tt(m, a, TMP, A.add)
+        ts(m, b, by, A.mult)
+        tt(m, m, a, A.add)
         return m
     TRS = masked(A.is_gt, 0.0); TRI = masked(A.is_ge, 0.0); TGE = masked(A.is_le, 0.0); IDN = masked(A.is_equal, 0.0)
     TGT = masked(A.is_lt, 0.0); S0 = masked(A.is_equal, 1.0); S1 = masked(A.is_equal, -15.0)
@@ -252,19 +256,12 @@ def rank_program(g, core, T, topo):
     BP8 = scaled(BLK, 8192.0); BP17 = scaled(BLK, float(2 ** 17))
     NTRS = scaled(TRS, -1.0); NTGE = scaled(TGE, -1.0); NTRI = scaled(TRI, -1.0); NTGT = scaled(TGT, -1.0)
     ID = {}
-    for c in (94.0, 128.0, float(DUMP), float(2 ** 20), 512.0, -512.0, -4096.0, 4096.0, 8192.0, -8192.0, -1024.0, 0.5 - me / 4, 1.0 - me / 4):
+    for c in (-1.0, float(RW), 94.0, 128.0, float(DUMP), float(2 ** 20), 512.0, -512.0, -4096.0, 4096.0, 8192.0, -8192.0, -1024.0, 0.5 - me / 4, 1.0 - me / 4):
         if c not in ID:
             ID[c] = scaled(IDN, c)
     K1 = new("CR", 512); IQ = new("CR", 256); KT1 = new("CR", 32); KD = new("CR", 32); KS = new("CR", 16); ZR = new("CR", 264)
     RS = new("CM", 136); PADC = new("CM", 136); RS2 = new("CM", 64)
-    iota(K1, [[1, 512]], 1 - 4096, 0)
-    iota(IQ, [[1, 256]], 0, 0)
-    iota(R("J1"), [[1, 256]], 1, 0)
-    gfill(R("ONE"), 1)
-    gfill(R("STO"), -1)
-    gfill(ZR, 0)
-    for r in range(RO):
-        fill(R("RPL", SNW * r, SNW * r + SNW), 1.0)
+    fill(ZR, 0.0)
     ts(KT1, ktI, PM, A.add, 1.0, A.add)
     ts(KD, KT1, float(DUMP - 1), A.add)
     ts(KS, part(KT1, 0, 16), float(TS + 16), A.add)
@@ -272,29 +269,34 @@ def rank_program(g, core, T, topo):
     for o in range(N):
         fill(part(RS, 34 * o + 1, 34 * o + 2), 0.0)
         fill(part(PADC, 34 * o + 1, 34 * o + 2), 512.0 * o - 4096.0)
-    fill(part(RS2, 32, 33), 0.0)
+    fill(part(RS2, 16, 17), 0.0)
     fill(R("OHB"), 0.0); fill(R("CD"), 0.0); fill(R("CU"), -1.0); fill(R("NL"), 0.0); fill(R("LN"), 0.0); fill(R("INV"), 0.0)
-    fill(R("NS", 0, 16), 0.0)
+    fill(R("NS", 0, 16), 0.0); fill(R("SNT"), 0.0)
     fill(R("UV", 0, 8), 1.0); fill(R("UV", P, P + 16), 1.0)
     copy(R("CU", 1, 2), SGN)
-    aI = new("CI", 512)
-    iota(aI, [[0, 32], [1, 16]], 0, 0, False)
-    PN = new("CF", 1)
-    ts(PN, PM, 1.0, A.add, 16.0, A.is_lt)
-    ts(PN, PM, 1.0, A.add, PN, A.mult)
-    ts(R("LA"), aI, PM, A.is_equal, -float(2 ** 40), A.mult)
-    ts(R("T0"), aI, PN, A.is_equal, -2.0, A.mult)
-    tt(R("LA"), R("LA"), R("T0"), A.add)
-    ts(R("RL"), R("LA"), 1.0, A.add)
+    ts(R("LR", 0, 128), DK, 0.0, A.is_equal, -float(2 ** 40), A.mult)
+    ts(R("LR", 128, 256), DK, 1.0, A.is_equal, -2.0, A.mult)
+    ts(R("LR", 256, 384), DK, -15.0, A.is_equal, -2.0, A.mult)
+    tt(R("LR", 0, 128), R("LR", 0, 128), R("LR", 128, 256), A.add)
+    tt(R("LR", 0, 128), R("LR", 0, 128), R("LR", 256, 384), A.add)
+    for k in range(4):
+        act(R("RL", 128 * k, 128 * k + 128), R("LR", 0, 128), AF.Identity, 1.0)
+    OH = new("CF", 16)
+    ts(OH, part(CMF, 0, 16), PM, A.is_equal)
+
+    def row(i, k):
+        return R("SEL", 256 * i + 128 * k, 256 * i + 128 * k + 128)
     for i in range(16):
-        c = new("CF", 1) if i < 2 else (cs[i % 2])
-        if i == 0:
-            cs = [c]
-        elif i == 1:
-            cs.append(c)
-        ts(c, PM, float(i), A.is_equal)
-        ts(R("SEL", 256 * i, 256 * i + 128), B1, c, A.mult, 4096.0, A.mult)
-        ts(R("SEL", 256 * i + 128, 256 * i + 256), B1, c, A.mult)
+        ts(row(i, 0), B1, part(OH, i, i + 1), A.mult, 4096.0, A.mult)
+        ts(row(i, 1), B1, part(OH, i, i + 1), A.mult)
+    NSET = len(ops)
+    iota(K1, [[1, 512]], 1 - 4096, 0)
+    iota(IQ, [[1, 256]], 0, 0)
+    iota(R("J1"), [[1, 256]], 1, 0)
+    gfill(R("ONE"), 1)
+    for a in range(0, TS + 272, 464):
+        gfill(R("STO", a, a + 464), -1)
+    gfill(R("RPL"), 1)
 
     def sums(out, m, b, lo):
         return [(out, win(m, i), R(b, lo + i, lo + 16 * out[2], 16)) for i in range(16)]
@@ -312,16 +314,18 @@ def rank_program(g, core, T, topo):
             gfill(R("SND", 512 * o, 512 * o + CAP), -1)
         for c, (a, n) in enumerate(CH):
             act(R("VV", a, a + n), I(L("VEC"), R("KU", 256 + a // 16, 256 + (a + n) // 16)), AF.Copy)
+            ops[-1]["up"] = 1000.0 if c < 2 else 0.0
             tt(R("DF", a, a + n), I(L("VEC"), R("KU", a // 16, (a + n) // 16)), R("VV", a, a + n), A.subtract)
             scan(R("D", a, a + n), R("MF", a, a + n), R("DF", a, a + n), R("D", a - 1, a) if a else 0.0, A.mult, A.add)
             act(R("AB", a, a + n), R("D", a, a + n), AF.Abs)
-            j0, j1 = a // 16, (a + n) // 16
-            mm([(R("BA", j0, j1), win(MSL, 15), R("LASTF", j0, j1))] + sums(R("BA", j0, j1), MST, "AB", a))
+        for a, n in AH:
+            b = R("BA", a // 16, (a + n) // 16)
+            mm([(b, win(MSL, 15), R("LASTF", a // 16, (a + n) // 16))] + sums(b, MST, "AB", a))
+        act(R("CU", 2, 258), R("BA", 0, 256), AF.Sign, 0.5, -1.0)
 
     def comp():
         ts(R("KF"), R("KU"), -float(HALF), A.add)
         tt(R("EQ"), R("KF", 0, 256), R("KF", 256, 512), A.is_equal)
-        act(R("CU", 2, 258), R("BA", 0, 256), AF.Sign, 0.5, -1.0)
         z, b = R("BD", 0, 256), R("BE", 0, 256)
         mm([(b, ID[128.0], R("EQ"))], [(b, A0C, R("CU", 2, 258)), (b, A1, R("CU", 1, 257)), (b, TGE, R("CU", 0, 256))])
         mm([(z, ID[94.0], R("ONE"))], [(z, A0, R("CU", 2, 258)), (z, A1, R("CU", 1, 257)), (z, TGE, R("CU", 0, 256))])
@@ -363,12 +367,12 @@ def rank_program(g, core, T, topo):
     def pairs():
         for i in range(16):
             b = R(("BB", "BC")[i % 2], 0, 256)
-            mm([(b, R("SEL", 256 * i, 256 * i + 128), R("KF", 0, 256)), (b, R("SEL", 256 * i + 128, 256 * i + 256), R("KF", 256, 512))])
+            mm([(b, row(i, 0), R("KF", 0, 256)), (b, row(i, 1), R("KF", 256, 512))])
             act(R("UV", 1 + i, 1 + P, 16), b, AF.Identity, float(4097 * HALF + 1))
 
-    def fused(src, buf, base, step, lsem, rsem):
+    def fused(src, buf, base, step, lsem, rsem, ready=()):
         m = masks(me)
-        tr, rd, tot = [], [], 0
+        tr, rd, tot = [], list(ready), 0
         dst = R(buf, base + step * me, base + step * me + CAP)
         for d in range(N):
             if d != me:
@@ -401,16 +405,46 @@ def rank_program(g, core, T, topo):
         tt(R("RQ"), R("R2", 0, 32), R("R2", 34, 66), A.max)
         copy(R("OFF"), R("RQ"))
         copy(I(R("SND"), R("OFF")), R("ZB"))
-        fused(lambda d: R("SND", 512 * d, 512 * d + CAP), "ARR", 256 * r, CAP, "lk%d" % r, "ka%d" % r)
+        fused(lambda d: R("SND", 512 * d, 512 * d + CAP), "ARR", 256 * r, CAP, "lk%d" % r, "ka%d" % r,
+              R("RPL", RW * r, RW * r + RW)[1])
         gfill(R("NXT", 0, 256), 0)
         act(R("LA"), I(R("EM"), R("T1")), AF.Identity, RND, 1.0 / CL)
         act(R("LR"), R("LA"), AF.Identity, -RND)
         t = R("BE")
         mm([(t, B1, R("JK")), (t, BI, R("OO")), (t, BL, R("LR"))])
         act(R("T0"), t, AF.Identity, -14.0)
-        t = R("BG", 0, 32)
-        mm(sums(t, MS, "LR", 0))
-        act(R("LN", 1, 33), t, AF.Copy)
+        gfill(R("JW2", 0, 256), 0)
+        ts(R("O3"), R("OW"), 3.0, A.min)
+        act(R("TH"), R("O3"), AF.Identity, 64.0, 512.0)
+        act(R("O4"), R("O3"), AF.Identity, -256.0, -448.0)
+        tt(R("SNT", 1, 33), R("RQ"), R("TH"), A.is_lt)
+        tt(R("SLT"), R("RQ"), R("O4"), A.add)
+        b, x, t = R("BG", 0, 33), R("BG", 64, 96), R("BG", 96, 128)
+        mm([(x, IDN, R("J1", 0, 32)), (x, ID[float(RW)], R("ONE", 0, 32))],
+           [(b, B1, R("SNT", 0, 33)), (x, BN8, R("SNT", 1, 33)), (t, TRX, R("SNT", 1, 33))])
+        scan(R("SC2", 0, 33), b, part(ZR, 0, 33), 1.0, A.add, A.add)
+        tt(R("X2"), x, R("SC2", 0, 32), A.max)
+        ts(R("OP2"), relay(R("Y2"), R("X2")), SGN, A.mult, -1.0, A.add)
+        tt(R("XC2"), t, R("SC2", 0, 32), A.add)
+        copy(I(R("JW2"), R("OP2")), R("J1", 0, 32))
+        scan(R("JK2"), R("JW2", 0, 256), R("JW2", 0, 256), 1.0, A.max, A.max)
+        y = relay(R("YJ2"), R("JK2"))
+        ts(R("JT2"), y, SGN, A.mult, -1.0, A.add)
+        act(R("JB2"), y, AF.Identity, 0.0, SG16)
+        tt(R("OO2"), I(R("XC2"), R("JT2")), part(K1, 0, 256), A.is_equal)
+        act(R("SG"), I(R("SLT"), R("JT2")), AF.Copy)
+        tt(R("PR"), R("OO2"), R("SG"), A.mult)
+        t = R("BG", 0, 16)
+        mm([(t, IDN, R("JB2"))], sums(t, MSI, "OO2", 0))
+        ts(R("KS2"), t, -16.0, A.add)
+        t = R("BF", 0, 16)
+        mm(sums(t, MST, "PR", 0))
+        ts(R("OFS"), t, 256.0, A.add)
+        act(R("LR2"), I(R("LR"), R("KS2")), AF.Copy)
+        act(R("T2"), I(R("T0"), R("KS2")), AF.Copy)
+        t = R("BG", 0, 16)
+        mm(sums(t, MS, "LR2", 0))
+        act(R("LN", 1, 17), t, AF.Copy)
         act(R("SL"), t, AF.Identity, 0.0, SGN)
 
     def owner(r):
@@ -427,10 +461,10 @@ def rank_program(g, core, T, topo):
         s, n = R("BA", 0, 256), R("BD", 0, 256)
         mm([(s, ID[4096.0], R("ONE")), (s, BP8, R("NEG"))], [(s, BN4, R("NQ"))])
         copy(R("R1"), R("P1"))
-        act(R("NP1"), R("P1"), AF.Identity, 0.0, -1.0)
+        act(R("BE", 0, 256), R("P1"), AF.Identity, 0.0, -1.0)
         tt(R("PMR"), s, R("P1"), A.max)
         relay(R("YM"), R("PMR"))
-        tt(R("ED"), R("YM"), R("NP1"), A.is_equal)
+        tt(R("ED"), R("YM"), R("BE", 0, 256), A.is_equal)
         eo = [[(n, ID[4096.0], R("ONE")), (n, BP8, R("NEG")), (n, BN4, R("NQ"))]]
         lo = 0
         for m in range(15):
@@ -441,7 +475,7 @@ def rank_program(g, core, T, topo):
         eo.insert(8, [(n, BP17, R("ED"))])
         mm(*eo)
         ts(R("NEW", b, b + 256), n, 0.0, A.is_le, 1.0, A.add)
-        fused(lambda d: R("NEW", b + CAP * d, b + CAP * d + CAP), "RPL", SNW * r, 512, "lr%d" % r, "ra%d" % r)
+        fused(lambda d: R("NEW", b + CAP * d, b + CAP * d + CAP), "RPL", RW * r, CAP, "lr%d" % r, "ra%d" % r)
         act(R("PF"), yp, AF.Abs)
         ts(R("S1"), relay(R("YN"), R("NEW", b, b + 256)), NSG, A.mult, 2.0, A.add)
         tt(R("S2"), R("S1"), KS, A.mult)
@@ -452,31 +486,32 @@ def rank_program(g, core, T, topo):
             dma("y", "st0", H(T.yt[:]), R("STO", 0, TS), DMA0 + 2 * TS * DMAB)
 
     def nextfront(r):
-        rp = R("RPL", SNW * r, SNW * r + SNW)
-        act(R("NK", 0, 224), I(rp, R("OFF", 0, 14)), AF.Copy)
-        copy(R("NK", 224, 512), I(rp, R("OFF", 14, 32)))
-        tt(R("NL", 1, 33), relay(R("YK"), R("NK")), R("SL"), A.mult)
-        st, en, du = R("BF", 0, 32), R("BF", 32, 64), R("BF", 64, 96)
-        l1, l0, n1, n0 = R("LN", 1, 33), R("LN", 0, 32), R("NL", 1, 33), R("NL", 0, 32)
+        rp = R("RPL", RW * r, RW * r + RW)
+        act(R("NK", 0, 96), I(rp, R("OFS", 0, 6)), AF.Copy)
+        copy(R("NK", 96, 256), I(rp, R("OFS", 6, 16)))
+        tt(R("NL", 1, 17), relay(R("YK"), R("NK")), R("SL"), A.mult)
+        st, en, du = R("BF", 0, 16), R("BF", 16, 32), R("BF", 32, 48)
+        l1, l0, n1, n0 = R("LN", 1, 17), R("LN", 0, 16), R("NL", 1, 17), R("NL", 0, 16)
         mm([(st, NTRS, l1), (st, NTGE, l0), (en, NTRI, l1), (en, NTGT, l0), (du, ID[8192.0], l1)],
            [(st, TRS, n1), (st, TGE, n0), (en, TRI, n1), (en, TGT, n0), (du, ID[-8192.0], n1)])
-        scan(R("SE"), RS2, R("BF", 0, 64), 0.0, A.mult, A.add)
-        tt(R("DU"), du, KD, A.add)
-        tt(R("X1"), R("SE", 0, 32), R("DU"), A.max)
+        scan(R("SE"), part(RS2, 0, 32), R("BF", 0, 32), 0.0, A.mult, A.add)
+        tt(R("DU"), du, part(KD, 0, 16), A.add)
+        tt(R("X1"), R("SE", 0, 16), R("DU"), A.max)
         copy(R("OF2"), R("X1"))
+        act(R("GF"), R("SE", 16, 32), AF.Relu, 64.0 * 257, -64.0)
         act(R("NR"), du, AF.Identity, 0.0, -1.0 / 8192)
-        act(R("GF"), R("SE", 32, 64), AF.Relu, 64.0 * 257, -64.0)
         tt(R("KB"), R("NR"), R("GF"), A.min)
-        mm([(R("BG", 0, 32), B1, R("KB"))])
-        act(R("X3"), R("BG", 0, 32), AF.Copy, acc=R("TOT", 0, 1))
-        act(R("TOB", 0, 1), R("TOT", 0, 1), AF.Identity, 8192.0, -16384.0)
+        mm([(R("BG", 0, 16), B1, R("KB"))])
+        act(R("X3"), R("BG", 0, 16), AF.Identity, 512.0, -16384.0, R("TOB", 0, 1))
         act(R("F0"), IQ, AF.Relu, R("TOB", 0, 1), 16384.0)
         act(R("FF"), R("F0"), AF.Identity, 1.0)
         act(R("FA"), R("F0"), AF.Relu, 0.5, -1.0)
-        copy(I(R("NXT"), R("OF2")), R("T0"))
+        copy(I(R("NXT"), R("OF2")), R("T2"))
         scan(R("PP"), R("FF"), R("NXT", 0, 256), 0.0, A.add, A.max)
         ts(R("CT"), relay(R("YQ"), R("PP")), SGN, A.mult, float(ZC), A.min)
-        tt(R("MF", 0, P, 16), R("FA"), R("NXT", 0, 256), A.is_gt)
+        act(R("NEG"), R("NXT", 0, 256), AF.Relu, 1.0, -1.0)
+        mm([(R("BH", 0, 256), IDN, R("FA"))], [(R("BH", 0, 256), IDN, R("NEG"))])
+        act(R("MF", 0, P, 16), R("BH", 0, 256), AF.Relu, -2.0, 2.0)
         if r < RO - 1:
             copy(R("GU"), I(R("UV"), R("CT")))
             ts(R("WI"), relay(R("YU"), R("GU")), SGN, A.mult, -1.0, A.add)
@@ -527,23 +562,49 @@ def rank_program(g, core, T, topo):
         return ops[y]["hold"] + ops[y]["lat"] + (0.0 if ops[x]["ch"] and ops[y]["q"] == "t" else WAKE)
     rank = [0.0] * n
     for x in range(n - 1, -1, -1):
-        rank[x] = max(rank[x], ops[x]["hold"] + ops[x]["lat"]) + (1e9 if x < NLOAD else 0.0)
+        rank[x] = max(rank[x], ops[x]["hold"] + ops[x]["lat"]) + (1e9 if x < NLOAD else ops[x].get("up", 0.0))
         for y in pred[x]:
             rank[y] = max(rank[y], rank[x] + gap(y, x))
-    start = [0.0] * n
-    busy = {}
-    for x in sorted(range(n), key=lambda x: (-rank[x], x)):
-        t = max([start[y] + gap(y, x) for y in pred[x]] + [0.0])
-        lst = busy.setdefault(ops[x]["q"], [])
-        k = 0
-        while k < len(lst):
-            if lst[k][1] > t:
-                if lst[k][0] >= t + ops[x]["hold"]:
-                    break
-                t = lst[k][1]
-            k += 1
-        lst.insert(k, (t, t + ops[x]["hold"]))
-        start[x] = t
+    succ = [[] for _ in range(n)]
+    for x in range(n):
+        for y in pred[x]:
+            succ[y].append(x)
+
+    def place(order, back):
+        at = [0.0] * n
+        busy = {}
+        for x in order:
+            h = ops[x]["hold"]
+            if back:
+                t = max([at[y] + ops[y]["hold"] + gap(x, y) - h for y in succ[x]] + [ops[x]["lat"]])
+            else:
+                t = max([at[y] + gap(y, x) for y in pred[x]] + [0.0])
+            lst = busy.setdefault(ops[x]["q"], [])
+            a, b = 0, len(lst)
+            while a < b:
+                m = (a + b) // 2
+                if lst[m][1] > t:
+                    b = m
+                else:
+                    a = m + 1
+            while a < len(lst) and lst[a][0] < t + h:
+                t = lst[a][1]
+                a += 1
+            lst.insert(a, (t, t + h))
+            at[x] = t
+        return at
+
+    def first(x):
+        return 0 if x < NLOAD else 1 if x < NSET else 2
+    order = sorted(range(n), key=lambda x: (first(x), -rank[x], x))
+    start, span = None, None
+    for _ in range(PASSES):
+        at = place(order, False)
+        e = max(at[x] + ops[x]["hold"] + ops[x]["lat"] for x in range(n))
+        if span is None or e < span:
+            start, span = at, e
+        bk = place(sorted(range(n), key=lambda x: (-at[x] - ops[x]["hold"], -x)), True)
+        order = sorted(range(n), key=lambda x: (first(x), -bk[x] - ops[x]["hold"], x))
 
     count = {}
     known = {q: {} for q in queues}

@@ -1,3 +1,4 @@
+import math
 from concourse.bass import DstId, RemoteDMATransfer
 from concourse.mybir import AluOpType, ActivationFunctionType
 
@@ -12,10 +13,12 @@ HALF = W // 2
 CH = [(0, 256), (256, 256)] + [(512 * c, 512) for c in range(1, 8)]
 QH = [(512 * c, 512) for c in range(8)]
 AH = [(0, 1024), (1024, 1024), (2048, 1024), (3072, 512), (3584, 512)]
-EH = [(1024 * c, 1024) for c in range(4)]
+EH = AH
+BH = AH
+RC = [3584]
+EV = 11
 RW = 272
 DUMP = 4128
-SNW = 2560
 ZC = P + 1
 
 
@@ -24,19 +27,19 @@ def shapes(kind, dtype, text):
 
 
 SCRATCH = {}
-SCRATCH.update(shapes("sbuf", "int32", "KID:3456 FUI:32 FSI:256 ZI:512 Z8:512 HI:32 OW:32 WI:16 UI:32 CI:1024"))
-SCRATCH.update(shapes("sbuf", "uint16", "FUV:32 KU:512 OPU:16 JT:32 T1:32 OFF:32 PU:16 R1:256 SU:16 OF2:16 CT:16 OP2:2 JT2:16 KS2:16 OFS:16"))
-SCRATCH.update(shapes("sbuf", "float16", "KF:512 SEL:4096"))
-SCRATCH.update(shapes("sbuf", "bfloat16", "VEC:3456 FSB:256 LASTF:256 EQ:256 MF:4112 VV:4096 CU:264 NS:4112 AP:256 CD:264 "
-                      "JW:4384 JK:512 YJ:512 JB:32 OO:512 LR:512 ZB:512 OHB:144 INV:40 STO:2320 NQ:256 NEG:256 ED:256 EO:1920 YN:256 "
-                      "NK:256 YK:256 NL:24 LN:24 SL:16 KB:16 SNT:40 JW2:320 JK2:256 YJ2:256 JB2:16 OO2:256 SG:256 PR:256 LR2:256 "
-                      "CM:6656 RL:512 SND:2560 ARR:768 NEW:768 RPL:816 ONE:256 J1:256 FF:256 FA:256"))
+SCRATCH.update(shapes("sbuf", "int32", "KID:3456 FUI:32 FSI:256 ZI:512 Z8:512 HI:32 OW:32 WI:16 UI:16 CI:64"))
+SCRATCH.update(shapes("sbuf", "uint16", "FUV:32 KU:512 OPU:16 JT:32 T1:32 OFF:32 PU:16 R1:256 SU:16 OF2:16 CT:16 OP2:2 REP:10 JT2:16 KS2:16 OFS:16"))
+SCRATCH.update(shapes("sbuf", "float16", "KF:512"))
+SCRATCH.update(shapes("sbuf", "bfloat16", "VEC:3456 FSB:256 LASTF:256 EQ:256 MF:4112 VV:4096 CU:264 NS:4112 AP:256 CD:264 SEL:4096 "
+                      "JW:4384 JK:512 YJ:512 JB:32 OO:512 LR:512 ZB:512 OHB:160 INV:40 STO:2320 NQ:256 NEG:256 ED:256 EO:2240 YN:256 "
+                      "NK:256 YK:272 LN:24 KB:16 SNT:40 JW2:320 JK2:256 YJ2:256 JB2:16 OO2:256 SG:256 PR:256 LR2:256 "
+                      "CM:7168 RL:512 SND:4096 ARR:768 NEW:768 RPL:816 ONE:256 J1:256 FF:256 FA:256 QB:%d CC:512" % max(16, 1024 * len(RC))))
 SCRATCH.update(shapes("sbuf", "float32", "MRK:3456 QV:4096 D:4640 UV:4112 SC:264 XX:256 YX:256 XC:256 LA:512 T0:512 "
                       "RK:136 R2:72 RR:256 P1:256 T2:256 YP:256 PMR:256 YM:256 PP:256 YQ:256 GU:256 YU:256 F0:256 OUTF:768 "
-                      "CF:768 CR:1280 SM:576"))
+                      "CF:1152 CR:1536 SM:576"))
 VIEW = {}
 for _w in ("RQ:32 S1:16 S2:16 S3:16 PF:16 SE:32 DU:16 X1:16 NR:16 GF:16 X3:16 O3:32 TH:32 O4:32 SLT:32 SC2:40 X2:32 Y2:32 XC2:32 "
-           "TOB:8").split():
+           "TOB:8 YB:32").split():
     _n, _k = _w.split(":")
     VIEW[_n] = ("SM", sum(x[2] for x in VIEW.values()), int(_k))
 SAME = {"DF": "VV", "AB": "VV", "EM": "QV", "NXT": "D"}
@@ -45,8 +48,17 @@ SCRATCH.update({b: ("psum", [128, 512], "float32") for b in BANKS})
 SEMAPHORES = ["qv", "qs", "qt", "qg"] + ["ld%d" % k for k in range(9)] + ["st%d" % k for k in range(4)] + ["ac%d" % k for k in range(len(AH))] + \
              ["%s%d" % (s, r) for s in ("ka", "ra", "lk", "lr") for r in range(RO)]
 SIZE = {"int32": 4, "float32": 4, "uint16": 2, "float16": 2, "bfloat16": 2}
-PASSES = 8
-CY, PC, GA, SCA, WAKE, NET, DMA0, DMAB, FIX = 0.92, 0.65, 1.56, 3.5, 100.0, 2200.0, 2000.0, 0.6, 30.0
+WAKE, NET, DMA0, DMAB = 120.0, 2150.0, 2000.0, 0.5
+PACE = ((0.83, 0.6, 1.56, 3.0, 50.0), (1.2, 0.95, 2.0, 5.5, 30.0), (0.83, 0.55, 1.15, 2.0, 40.0))
+WEIGHT = (1.0, 0.5, 1.0)
+TRIES, HEAT, SEED = 45000, 40.0, 12345
+ORDER = {}
+
+
+def lasts(q, c, pace):
+    if not isinstance(c, tuple):
+        return c
+    return c[0] + pace[0] * (c[1] + pace[2] * c[2] + pace[3] * c[3]) + pace[1] * c[4] + (pace[4] if q in "vs" else 0.0) + (15.0 if q == "s" else 0.0)
 
 
 def rank_program(g, core, T, topo):
@@ -65,6 +77,8 @@ def rank_program(g, core, T, topo):
         for ds in (out, on):
             if ds:
                 lst = [e for e in topo.engines(s, cores[ds[0]]) if e not in used]
+                if ds is on and out:
+                    lst = lst[::max(1, len(lst) // (len(on) * len(res[out[0]])))]
                 n = 1
                 while n * 2 * len(ds) <= len(lst):
                     n *= 2
@@ -75,10 +89,11 @@ def rank_program(g, core, T, topo):
 
     ops = []
 
-    def put(q, fn, reads, writes, hold, lat=0.0, sem=None, inc=1, chained=False):
-        w = [(x[0], 0, 512) if x[0] in BANKS else x for x in writes] + [(x[0], 0, 512) for x in reads if x[0] in BANKS]
-        r = [x for x in reads if x[0] not in BANKS]
-        ops.append({"q": q, "fn": fn, "r": r, "w": w, "hold": hold + (FIX if q in "vs" else 0.0), "lat": lat, "sem": sem or "q" + q, "inc": inc, "ch": chained})
+    def put(q, fn, reads, writes, hold, lat=0.0, sem=None, inc=1, chained=False, load=0.0):
+        w = [(x[0], 0, 512) if x[0] in BANKS else x for x in writes]
+        r = [(x[0], 0, 512) if x[0] in BANKS else x for x in reads]
+        ops.append({"q": q, "fn": fn, "r": r, "w": w, "hold": [lasts(q, hold, p) for p in PACE], "lat": lat, "sem": sem or "q" + q,
+                    "inc": inc, "ch": chained, "load": load})
 
     def R(name, lo=None, hi=None, step=None, p=None):
         name = SAME.get(name, name)
@@ -108,13 +123,13 @@ def rank_program(g, core, T, topo):
 
     def cost(out, *ins, both=False):
         if out[5]:
-            return 50 + out[2] * SCA * CY
+            return (50, 0, 0, out[2], 0)
         if ins and ins[0][5]:
-            return 50 + out[2] * GA * CY
+            return (50, 0, out[2], 0, 0)
         f = 0.5 if all(x[3] == 2 for x in (out,) + ins) else 1.0
         if both and not any(x[4] for x in ins):
             f *= 2
-        return max(64, out[2] * f) * CY
+        return (0, max(64, out[2] * f), 0, 0, 0)
 
     def copy(out, in_):
         put("v", lambda: g.vector.tensor_copy(out=out[0], in_=in_[0]), rg(in_) + out[1][1:], out[1][:1], cost(out, in_))
@@ -135,11 +150,11 @@ def rank_program(g, core, T, topo):
         put("v", lambda: g.vector.memset(out[0], c), [], out[1], cost(out))
 
     def act(out, in_, f, bias=0.0, scale=1.0, acc=None):
-        c = 65 + out[2] * GA * CY if in_[5] else max(64, out[2]) * CY
+        c = (65, 0, out[2], 0, 0) if in_[5] else (0, max(64, out[2]), 0, 0, 0)
         if acc is None:
             put("s", lambda: g.scalar.activation(out=out[0], in_=in_[0], func=f, bias=va(bias), scale=va(scale)), rg(in_, bias, scale), out[1], c)
         else:
-            put("s", lambda: g.scalar.activation(out=out[0], in_=in_[0], func=f, bias=bias, scale=scale, accum_out=acc[0]), rg(in_), out[1] + acc[1], c + 20)
+            put("s", lambda: g.scalar.activation(out=out[0], in_=in_[0], func=f, bias=bias, scale=scale, accum_out=acc[0]), rg(in_), out[1] + acc[1], c)
 
     def mm(*parts):
         for x, part in enumerate(parts):
@@ -148,33 +163,25 @@ def rank_program(g, core, T, topo):
                 for k, (o, l, r) in enumerate(part):
                     ins = g.tensor.matmul(out=o[0], lhsT=l[0], rhs=r[0], start=(first and k == 0), stop=(last and k == len(part) - 1))
                 return ins
-            put("t", fn, rg(*[y for p in part for y in p[1:]]), part[0][0][1], sum(max(64, p[0][2]) for p in part) * PC, chained=(x > 0))
+            put("t", fn, rg(*[y for p in part for y in p[1:]]), part[0][0][1], (0, 0, 0, 0, sum(max(64, p[0][2]) * (p[2][3] ** 2 // 4) for p in part)), chained=(x > 0))
 
     def iota(out, pat, base, cm, flag=True):
         if flag:
-            put("g", lambda: g.iota(out[0], pat, base, cm, allow_small_or_imprecise_dtypes=True), [], out[1], 130 + 2 * out[2] * CY)
+            put("g", lambda: g.iota(out[0], pat, base, cm, allow_small_or_imprecise_dtypes=True), [], out[1], (130, 2 * out[2], 0, 0, 0))
         else:
-            put("g", lambda: g.iota(out[0], pat, base, cm), [], out[1], 130 + 2 * out[2] * CY)
+            put("g", lambda: g.iota(out[0], pat, base, cm), [], out[1], (130, 2 * out[2], 0, 0, 0))
 
     def gfill(out, c):
         iota(out, [[0, out[2]]], c, 0)
 
     queues = {"v": g.vector, "s": g.scalar, "t": g.tensor, "g": g, "y": g.sync}
 
-    def dma(q, sem, out, in_, lat, after=()):
-        put(q, lambda: queues[q].dma_start(out=out[0], in_=in_[0]), in_[1] + list(after), out[1], 60.0, lat, sem, 16)
+    def dma(q, sem, out, in_, load):
+        put(q, lambda: queues[q].dma_start(out=out[0], in_=in_[0]), in_[1], out[1], 60.0, DMA0 - 500.0, sem, 16, load=load * DMAB + 1.0)
 
     def addto(out, in_, sem, after=()):
-        put("g", lambda: g.dma_start(out=out[0], in_=in_[0], accum_op=A.add), in_[1] + list(after), out[1], 600.0, DMA0 + 4 * out[2] * DMAB, sem, 16)
+        put("g", lambda: g.dma_start(out=out[0], in_=in_[0], accum_op=A.add), in_[1] + list(after), out[1], 600.0, DMA0, sem, 16, load=4 * out[2] * DMAB)
 
-    dma("y", "ld0", R("FUI", 0, 16), H(T.fu[:]), DMA0)
-    dma("s", "ld1", R("FUI", 16, 32), H(T.fv[:]), DMA0)
-    dma("s", "ld2", R("FSI", 0, 256, p=(0, 8)), H(T.fs[:]), DMA0)
-    lat = DMA0
-    for k, (b, x) in enumerate((("KID", T.kids), ("VEC", T.vec))):
-        lat += SIZE[SCRATCH[b][2]] * W * DMAB
-        for q, lo in (("y", 0), ("s", 64)):
-            dma(q, "ld%d" % (3 + 2 * k + lo // 64), (T[b][lo:lo + 64, :], [(b, W + lo // 64, W + lo // 64 + 1)]), H(x[lo:lo + 64, :]), lat)
     free = {"CI": 0, "CF": 0, "CM": 0, "CR": 0}
 
     def new(buf, n):
@@ -191,55 +198,57 @@ def rank_program(g, core, T, topo):
     def L(name):
         x = R(name)
         return (x[0], [(name, 0, W + 2)]) + x[2:]
-    pI = new("CI", 1); cI = new("CI", 144); ktI = new("CI", 32)
+
+    dma("y", "ld0", R("FUI", 0, 16), H(T.fu[:]), 64)
+    dma("s", "ld1", R("FUI", 16, 32), H(T.fv[:]), 64)
+    dma("s", "ld2", R("FSI", 0, 256, p=(0, 8)), H(T.fs[:]), 64)
+    for k, (b, x) in enumerate((("KID", T.kids), ("VEC", T.vec))):
+        for q, lo in (("y", 0), ("s", 64)):
+            dma(q, "ld%d" % (3 + 2 * k + lo // 64), (T[b][lo:lo + 64, :], [(b, W + lo // 64, W + lo // 64 + 1)]), H(x[lo:lo + 64, :]),
+                SIZE[SCRATCH[b][2]] * HALF)
+    pI = new("CI", 1); CG = new("CF", 144); CMF = new("CF", 144); PX = new("CF", 1)
     iota(pI, [[0, 1]], 0, 1, False)
-    iota(cI, [[1, 144]], 0, 0, False)
-    iota(ktI, [[16, 32]], 0, 0, False)
+    iota(CG, [[1, 9], [0, 16]], 0, 0)
+    iota(CMF, [[0, 9], [1, 16]], 0, 0)
+    iota(PX, [[0, 1]], 0, 1)
     NLOAD = len(ops)
-    gfill(R("MRK"), CL)
+    fill(R("MRK", 0, HALF), float(CL))
+    gfill(R("MRK", HALF, W), CL)
     for k in range(2):
         addto(R("MRK", HALF * k, HALF * k + HALF), H(T.mark[:, HALF * k:HALF * k + HALF]), "ld%d" % (7 + k), L("KID")[1])
-        ops[-1]["lat"] = DMA0 + (2 * W + 4 * HALF * (k + 1)) * DMAB
 
-    pmI = new("CI", 1); pgI = new("CI", 1); cgI = new("CI", 144); cmI = new("CI", 144)
+    pmI = new("CI", 1); pgI = new("CI", 1); PM = new("CF", 1); PG = new("CF", 1)
     ts(pmI, pI, 15, A.bitwise_and)
     ts(pgI, pI, 4, A.arith_shift_right)
-    ts(cgI, cI, 4, A.arith_shift_right)
-    ts(cmI, cI, 15, A.bitwise_and)
-    PM = new("CF", 1); PG = new("CF", 1); CG = new("CF", 144); CMF = new("CF", 144); PX = new("CF", 1)
-    copy(PM, pmI); copy(PG, pgI); copy(CG, cgI); copy(CMF, cmI); copy(PX, pI)
-    BLK = new("CM", 144); C15 = new("CM", 144); MST = new("CM", 144); R8 = new("CM", 128)
+    copy(PM, pmI); copy(PG, pgI)
+    BLK = new("CM", 144); MST = new("CM", 144); R8 = new("CM", 128)
     ts(BLK, CG, PG, A.is_equal)
-    ts(C15, CMF, 15.0, A.is_equal)
-    tt(MST, BLK, C15, A.mult)
+    ts(MST, CMF, 15.0, A.is_equal)
+    tt(MST, MST, BLK, A.mult)
     ts(R8, part(CG, 0, 128), PX, A.is_equal)
     fill(R("MF", 0, P), 1.0)
-    fill(R("MF", P, P + 16), 0.0)
+    gfill(R("MF", P, P + 16), 0)
     ts(R("FSB", 0, 256, p=(0, 8)), R("FSI", 0, 256, p=(0, 8)), -1.0, A.mult, 1.0, A.add)
     r0 = R8[1][0][1]
     mm([(R("BA", 0, 256), R("CM", r0, r0 + 128, p=(0, 8)), R("FSB", 0, 256, p=(0, 8)))])
     copy(R("MF", 0, P, 16), R("BA", 0, 256))
     copy(R("FUV"), R("FUI"))
-    WC = new("CF", 1); W4 = new("CF", 1); SGN = new("CF", 1); SG16 = new("CF", 1); SGH = new("CF", 1); NSG = new("CF", 1)
+    WC = new("CF", 1); W4 = new("CF", 1); SGN = new("CF", 1); SG16 = new("CF", 1); SGH = new("CF", 1); NSG = new("CF", 1); SG12 = new("CF", 1)
     ts(WC, PM, -14.0, A.mult, 255.0, A.add)
-    ts(W4, WC, 0.25, A.mult)
+    ts(W4, PM, -3.5, A.mult, 63.75, A.add)
     ts(SGH, PM, 15.0, A.is_equal, -0.5, A.add)
-    ts(SGN, SGH, 2.0, A.mult)
-    ts(SG16, SGH, 32.0, A.mult)
-    ts(NSG, SGH, -2.0, A.mult)
+    for x, c in ((SGN, 2.0), (SG16, 32.0), (NSG, -2.0), (SG12, 2.0 ** -11)):
+        ts(x, SGH, c, A.mult)
 
-    def scaled(src, by, n=128):
-        m = new("CM", n)
+    def scaled(src, by, n=128, m=None):
+        m = m or new("CM", n)
         act(m, part(src, 0, n), AF.Identity, 0.0, by)
         return m
     B1 = part(BLK, 0, 128)
-    DK = new("CF", 128); CM1 = part(CMF, 0, 128)
-    ts(DK, CM1, PM, A.subtract)
 
-    def masked(o, c):
+    def masked(o, sign, base):
         m = new("CM", 128)
-        ts(m, DK, c, o)
-        tt(m, m, B1, A.mult)
+        put("g", lambda: g.affine_select(m[0], B1[0], [[sign, 128]], o, 0.0, base, -sign), B1[1], m[1], (170, 256, 0, 0, 0))
         return m
 
     def comb(a, b, by):
@@ -247,56 +256,46 @@ def rank_program(g, core, T, topo):
         ts(m, b, by, A.mult)
         tt(m, m, a, A.add)
         return m
-    TRS = masked(A.is_gt, 0.0); TRI = masked(A.is_ge, 0.0); TGE = masked(A.is_le, 0.0); IDN = masked(A.is_equal, 0.0)
-    TGT = masked(A.is_lt, 0.0); S0 = masked(A.is_equal, 1.0); S1 = masked(A.is_equal, -15.0)
+    IDN = masked(A.is_equal, 1, 0); TRS = masked(A.is_gt, 1, 0); TGE = masked(A.is_ge, -1, 0); S0 = masked(A.is_equal, 1, -1)
+    S1 = masked(A.is_equal, 1, 15); TRI = masked(A.is_ge, 1, 0); TGT = masked(A.is_gt, -1, 0)
     A0 = comb(TRS, S0, 63.0); A1 = comb(B1, S1, 63.0); A0C = comb(A0, IDN, -128.0)
-    TRX = comb(TRS, IDN, -4096.0); TRB = comb(TRS, IDN, 4096.0)
+    TRX = comb(TRS, IDN, -4096.0); TRB = comb(TRS, IDN, 8192.0)
     MSL = scaled(MST, -float(2 ** 36), 144); MS = scaled(MST, 0.0625, 144); MSW = scaled(MST, WC, 144); MSI = scaled(MST, PM, 144)
     BW4 = scaled(BLK, W4); BI = scaled(BLK, PM); BL = scaled(BLK, -0.0625); BN8 = scaled(BLK, -8192.0); BN4 = scaled(BLK, -4096.0)
     BP8 = scaled(BLK, 8192.0); BP17 = scaled(BLK, float(2 ** 17))
-    NTRS = scaled(TRS, -1.0); NTGE = scaled(TGE, -1.0); NTRI = scaled(TRI, -1.0); NTGT = scaled(TGT, -1.0)
     ID = {}
-    for c in (-1.0, float(RW), 94.0, 128.0, float(DUMP), float(2 ** 20), 512.0, -512.0, -4096.0, 4096.0, 8192.0, -8192.0, -1024.0, 0.5 - me / 4, 1.0 - me / 4):
-        if c not in ID:
-            ID[c] = scaled(IDN, c)
-    K1 = new("CR", 512); IQ = new("CR", 256); KT1 = new("CR", 32); KD = new("CR", 32); KS = new("CR", 16); ZR = new("CR", 264)
-    RS = new("CM", 136); PADC = new("CM", 136); RS2 = new("CM", 64)
-    fill(ZR, 0.0)
-    ts(KT1, ktI, PM, A.add, 1.0, A.add)
-    ts(KD, KT1, float(DUMP - 1), A.add)
+    for c in (-1.0, float(RW), 94.0, 128.0, float(DUMP), 1024.0, -1024.0, 4096.0, 8192.0, -8192.0, 0.5 - me / 4, 1.0 - me / 4):
+        ID[c] = scaled(IDN, c)
+    NTRS = scaled(TRS, -1.0); NTGE = scaled(TGE, -1.0); NTRI = scaled(TRI, -1.0); NTGT = scaled(TGT, -1.0)
+    STRS = scaled(TRS, SGN); STGE = scaled(TGE, SGN); STRI = scaled(TRI, SGN); STGT = scaled(TGT, SGN); SID = scaled(ID[-8192.0], SGN)
+    IDF = scaled(IDN, 1.0, 128, new("CF", 128))
+    K1 = new("CR", 512); IQ = new("CR", 256); KT1 = new("CR", 32); KD = new("CR", 16); KS = new("CR", 16); ZR = new("CR", 264)
+    KH = new("CR", 32); OC = new("CR", 144); QM = new("CF", 170); QO = new("CF", 170); KT = new("CF", 32)
+    RS = new("CM", 136); PADC = new("CM", 136); RS2 = new("CM", 32)
+    iota(KT, [[16, 32]], 1, 0)
+    iota(QM, [[0, 5], [1, 34]], 0, 0)
+    iota(QO, [[1, 5], [0, 34]], 0, 0)
+    ts(KT1, KT, PM, A.add)
+    ts(KD, part(KT1, 0, 16), float(DUMP - 1), A.add)
     ts(KS, part(KT1, 0, 16), float(TS + 16), A.add)
-    fill(RS, 1.0); fill(PADC, 0.0); fill(RS2, 1.0)
-    for o in range(N):
-        fill(part(RS, 34 * o + 1, 34 * o + 2), 0.0)
-        fill(part(PADC, 34 * o + 1, 34 * o + 2), 512.0 * o - 4096.0)
-    fill(part(RS2, 16, 17), 0.0)
-    fill(R("OHB"), 0.0); fill(R("CD"), 0.0); fill(R("CU"), -1.0); fill(R("NL"), 0.0); fill(R("LN"), 0.0); fill(R("INV"), 0.0)
-    fill(R("NS", 0, 16), 0.0); fill(R("SNT"), 0.0)
-    fill(R("UV", 0, 8), 1.0); fill(R("UV", P, P + 16), 1.0)
+    ts(KH, KT1, 0.5, A.add)
+    ts(RS, part(QM, 0, 136), 1.0, A.not_equal)
+    ts(PADC, part(QO, 0, 136), 512.0, A.mult, -8192.0, A.add)
+    ts(R("LR", 0, 136), part(QM, 0, 136), 1.0, A.is_equal)
+    tt(PADC, PADC, R("LR", 0, 136), A.mult)
+    ts(R("T0", 0, 144), part(QM, 0, 144), 2.0, A.is_lt, -9.0, A.mult)
+    tt(OC, part(QO, 0, 144), R("T0", 0, 144), A.add)
+    ts(RS2, part(CMF, 0, 32), 0.0, A.not_equal)
     copy(R("CU", 1, 2), SGN)
-    ts(R("LR", 0, 128), DK, 0.0, A.is_equal, -float(2 ** 40), A.mult)
-    ts(R("LR", 128, 256), DK, 1.0, A.is_equal, -2.0, A.mult)
-    ts(R("LR", 256, 384), DK, -15.0, A.is_equal, -2.0, A.mult)
-    tt(R("LR", 0, 128), R("LR", 0, 128), R("LR", 128, 256), A.add)
-    tt(R("LR", 0, 128), R("LR", 0, 128), R("LR", 256, 384), A.add)
+    DK = new("CF", 128)
+    ts(DK, part(CMF, 0, 128), PM, A.subtract)
+    ts(R("OO", 0, 128), DK, 0.0, A.is_equal, -float(2 ** 40), A.mult)
+    ts(R("OO", 128, 256), DK, 1.0, A.is_equal, -2.0, A.mult)
+    ts(R("OO", 256, 384), DK, -15.0, A.is_equal, -2.0, A.mult)
+    tt(R("OO", 0, 128), R("OO", 0, 128), R("OO", 128, 256), A.add)
+    tt(R("OO", 0, 128), R("OO", 0, 128), R("OO", 256, 384), A.add)
     for k in range(4):
-        act(R("RL", 128 * k, 128 * k + 128), R("LR", 0, 128), AF.Identity, 1.0)
-    OH = new("CF", 16)
-    ts(OH, part(CMF, 0, 16), PM, A.is_equal)
-
-    def row(i, k):
-        return R("SEL", 256 * i + 128 * k, 256 * i + 128 * k + 128)
-    for i in range(16):
-        ts(row(i, 0), B1, part(OH, i, i + 1), A.mult, 4096.0, A.mult)
-        ts(row(i, 1), B1, part(OH, i, i + 1), A.mult)
-    NSET = len(ops)
-    iota(K1, [[1, 512]], 1 - 4096, 0)
-    iota(IQ, [[1, 256]], 0, 0)
-    iota(R("J1"), [[1, 256]], 1, 0)
-    gfill(R("ONE"), 1)
-    for a in range(0, TS + 272, 464):
-        gfill(R("STO", a, a + 464), -1)
-    gfill(R("RPL"), 1)
+        act(R("RL", 128 * k, 128 * k + 128), R("OO", 0, 128), AF.Identity, 1.0)
 
     def sums(out, m, b, lo):
         return [(out, win(m, i), R(b, lo + i, lo + 16 * out[2], 16)) for i in range(16)]
@@ -304,6 +303,36 @@ def rank_program(g, core, T, topo):
     def relay(out, in_):
         scan(out, R("RL", 0, out[2]), in_, SGH, A.mult, A.min)
         return part(out, 15, out[2], 16)
+
+    ts(R("LA", 0, 144), part(QM, 0, 144), 1.0, A.max, -1.0, A.add)
+    ts(R("LA", 0, 144), R("LA", 0, 144), 1.0, A.max)
+    ts(R("REP", 0, 9), relay(R("LA", 256, 400), R("LA", 0, 144)), SGN, A.mult, -1.0, A.add)
+    OH = new("CF", 16)
+    ts(OH, part(CMF, 0, 16), PM, A.is_equal)
+
+    def row(i, k):
+        return R("SEL", 256 * i + 128 * k, 256 * i + 128 * k + 128)
+    for i in range(15, -1, -1):
+        scaled(BLK, part(OH, i, i + 1), 128, row(i, 1))
+    NSET = len(ops)
+    C4 = new("CM", 128)
+    gfill(C4, 4096)
+    for i in range(16):
+        put("g", lambda i=i: g.affine_select(row(i, 0)[0], C4[0], [[-16, 8], [0, 16]], A.is_equal, 0.0, -i, 1), C4[1], row(i, 0)[1], (170, 256, 0, 0, 0))
+    iota(K1, [[1, 512]], 1 - 4096, 0)
+    iota(IQ, [[1, 256]], 0, 0)
+    iota(R("J1"), [[1, 256]], 1, 0)
+    gfill(R("ONE"), 1)
+    gfill(ZR, 0)
+    gfill(R("CU", 0, 1), -1)
+    for b, a, c in (("CD", 0, 0), ("OHB", 0, 0), ("SNT", 0, 0), ("YK", 15, 0), ("LN", 0, 0), ("INV", 0, 1), ("UV", 0, 1)):
+        gfill(R(b, a, a + 1), c)
+    gfill(R("UV", ZC, P + 16), 1)
+    for a in range(0, TS + 272, 464):
+        gfill(R("STO", a, a + 464), -1)
+    gfill(R("RPL"), 1)
+    if RC:
+        gfill(R("CC"), CL)
 
     def vphase():
         copy(R("KU", 256, 512), I(L("KID"), R("FUV", 16, 32)))
@@ -317,6 +346,7 @@ def rank_program(g, core, T, topo):
             ops[-1]["up"] = 1000.0 if c < 2 else 0.0
             tt(R("DF", a, a + n), I(L("VEC"), R("KU", a // 16, (a + n) // 16)), R("VV", a, a + n), A.subtract)
             scan(R("D", a, a + n), R("MF", a, a + n), R("DF", a, a + n), R("D", a - 1, a) if a else 0.0, A.mult, A.add)
+        for a, n in BH:
             act(R("AB", a, a + n), R("D", a, a + n), AF.Abs)
         for a, n in AH:
             b = R("BA", a // 16, (a + n) // 16)
@@ -344,7 +374,7 @@ def rank_program(g, core, T, topo):
         ts(R("JT"), y, SGN, A.mult, -1.0, A.add)
         act(R("JB"), y, AF.Identity, 0.0, SG16)
         tt(R("XC"), R("BH", 0, 256), R("SC", 0, 256), A.add)
-        ts(R("INV", 1, 33), KT1, R("SC", 256, 257), A.is_ge)
+        act(R("INV", 1, 33), KH, AF.Sign, R("SC", 256, 257), -1.0)
         tt(R("OO"), I(R("XC"), R("JT")), K1, A.is_equal)
         t = R("BD", 0, 32)
         mm([(t, IDN, R("JB"))], sums(t, MSI, "OO", 0))
@@ -352,28 +382,43 @@ def rank_program(g, core, T, topo):
 
     def qphase():
         for a, n in QH:
-            act(R("QV", a, a + n), I(R("MRK"), R("KU", 256 + a // 16, 256 + (a + n) // 16)), AF.Copy)
-            tt(R("QV", a, a + n), I(R("MRK"), R("KU", a // 16, (a + n) // 16)), R("QV", a, a + n), A.max)
+            u, v = I(R("MRK"), R("KU", a // 16, (a + n) // 16)), I(R("MRK"), R("KU", 256 + a // 16, 256 + (a + n) // 16))
+            if a in RC:
+                k = RC.index(a)
+                qu, qv, b = R("QB", 1024 * k, 1024 * k + n), R("QB", 1024 * k + 512, 1024 * k + 512 + n), R("BE", 0, n)
+                act(qv, v, AF.Identity, -float(CL))
+                act(qu, u, AF.Identity, -float(CL))
+                mm([(b, ID[-1.0], qv)], [(b, IDN, qu)])
+                act(qu, b, AF.Relu)
+                x = R("BG", 0, n)
+                mm([(x, IDF, R("D", a, a + n))], [(x, IDN, R("CC", 0, n))], [(x, IDN, qv)], [(x, IDN, qu)])
+            else:
+                act(R("QV", a, a + n), v, AF.Copy)
+                tt(R("QV", a, a + n), u, R("QV", a, a + n), A.max)
         for c, (a, n) in enumerate(AH):
-            addto(R("D", a, a + n), R("QV", a, a + n), "ac%d" % c)
+            if a not in RC:
+                addto(R("D", a, a + n), R("QV", a, a + n), "ac%d" % c)
         for c in range(8):
             b = R(("BB", "BC")[c % 2])
             mm([(b, B1, R("AB", 512 * c, 512 * c + 512))])
             act(R("NS", 512 * c + 1, 512 * c + 513), b, AF.Sign)
+        b = R("BA", 256, 512)
+        mm([(b, row(15, 1), R("CU", 1, 257))])
         for a, n in EH:
-            tt(R("NS", a, a + n, 16), R("NS", a, a + n, 16), R("MF", a, a + n, 16), A.mult)
-            scan(R("EM", a, a + n), R("NS", a, a + n), R("D", a, a + n), R("EM", a - 1, a) if a else 0.0, A.mult, A.add)
+            act(R("NS", a, a + n, 16), part(b, a // 16, (a + n) // 16), AF.Relu, 0.0, -1.0)
+            x = R("BG", 0, n) if a in RC else R("D", a, a + n)
+            scan(R("EM", a, a + n), R("NS", a, a + n), x, R("EM", a - 1, a) if a else 0.0, A.mult, A.add)
 
     def pairs():
         for i in range(16):
             b = R(("BB", "BC")[i % 2], 0, 256)
-            mm([(b, row(i, 0), R("KF", 0, 256)), (b, row(i, 1), R("KF", 256, 512))])
+            mm([(b, row(i, 1), R("KF", 0, 256)), (b, row(i, 0), R("KF", 256, 512))])
             act(R("UV", 1 + i, 1 + P, 16), b, AF.Identity, float(4097 * HALF + 1))
 
-    def fused(src, buf, base, step, lsem, rsem, ready=()):
+    def fused(src, buf, base, lsem, rsem, ready=()):
         m = masks(me)
         tr, rd, tot = [], list(ready), 0
-        dst = R(buf, base + step * me, base + step * me + CAP)
+        dst = R(buf, base + CAP * me, base + CAP * me + CAP)
         for d in range(N):
             if d != me:
                 rid, pid = topo.addr(cores[d])[:2]
@@ -381,31 +426,29 @@ def rank_program(g, core, T, topo):
                 rd += x[1]
                 tot += len(m[d])
                 tr.append(RemoteDMATransfer(dst_ids=[DstId(rid=rid, pnc=pid)], dma_engine_mask=sum(1 << e for e in m[d]), remote_sem=T.sem[rsem], src=x[0], dst=dst[0]))
-        put("g", lambda: g.remote_dma_fused(tr, local_sem=T.sem[lsem]), rd, [(lsem, 0, 1)], 500.0, 1000.0, lsem, -tot)
+        put("g", lambda: g.remote_dma_fused(tr, local_sem=T.sem[lsem]), rd, [(lsem, 0, 1)], 400.0, 1400.0, lsem, -tot)
         act(dst, src(me), AF.Copy)
         tot = sum(len(masks(s)[me]) for s in range(N) if s != me)
-        put("n", None, [(lsem, 0, 1)], [(buf, base + step * s, base + step * s + CAP) for s in range(N) if s != me], 1.0, NET - 1500.0, rsem, tot)
+        put("n", None, [(lsem, 0, 1)], [(buf, base + CAP * s, base + CAP * s + CAP) for s in range(N) if s != me], 1.0, NET - 1800.0, rsem, tot)
 
     def keys(r):
         ts(R("ZI"), I(R("EM"), R("T1")), float(2 ** 30), A.min, -float(2 ** 30), A.max)
         ts(R("Z8"), R("ZI"), 255, A.bitwise_and)
         copy(R("ZB"), R("Z8"))
         h = R("BD", 0, 32)
-        mm([(h, ID[float(2 ** 20)], R("INV", 1, 33))], sums(h, MSW, "ZB", 0))
+        mm(sums(h, MSW, "ZB", 0))
         copy(R("HI"), h)
-        ts(R("OW"), R("HI"), 3 + 2 ** 20, A.bitwise_and)
-        for o in range(N):
-            ts(R("OHB", 34 * o + 3, 34 * o + 35), R("OW"), float(o), A.is_equal if o < N - 1 else A.is_ge)
+        ts(R("OW"), R("HI"), 3, A.bitwise_and)
+        tt(R("OHB", 1, 145), I(R("OW"), R("REP", 0, 9)), OC, A.is_equal)
         k = R("BF", 0, 136)
-        k3 = R("BF", 104, 136)
-        mm([(k, IDN, PADC), (k3, ID[512.0], R("INV", 1, 33)), (k3, ID[-512.0], R("INV", 0, 32))],
-           [(k, TRB, R("OHB", 1, 137)), (k, TGE, R("OHB", 0, 136)), (k, ID[-4096.0], R("OHB", 0, 136))])
+        mm([(k, IDN, PADC)] + [(R("BF", 34 * o + 2, 34 * o + 34), ID[c], R("INV", a, a + 32)) for o in range(N) for c, a in ((-1024.0, 1), (1024.0, 0))],
+           [(k, TRB, R("OHB", 1, 137)), (k, TGE, R("OHB", 0, 136)), (k, ID[-8192.0], R("OHB", 0, 136))])
         scan(R("RK"), RS, k, 0.0, A.mult, A.add)
         tt(R("R2", 0, 66), R("RK", 2, 68), R("RK", 70, 136), A.max)
         tt(R("RQ"), R("R2", 0, 32), R("R2", 34, 66), A.max)
         copy(R("OFF"), R("RQ"))
         copy(I(R("SND"), R("OFF")), R("ZB"))
-        fused(lambda d: R("SND", 512 * d, 512 * d + CAP), "ARR", 256 * r, CAP, "lk%d" % r, "ka%d" % r,
+        fused(lambda d: R("SND", 512 * d, 512 * d + CAP), "ARR", 256 * r, "lk%d" % r, "ka%d" % r,
               R("RPL", RW * r, RW * r + RW)[1])
         gfill(R("NXT", 0, 256), 0)
         act(R("LA"), I(R("EM"), R("T1")), AF.Identity, RND, 1.0 / CL)
@@ -414,7 +457,7 @@ def rank_program(g, core, T, topo):
         mm([(t, B1, R("JK")), (t, BI, R("OO")), (t, BL, R("LR"))])
         act(R("T0"), t, AF.Identity, -14.0)
         gfill(R("JW2", 0, 256), 0)
-        ts(R("O3"), R("OW"), 3.0, A.min)
+        copy(R("O3"), R("OW"))
         act(R("TH"), R("O3"), AF.Identity, 64.0, 512.0)
         act(R("O4"), R("O3"), AF.Identity, -256.0, -448.0)
         tt(R("SNT", 1, 33), R("RQ"), R("TH"), A.is_lt)
@@ -440,18 +483,18 @@ def rank_program(g, core, T, topo):
         t = R("BF", 0, 16)
         mm(sums(t, MST, "PR", 0))
         ts(R("OFS"), t, 256.0, A.add)
-        act(R("LR2"), I(R("LR"), R("KS2")), AF.Copy)
+        act(R("SG"), I(R("LR"), R("KS2")), AF.Relu, -1.0)
+        act(R("LR2"), R("SG"), AF.Identity, 1.0)
         act(R("T2"), I(R("T0"), R("KS2")), AF.Copy)
         t = R("BG", 0, 16)
         mm(sums(t, MS, "LR2", 0))
         act(R("LN", 1, 17), t, AF.Copy)
-        act(R("SL"), t, AF.Identity, 0.0, SGN)
 
     def owner(r):
         b = 256 * r
         arr = R("ARR", b, b + 256)
         pa, pb = R("BH", 0, 256), R("BH", 256, 512)
-        mm([(pa, ID[-1024.0], R("ONE")), (pa, ID[0.5 - me / 4], R("ONE")), (pb, ID[1.0 - me / 4], R("ONE"))], [(pa, BW4, arr), (pb, BW4, arr)])
+        mm([(pa, ID[-1024.0], R("ONE")), (pa, ID[0.5 - me / 4], R("ONE")), (pb, ID[1.0 - me / 4], R("ONE"))], [(pa, BW4, arr)], [(pb, BW4, arr)])
         act(R("NEG"), arr, AF.Relu, 0.0, -1.0)
         ts(R("RR"), pa, M11, A.add, M11, A.subtract)
         tt(R("P1"), pb, R("RR"), A.subtract)
@@ -467,15 +510,27 @@ def rank_program(g, core, T, topo):
         tt(R("ED"), R("YM"), R("BE", 0, 256), A.is_equal)
         eo = [[(n, ID[4096.0], R("ONE")), (n, BP8, R("NEG")), (n, BN4, R("NQ"))]]
         lo = 0
+        es = []
+        act(R("YB", 0, 16), R("YM", 15, 256, 16), AF.Identity, 0.5, NSG)
+        act(R("YB", 16, 32), R("YM", 15, 256, 16), AF.Identity, 0.5, SGN)
         for m in range(15):
             k = 240 - 16 * m
-            ts(R("EO", lo, lo + k), R("R1", 16 * m + 16, 256), SGN, A.mult, R("YM", 16 * m + 15, 16 * m + 16), A.is_equal)
-            eo.append([(R("BD", 16 * m + 16, 256), BP17, R("EO", lo, lo + k))])
-            lo += k
-        eo.insert(8, [(n, BP17, R("ED"))])
+            o = R("BD", 16 * m + 16, 256)
+            if m < EV:
+                ts(R("EO", lo, lo + k), R("R1", 16 * m + 16, 256), SGN, A.mult, R("YM", 16 * m + 15, 16 * m + 16), A.is_equal)
+                eo.append([(o, BP17, R("EO", lo, lo + k))])
+                lo += k
+            else:
+                act(R("EO", lo, lo + k), R("P1", 16 * m + 16, 256), AF.Sign, R("YB", m, m + 1))
+                act(R("EO", lo + k, lo + 2 * k), R("P1", 16 * m + 16, 256), AF.Sign, R("YB", 16 + m, 17 + m), -1.0)
+                es.append([(o, BP17, R("EO", lo, lo + k)), (o, BP17, R("EO", lo + k, lo + 2 * k))])
+                lo += 2 * k
+        eo.insert(6, [(n, BP17, R("ED"))])
+        for x, e in enumerate(es):
+            eo.insert(5 + 2 * x, e)
         mm(*eo)
         ts(R("NEW", b, b + 256), n, 0.0, A.is_le, 1.0, A.add)
-        fused(lambda d: R("NEW", b + CAP * d, b + CAP * d + CAP), "RPL", RW * r, CAP, "lr%d" % r, "ra%d" % r)
+        fused(lambda d: R("NEW", b + CAP * d, b + CAP * d + CAP), "RPL", RW * r, "lr%d" % r, "ra%d" % r)
         act(R("PF"), yp, AF.Abs)
         ts(R("S1"), relay(R("YN"), R("NEW", b, b + 256)), NSG, A.mult, 2.0, A.add)
         tt(R("S2"), R("S1"), KS, A.mult)
@@ -483,24 +538,22 @@ def rank_program(g, core, T, topo):
         ts(R("SU"), R("S3"), -1.0, A.add)
         copy(I(R("STO"), R("SU")), arr)
         if r == RO - 1:
-            dma("y", "st0", H(T.yt[:]), R("STO", 0, TS), DMA0 + 2 * TS * DMAB)
+            dma("y", "st0", H(T.yt[:]), R("STO", 0, TS), 2 * TS)
 
     def nextfront(r):
         rp = R("RPL", RW * r, RW * r + RW)
-        act(R("NK", 0, 96), I(rp, R("OFS", 0, 6)), AF.Copy)
-        copy(R("NK", 96, 256), I(rp, R("OFS", 6, 16)))
-        tt(R("NL", 1, 17), relay(R("YK"), R("NK")), R("SL"), A.mult)
+        tt(R("NK"), I(rp, R("OFS")), R("LR2"), A.mult)
+        n1, n0 = relay(R("YK", 16, 272), R("NK")), R("YK", 15, 256, 16)
         st, en, du = R("BF", 0, 16), R("BF", 16, 32), R("BF", 32, 48)
-        l1, l0, n1, n0 = R("LN", 1, 17), R("LN", 0, 16), R("NL", 1, 17), R("NL", 0, 16)
+        l1, l0 = R("LN", 1, 17), R("LN", 0, 16)
         mm([(st, NTRS, l1), (st, NTGE, l0), (en, NTRI, l1), (en, NTGT, l0), (du, ID[8192.0], l1)],
-           [(st, TRS, n1), (st, TGE, n0), (en, TRI, n1), (en, TGT, n0), (du, ID[-8192.0], n1)])
-        scan(R("SE"), part(RS2, 0, 32), R("BF", 0, 32), 0.0, A.mult, A.add)
-        tt(R("DU"), du, part(KD, 0, 16), A.add)
+           [(st, STRS, n1), (st, STGE, n0), (en, STRI, n1), (en, STGT, n0), (du, SID, n1)])
+        scan(R("SE"), RS2, R("BF", 0, 32), 0.0, A.mult, A.add)
+        tt(R("DU"), du, KD, A.add)
         tt(R("X1"), R("SE", 0, 16), R("DU"), A.max)
         copy(R("OF2"), R("X1"))
-        act(R("GF"), R("SE", 16, 32), AF.Relu, 64.0 * 257, -64.0)
-        act(R("NR"), du, AF.Identity, 0.0, -1.0 / 8192)
-        tt(R("KB"), R("NR"), R("GF"), A.min)
+        ts(R("GF"), R("SE", 16, 32), 256.0, A.is_le, -1.0 / 8192, A.mult)
+        tt(R("KB"), du, R("GF"), A.mult)
         mm([(R("BG", 0, 16), B1, R("KB"))])
         act(R("X3"), R("BG", 0, 16), AF.Identity, 512.0, -16384.0, R("TOB", 0, 1))
         act(R("F0"), IQ, AF.Relu, R("TOB", 0, 1), 16384.0)
@@ -514,20 +567,21 @@ def rank_program(g, core, T, topo):
         act(R("MF", 0, P, 16), R("BH", 0, 256), AF.Relu, -2.0, 2.0)
         if r < RO - 1:
             copy(R("GU"), I(R("UV"), R("CT")))
-            ts(R("WI"), relay(R("YU"), R("GU")), SGN, A.mult, -1.0, A.add)
-            ts(R("UI", 16, 32), R("WI"), 4095, A.bitwise_and)
-            ts(R("UI", 0, 16), R("WI"), 12, A.arith_shift_right)
-            copy(R("FUV", 16, 32), R("UI", 16, 32))
-            copy(R("FUV", 0, 16), R("UI", 0, 16))
+            y = relay(R("YU"), R("GU"))
+            ts(R("FUV", 16, 32), y, SG12, A.mult, -0.5, A.add)
+            ts(R("WI"), y, SGN, A.mult, -1.0, A.add)
+            ts(R("UI"), R("WI"), 4095, A.bitwise_and)
+            copy(R("FUV", 0, 16), R("UI"))
         else:
             ts(R("ZI", 0, 256), I(R("UV"), R("CT")), -1.0, A.add)
-            ts(R("Z8", 0, 256), R("ZI", 0, 256), 12, A.arith_shift_right)
-            ts(R("Z8", 256, 512), R("ZI", 0, 256), 4095, A.bitwise_and)
+            ts(R("Z8", 0, 256), R("ZI", 0, 256), 4095, A.bitwise_and)
             copy(R("OUTF", 0, 256), R("Z8", 0, 256))
-            copy(R("OUTF", 256, 512), R("Z8", 256, 512))
+            act(R("GU"), I(R("UV"), R("CT")), AF.Identity, -0.5, 2.0 ** -12)
+            act(R("YU"), R("GU"), AF.Identity, RND)
+            act(R("OUTF", 256, 512), R("YU"), AF.Identity, -RND)
             act(R("OUTF", 512, 768), R("MF", 0, P, 16), AF.Identity, 1.0, -1.0)
             for k, (q, y) in enumerate((("y", T.yu), ("s", T.yv), ("y", T.ys))):
-                dma(q, "st%d" % (k + 1), H(y[:]), R("OUTF", 256 * k, 256 * k + 256, p=(0, 128, 16)), DMA0)
+                dma(q, "st%d" % (k + 1), H(y[:]), R("OUTF", 256 * k, 256 * k + 256, p=(0, 128, 16)), 64)
 
     for r in range(RO):
         vphase()
@@ -539,78 +593,162 @@ def rank_program(g, core, T, topo):
         nextfront(r)
 
     n = len(ops)
-    recs = {}
-    pred = []
-    for x, o in enumerate(ops):
-        ps = set()
-        for regs, wr in ((o["r"], False), (o["w"], True)):
-            for (b, lo, hi) in regs:
-                for rec in recs.get(b, []):
-                    if rec[0] < hi and lo < rec[1] and (wr or rec[2]):
-                        ps.add(rec[3])
-        if x < NLOAD:
-            ps.update(y for y in range(x) if ops[y]["q"] == o["q"])
-        pred.append(ps)
-        for (b, lo, hi) in o["w"]:
-            recs[b] = [r for r in recs.get(b, []) if not (lo <= r[0] and r[1] <= hi)] + [(lo, hi, True, x)]
-        for (b, lo, hi) in o["r"]:
-            recs.setdefault(b, []).append((lo, hi, False, x))
 
-    def gap(y, x):
-        if x < NLOAD:
-            return ops[y]["hold"]
-        return ops[y]["hold"] + ops[y]["lat"] + (0.0 if ops[x]["ch"] and ops[y]["q"] == "t" else WAKE)
-    rank = [0.0] * n
-    for x in range(n - 1, -1, -1):
-        rank[x] = max(rank[x], ops[x]["hold"] + ops[x]["lat"]) + (1e9 if x < NLOAD else ops[x].get("up", 0.0))
-        for y in pred[x]:
-            rank[y] = max(rank[y], rank[x] + gap(y, x))
-    succ = [[] for _ in range(n)]
-    for x in range(n):
-        for y in pred[x]:
-            succ[y].append(x)
+    def depends(wide):
+        recs = {}
+        pred = []
+        for x, o in enumerate(ops):
+            ps = set()
+            rw = [o["r"], o["w"]]
+            for k in range(2):
+                rw[k] = [(b, lo // wide[b] * wide[b], -(-hi // wide[b]) * wide[b]) if b in wide else (b, lo, hi) for b, lo, hi in rw[k]]
+                for (b, lo, hi) in rw[k]:
+                    for rec in recs.get(b, []):
+                        if rec[0] < hi and lo < rec[1] and (k or rec[2] or (b in BANKS and ops[rec[3]]["q"] != o["q"])):
+                            ps.add(rec[3])
+            pred.append(ps)
+            for (b, lo, hi) in rw[1]:
+                recs[b] = [r for r in recs.get(b, []) if b in wide or not (lo <= r[0] and r[1] <= hi)] + [(lo, hi, True, x)]
+            for (b, lo, hi) in rw[0]:
+                recs.setdefault(b, []).append((lo, hi, False, x))
+        return pred
 
-    def place(order, back):
-        at = [0.0] * n
-        busy = {}
-        for x in order:
-            h = ops[x]["hold"]
-            if back:
-                t = max([at[y] + ops[y]["hold"] + gap(x, y) - h for y in succ[x]] + [ops[x]["lat"]])
-            else:
-                t = max([at[y] + gap(y, x) for y in pred[x]] + [0.0])
-            lst = busy.setdefault(ops[x]["q"], [])
-            a, b = 0, len(lst)
-            while a < b:
-                m = (a + b) // 2
-                if lst[m][1] > t:
-                    b = m
-                else:
-                    a = m + 1
+    def chained(y, x):
+        return ops[x]["ch"] and ops[y]["q"] == "t" and ops[y]["w"] == ops[x]["w"]
+
+    def arrange():
+        pred = [a | b for a, b in zip(depends({}), depends({"ARR": 256, "NEW": 256, "RPL": RW, "SND": 4096}))]
+        for x in range(n):
+            pred[x] = set(y for y in pred[x] if ops[x]["q"] != "g" or ops[y]["q"] != "g" or not ops[x]["w"] or not ops[y]["w"]
+                          or ops[x]["w"][0][0] != "SND" or ops[y]["w"][0][0] != "SND")
+        succ = [set() for _ in range(n)]
+        for x in range(n):
+            for y in pred[x]:
+                succ[y].add(x)
+        hs = [[o["hold"][m] for o in ops] for m in range(len(PACE))]
+        lat = [o["lat"] for o in ops]
+        load = [o["load"] for o in ops]
+        arcs = [[(y, 0.0 if chained(y, x) else WAKE) for y in pred[x]] for x in range(n)]
+        qn = ["vstgyn".index(o["q"]) for o in ops]
+        rank = [0.0] * n
+        for x in range(n - 1, -1, -1):
+            rank[x] += hs[0][x] + lat[x] + load[x] + ops[x].get("up", 0.0)
+            for y, d in arcs[x]:
+                rank[y] = max(rank[y], rank[x] + d)
+        at, end, busy, dfree = [0.0] * n, [0.0] * n, [[] for _ in range(6)], 0.0
+        for x in sorted(range(n), key=lambda x: (0, x) if x < NLOAD else (1 if x < NSET else 2, -rank[x], x)):
+            h = hs[0][x]
+            t = max([end[y] + d for y, d in arcs[x]] + [0.0])
+            lst = busy[qn[x]]
+            a = 0
+            while a < len(lst) and lst[a][1] <= t:
+                a += 1
             while a < len(lst) and lst[a][0] < t + h:
                 t = lst[a][1]
                 a += 1
             lst.insert(a, (t, t + h))
             at[x] = t
-        return at
+            end[x] = t + h + lat[x] + load[x]
+            if load[x] and x < NSET:
+                dfree = max(t + lat[x] / 2, dfree) + load[x]
+                end[x] = dfree + lat[x] / 2
+        seq = sorted(range(n), key=lambda x: (at[x], x))
 
-    def first(x):
-        return 0 if x < NLOAD else 1 if x < NSET else 2
-    order = sorted(range(n), key=lambda x: (first(x), -rank[x], x))
-    start, span = None, None
-    for _ in range(PASSES):
-        at = place(order, False)
-        e = max(at[x] + ops[x]["hold"] + ops[x]["lat"] for x in range(n))
-        if span is None or e < span:
-            start, span = at, e
-        bk = place(sorted(range(n), key=lambda x: (-at[x] - ops[x]["hold"], -x)), True)
-        order = sorted(range(n), key=lambda x: (first(x), -bk[x] - ops[x]["hold"], x))
+        def run(m, st, lo):
+            h = hs[m]
+            end, fre, dma_ = st
+            fr = [0.0] * 6
+            df = dma_[seq[lo - 1]] if lo else 0.0
+            seen = 0
+            k = lo - 1
+            while k >= 0 and seen & 15 != 15:
+                x = seq[k]
+                if not seen >> qn[x] & 1:
+                    seen |= 1 << qn[x]
+                    fr[qn[x]] = fre[x]
+                k -= 1
+            for k in range(lo, n):
+                x = seq[k]
+                t = fr[qn[x]]
+                for y, d in arcs[x]:
+                    u = end[y] + d
+                    if u > t:
+                        t = u
+                fre[x] = fr[qn[x]] = t + h[x]
+                if load[x]:
+                    df = max(t + lat[x] / 2, df) + load[x]
+                    end[x] = df + lat[x] / 2
+                else:
+                    end[x] = t + h[x] + lat[x]
+                dma_[x] = df
+            return max(end[x] for x in seq[-60:])
+        cur = [[[0.0] * n for _ in range(3)] for _ in PACE]
+        val = sum(w * run(m, cur[m], 0) for m, w in enumerate(WEIGHT))
+        least, keep = val, list(seq)
 
+        def tight(m):
+            end, fre = cur[m][0], cur[m][1]
+            before, last = [None] * n, [None] * 6
+            for x in seq:
+                before[x], last[qn[x]] = last[qn[x]], x
+            x = max(seq[-60:], key=lambda x: end[x])
+            res = []
+            while x is not None and x >= NLOAD:
+                t = fre[x] - hs[m][x]
+                y = next((y for y, d in arcs[x] if end[y] + d >= t - 0.01), None)
+                if y is None:
+                    y = before[x]
+                    if y is not None and y >= NLOAD:
+                        res += [(x, -1), (y, 1)]
+                x = y
+            return res
+        z = SEED
+        hot = []
+        for it in range(TRIES):
+            if it % 40 == 0:
+                hot = tight(it // 40 % len(PACE))
+            z = (z * 1103515245 + 12345) % 2147483648
+            if z >> 10 & 3 and hot:
+                x, step = hot[(z >> 12) % len(hot)]
+                a = seq.index(x)
+            else:
+                a = NLOAD + (z >> 12) % (n - NLOAD)
+                step = 1 if z >> 9 & 1 else -1
+            z = (z * 1103515245 + 12345) % 2147483648
+            far = 1 + (z >> 8) % 4
+            x = seq[a]
+            near = succ[x] if step > 0 else pred[x]
+            b = a
+            while far and NLOAD <= b + step < n and seq[b + step] not in near:
+                b += step
+                if qn[seq[b]] == qn[x]:
+                    far -= 1
+            while b != a and qn[seq[b]] != qn[x]:
+                b -= step
+            if b == a:
+                continue
+            seq.insert(b, seq.pop(a))
+            lo = min(a, b)
+            new_ = [[list(y) for y in c] for c in cur]
+            v = sum(w * run(m, new_[m], lo) for m, w in enumerate(WEIGHT))
+            z = (z * 1103515245 + 12345) % 2147483648
+            if v <= val - HEAT * (1 - it / TRIES) * math.log((z + 1) / 2147483648):
+                val, cur = v, new_
+                if v < least:
+                    least, keep = v, list(seq)
+            else:
+                seq.insert(a, seq.pop(b))
+        return keep
+
+    if n not in ORDER:
+        ORDER[n] = arrange()
+
+    pred = depends({})
     count = {}
     known = {q: {} for q in queues}
     waited = {}
     token = {}
-    for x in sorted(range(n), key=lambda x: (start[x], x)):
+    for x in ORDER[n]:
         o = ops[x]
         q = o["q"]
         s = o["sem"]
@@ -620,7 +758,7 @@ def rank_program(g, core, T, topo):
             continue
         best = {}
         for y in pred[x]:
-            if x < NLOAD or (o["ch"] and ops[y]["q"] == "t" and ops[y]["w"] == o["w"]):
+            if chained(y, x):
                 continue
             a, v, clk = token[y]
             if known[q].get(a, 0) < v and best.get(a, (0, None))[0] < v:

@@ -10,13 +10,13 @@ RND = 1.5 * 2 ** 23
 M11 = 1.5 * 2 ** 34
 CL = 393216
 HALF = W // 2
-CH = [(0, 256), (256, 256)] + [(512 * c, 512) for c in range(1, 8)]
-QH = [(512 * c, 512) for c in range(8)]
+CH = QH = [(512 * c, 512) for c in range(8)]
 AH = [(0, 1024), (1024, 1024), (2048, 1024), (3072, 512), (3584, 512)]
 EH = AH
 BH = AH
 RC = [3584]
-EV = 11
+RD = [3072]
+EV = 13
 RW = 272
 DUMP = 4128
 ZC = P + 1
@@ -27,31 +27,31 @@ def shapes(kind, dtype, text):
 
 
 SCRATCH = {}
-SCRATCH.update(shapes("sbuf", "int32", "KID:3456 FUI:32 FSI:256 ZI:512 Z8:512 HI:32 OW:32 WI:16 UI:16 CI:64"))
+SCRATCH.update(shapes("sbuf", "int32", "KID:3456 FUI:32 FSI:256 ZI:512 Z8:512 HI:32 OW:32 CI:64"))
 SCRATCH.update(shapes("sbuf", "uint16", "FUV:32 KU:512 OPU:16 JT:32 T1:32 OFF:32 PU:16 R1:256 SU:16 OF2:16 CT:16 OP2:2 REP:10 JT2:16 KS2:16 OFS:16"))
-SCRATCH.update(shapes("sbuf", "float16", "KF:512"))
-SCRATCH.update(shapes("sbuf", "bfloat16", "VEC:3456 FSB:256 LASTF:256 EQ:256 MF:4112 VV:4096 CU:264 NS:4112 AP:256 CD:264 SEL:4096 "
-                      "JW:4384 JK:512 YJ:512 JB:32 OO:512 LR:512 ZB:512 OHB:160 INV:40 STO:2320 NQ:256 NEG:256 ED:256 EO:2240 YN:256 "
+SCRATCH.update(shapes("sbuf", "float16", "KF:512 TGB:128"))
+SCRATCH.update(shapes("sbuf", "bfloat16", "VEC:3456 FSB:256 LASTF:256 EQ:256 MF:4112 VV:4112 CU:264 NS:4112 AP:256 CD:264 SEL:4096 "
+                      "JW:4384 JK:512 YJ:512 JB:32 OO:512 LR:512 ZB:512 OHB:160 INV:40 STO:2320 NQ:256 NEG:256 ED:256 YN:256 "
                       "NK:256 YK:272 LN:24 KB:16 SNT:40 JW2:320 JK2:256 YJ2:256 JB2:16 OO2:256 SG:256 PR:256 LR2:256 "
-                      "CM:7168 RL:512 SND:4096 ARR:768 NEW:768 RPL:816 ONE:256 J1:256 FF:256 FA:256 QB:%d CC:512" % max(16, 1024 * len(RC))))
-SCRATCH.update(shapes("sbuf", "float32", "MRK:3456 QV:4096 D:4640 UV:4112 SC:264 XX:256 YX:256 XC:256 LA:512 T0:512 "
-                      "RK:136 R2:72 RR:256 P1:256 T2:256 YP:256 PMR:256 YM:256 PP:256 YQ:256 GU:256 YU:256 F0:256 OUTF:768 "
+                      "CM:7168 RL:512 SND:4096 ARR:768 NEW:768 RPL:816 ONE:256 J1:256 FF:256 FA:256 QB:2048 CC:512"))
+SCRATCH.update(shapes("sbuf", "float32", "MRK:3456 KDF:3456 QV:4112 D:4640 UV:4112 SC:264 XX:256 YX:256 XC:256 LA:512 T0:512 "
+                      "RK:136 R2:72 RR:256 P1:256 T2:256 YP:256 PMR:256 YM:256 PP:256 YQ:256 GU:256 YU:256 F0:256 "
                       "CF:1152 CR:1536 SM:576"))
 VIEW = {}
 for _w in ("RQ:32 S1:16 S2:16 S3:16 PF:16 SE:32 DU:16 X1:16 NR:16 GF:16 X3:16 O3:32 TH:32 O4:32 SLT:32 SC2:40 X2:32 Y2:32 XC2:32 "
            "TOB:8 YB:32").split():
     _n, _k = _w.split(":")
     VIEW[_n] = ("SM", sum(x[2] for x in VIEW.values()), int(_k))
-SAME = {"DF": "VV", "AB": "VV", "EM": "QV", "NXT": "D"}
+SAME = {"DF": "VV", "AB": "VV", "EM": "QV", "NXT": "D", "EO": "NS"}
 BANKS = ("BA", "BB", "BC", "BD", "BE", "BF", "BG", "BH")
 SCRATCH.update({b: ("psum", [128, 512], "float32") for b in BANKS})
 SEMAPHORES = ["qv", "qs", "qt", "qg"] + ["ld%d" % k for k in range(9)] + ["st%d" % k for k in range(4)] + ["ac%d" % k for k in range(len(AH))] + \
              ["%s%d" % (s, r) for s in ("ka", "ra", "lk", "lr") for r in range(RO)]
 SIZE = {"int32": 4, "float32": 4, "uint16": 2, "float16": 2, "bfloat16": 2}
-WAKE, NET, DMA0, DMAB = 120.0, 2150.0, 2000.0, 0.5
+WAKE, NET, DMA0, DMAB, DMAL = 120.0, 2150.0, 2000.0, 0.55, 0.48
 PACE = ((0.83, 0.6, 1.56, 3.0, 50.0), (1.2, 0.95, 2.0, 5.5, 30.0), (0.83, 0.55, 1.15, 2.0, 40.0))
 WEIGHT = (1.0, 0.5, 1.0)
-TRIES, HEAT, SEED = 45000, 40.0, 12345
+TRIES, HEAT, SEED = 55000, 30.0, 17
 ORDER = {}
 
 
@@ -96,6 +96,10 @@ def rank_program(g, core, T, topo):
                     "inc": inc, "ch": chained, "load": load})
 
     def R(name, lo=None, hi=None, step=None, p=None):
+        if name in ("DF", "AB"):
+            lo, hi = lo + 16, hi + 16
+        if name == "OUTF":
+            name, lo, hi = ("XX", "YX", "XC")[lo // 256], 0, 256
         name = SAME.get(name, name)
         if name in VIEW:
             name, at, n = VIEW[name]
@@ -177,7 +181,7 @@ def rank_program(g, core, T, topo):
     queues = {"v": g.vector, "s": g.scalar, "t": g.tensor, "g": g, "y": g.sync}
 
     def dma(q, sem, out, in_, load):
-        put(q, lambda: queues[q].dma_start(out=out[0], in_=in_[0]), in_[1], out[1], 60.0, DMA0 - 500.0, sem, 16, load=load * DMAB + 1.0)
+        put(q, lambda: queues[q].dma_start(out=out[0], in_=in_[0]), in_[1], out[1], 60.0, DMA0 - 500.0, sem, 16, load=load * DMAL + 1.0)
 
     def addto(out, in_, sem, after=()):
         put("g", lambda: g.dma_start(out=out[0], in_=in_[0], accum_op=A.add), in_[1] + list(after), out[1], 600.0, DMA0, sem, 16, load=4 * out[2] * DMAB)
@@ -212,7 +216,7 @@ def rank_program(g, core, T, topo):
     iota(CMF, [[0, 9], [1, 16]], 0, 0)
     iota(PX, [[0, 1]], 0, 1)
     NLOAD = len(ops)
-    fill(R("MRK", 0, HALF), float(CL))
+    gfill(R("MRK", 0, HALF), CL)
     gfill(R("MRK", HALF, W), CL)
     for k in range(2):
         addto(R("MRK", HALF * k, HALF * k + HALF), H(T.mark[:, HALF * k:HALF * k + HALF]), "ld%d" % (7 + k), L("KID")[1])
@@ -251,41 +255,46 @@ def rank_program(g, core, T, topo):
         put("g", lambda: g.affine_select(m[0], B1[0], [[sign, 128]], o, 0.0, base, -sign), B1[1], m[1], (170, 256, 0, 0, 0))
         return m
 
-    def comb(a, b, by):
-        m = new("CM", 128)
-        ts(m, b, by, A.mult)
-        tt(m, m, a, A.add)
-        return m
-    IDN = masked(A.is_equal, 1, 0); TRS = masked(A.is_gt, 1, 0); TGE = masked(A.is_ge, -1, 0); S0 = masked(A.is_equal, 1, -1)
-    S1 = masked(A.is_equal, 1, 15); TRI = masked(A.is_ge, 1, 0); TGT = masked(A.is_gt, -1, 0)
-    A0 = comb(TRS, S0, 63.0); A1 = comb(B1, S1, 63.0); A0C = comb(A0, IDN, -128.0)
-    TRX = comb(TRS, IDN, -4096.0); TRB = comb(TRS, IDN, 8192.0)
+    def select(out, in_, pat, o, c, base, cm, after=()):
+        put("g", lambda: g.affine_select(out[0], in_[0], pat, o, c, base, cm), in_[1] + list(after), out[1], (170, 2 * out[2], 0, 0, 0))
+        return out
+
+    def line(a, c, base):
+        return select(new("CM", 128), a, [[1, 128]], A.not_equal, c, base, -1)
+    IDN = masked(A.is_equal, 1, 0); TRS = masked(A.is_gt, 1, 0); TGE = masked(A.is_ge, -1, 0)
+    TRI = masked(A.is_ge, 1, 0); TGT = masked(A.is_gt, -1, 0)
+    A0 = line(TRS, 64.0, -1); A1 = line(B1, 64.0, 15)
+    select(A0, A0, [[-16, 8], [0, 16]], A.is_ge, 0.0, 0, 1)
+    select(A1, A1, [[16, 8], [0, 16]], A.is_gt, 0.0, 16, -1)
+    A0C = line(A0, -128.0, 0); TRX = line(TRS, -4096.0, 0); TRB = line(TRS, 2048.0, 0)
+    ts(R("TGB"), IDN, -2048.0, A.mult)
+    tt(R("TGB"), R("TGB"), TGE, A.add)
     MSL = scaled(MST, -float(2 ** 36), 144); MS = scaled(MST, 0.0625, 144); MSW = scaled(MST, WC, 144); MSI = scaled(MST, PM, 144)
     BW4 = scaled(BLK, W4); BI = scaled(BLK, PM); BL = scaled(BLK, -0.0625); BN8 = scaled(BLK, -8192.0); BN4 = scaled(BLK, -4096.0)
     BP8 = scaled(BLK, 8192.0); BP17 = scaled(BLK, float(2 ** 17))
     ID = {}
-    for c in (-1.0, float(RW), 94.0, 128.0, float(DUMP), 1024.0, -1024.0, 4096.0, 8192.0, -8192.0, 0.5 - me / 4, 1.0 - me / 4):
+    for c in (2.0 ** 24, -1.0, float(RW), 94.0, 128.0, float(DUMP), 1024.0, -1024.0, 4096.0, 8192.0, -8192.0, 0.5 - me / 4, 1.0 - me / 4):
         ID[c] = scaled(IDN, c)
     NTRS = scaled(TRS, -1.0); NTGE = scaled(TGE, -1.0); NTRI = scaled(TRI, -1.0); NTGT = scaled(TGT, -1.0)
     STRS = scaled(TRS, SGN); STGE = scaled(TGE, SGN); STRI = scaled(TRI, SGN); STGT = scaled(TGT, SGN); SID = scaled(ID[-8192.0], SGN)
     IDF = scaled(IDN, 1.0, 128, new("CF", 128))
     K1 = new("CR", 512); IQ = new("CR", 256); KT1 = new("CR", 32); KD = new("CR", 16); KS = new("CR", 16); ZR = new("CR", 264)
-    KH = new("CR", 32); OC = new("CR", 144); QM = new("CF", 170); QO = new("CF", 170); KT = new("CF", 32)
+    KH = new("CR", 32); OC = new("CR", 170); QM = new("CF", 170); KT = new("CF", 32)
     RS = new("CM", 136); PADC = new("CM", 136); RS2 = new("CM", 32)
     iota(KT, [[16, 32]], 1, 0)
-    iota(QM, [[0, 5], [1, 34]], 0, 0)
-    iota(QO, [[1, 5], [0, 34]], 0, 0)
-    ts(KT1, KT, PM, A.add)
-    ts(KD, part(KT1, 0, 16), float(DUMP - 1), A.add)
-    ts(KS, part(KT1, 0, 16), float(TS + 16), A.add)
-    ts(KH, KT1, 0.5, A.add)
-    ts(RS, part(QM, 0, 136), 1.0, A.not_equal)
-    ts(PADC, part(QO, 0, 136), 512.0, A.mult, -8192.0, A.add)
-    ts(R("LR", 0, 136), part(QM, 0, 136), 1.0, A.is_equal)
-    tt(PADC, PADC, R("LR", 0, 136), A.mult)
-    ts(R("T0", 0, 144), part(QM, 0, 144), 2.0, A.is_lt, -9.0, A.mult)
-    tt(OC, part(QO, 0, 144), R("T0", 0, 144), A.add)
-    ts(RS2, part(CMF, 0, 32), 0.0, A.not_equal)
+    act(KT1, KT, AF.Identity, PM)
+    act(KD, part(KT1, 0, 16), AF.Identity, float(DUMP - 1))
+    act(KS, part(KT1, 0, 16), AF.Identity, float(TS + 16))
+    act(KH, KT1, AF.Identity, 0.5)
+    gfill(R("ONE"), 1)
+    select(RS, R("ONE", 0, 136), [[0, 4], [1, 34]], A.not_equal, 0.0, -1, 0)
+    iota(PADC, [[512, 4], [0, 34]], -2048, 0)
+    select(PADC, PADC, [[0, 4], [1, 34]], A.is_equal, 0.0, -1, 0)
+    iota(OC, [[1, 5], [0, 34]], 0, 0)
+    select(OC, OC, [[0, 5], [1, 34]], A.is_ge, -9.0, -2, 0)
+    iota(QM, [[0, 5], [1, 34]], -1, 0)
+    select(QM, QM, [[0, 5], [1, 34]], A.is_ge, 1.0, -2, 0)
+    select(RS2, R("ONE", 0, 32), [[0, 2], [1, 16]], A.not_equal, 0.0, 0, 0)
     copy(R("CU", 1, 2), SGN)
     DK = new("CF", 128)
     ts(DK, part(CMF, 0, 128), PM, A.subtract)
@@ -304,47 +313,60 @@ def rank_program(g, core, T, topo):
         scan(out, R("RL", 0, out[2]), in_, SGH, A.mult, A.min)
         return part(out, 15, out[2], 16)
 
-    ts(R("LA", 0, 144), part(QM, 0, 144), 1.0, A.max, -1.0, A.add)
-    ts(R("LA", 0, 144), R("LA", 0, 144), 1.0, A.max)
-    ts(R("REP", 0, 9), relay(R("LA", 256, 400), R("LA", 0, 144)), SGN, A.mult, -1.0, A.add)
+    ts(R("REP", 0, 9), relay(R("LA", 256, 400), part(QM, 0, 144)), SGN, A.mult, -1.0, A.add)
     OH = new("CF", 16)
     ts(OH, part(CMF, 0, 16), PM, A.is_equal)
 
     def row(i, k):
         return R("SEL", 256 * i + 128 * k, 256 * i + 128 * k + 128)
-    for i in range(15, -1, -1):
-        scaled(BLK, part(OH, i, i + 1), 128, row(i, 1))
+    scaled(BLK, part(OH, 15, 16), 128, row(15, 1))
+    B25 = scaled(BLK, 2.0 ** 25); R24 = scaled(row(15, 1), -2.0 ** 24)
     NSET = len(ops)
     C4 = new("CM", 128)
     gfill(C4, 4096)
-    for i in range(16):
-        put("g", lambda i=i: g.affine_select(row(i, 0)[0], C4[0], [[-16, 8], [0, 16]], A.is_equal, 0.0, -i, 1), C4[1], row(i, 0)[1], (170, 256, 0, 0, 0))
+
+    def rows():
+        for i in range(31):
+            select(row(i % 16, i // 16), R("ONE", 0, 128) if i > 15 else C4, [[-16, 8], [0, 16]], A.is_equal, 0.0, -(i % 16), 1, [("ARR", 0, 1)])
     iota(K1, [[1, 512]], 1 - 4096, 0)
     iota(IQ, [[1, 256]], 0, 0)
+    IB = new("CM", 256)
+    iota(IB, [[16384, 256]], 0, 0)
     iota(R("J1"), [[1, 256]], 1, 0)
-    gfill(R("ONE"), 1)
     gfill(ZR, 0)
     gfill(R("CU", 0, 1), -1)
-    for b, a, c in (("CD", 0, 0), ("OHB", 0, 0), ("SNT", 0, 0), ("YK", 15, 0), ("LN", 0, 0), ("INV", 0, 1), ("UV", 0, 1)):
+    for b, a, c in (("CD", 0, 0), ("VV", 15, 0), ("OHB", 0, 0), ("SNT", 0, 0), ("YK", 15, 0), ("LN", 0, 0), ("INV", 0, 1), ("UV", 0, 1)):
         gfill(R(b, a, a + 1), c)
-    gfill(R("UV", ZC, P + 16), 1)
+    gfill(R("UV", ZC + 1, P + 16), 1)
+    gfill(R("QV", P, P + 1), 1)
+    gfill(R("QV", ZC + 1, P + 16), 1)
     for a in range(0, TS + 272, 464):
         gfill(R("STO", a, a + 464), -1)
     gfill(R("RPL"), 1)
     if RC:
         gfill(R("CC"), CL)
 
-    def vphase():
-        copy(R("KU", 256, 512), I(L("KID"), R("FUV", 16, 32)))
-        copy(R("KU", 0, 256), I(L("KID"), R("FUV", 0, 16)))
+    def vphase(r):
+        if r == 0:
+            copy(R("KU", 256, 512), I(L("KID"), R("FUV", 16, 32)))
+            copy(R("KU", 0, 256), I(L("KID"), R("FUV", 0, 16)))
+            for a in range(0, W, 432):
+                x = R("KID", a, a + 432)
+                copy(R("KDF", a, a + 432), (x[0], L("KID")[1]) + x[2:])
+                ops[-1]["late"] = -40000.0
+            act(R("QV", ZC, ZC + 1), R("KDF", 0, 1), AF.Copy)
+            act(R("UV", ZC, ZC + 1), R("KDF", 0, 1), AF.Copy)
+        else:
+            copy(R("KU", 256, 512), I(R("QV"), R("CT")))
+            copy(R("KU", 0, 256), I(R("UV"), R("CT")))
         act(R("LASTF"), R("MF", 16, P + 16, 16), AF.Identity, 1.0, -1.0)
         gfill(R("JW", 0, 512), 0)
         for o in range(N):
             gfill(R("SND", 512 * o, 512 * o + CAP), -1)
         for c, (a, n) in enumerate(CH):
-            act(R("VV", a, a + n), I(L("VEC"), R("KU", 256 + a // 16, 256 + (a + n) // 16)), AF.Copy)
-            ops[-1]["up"] = 1000.0 if c < 2 else 0.0
-            tt(R("DF", a, a + n), I(L("VEC"), R("KU", a // 16, (a + n) // 16)), R("VV", a, a + n), A.subtract)
+            act(R("DF", a, a + n), I(L("VEC"), R("KU", 256 + a // 16, 256 + (a + n) // 16)), AF.Copy)
+            ops[-1]["up"] = 1000.0 if c < 1 else 0.0
+            tt(R("DF", a, a + n), I(L("VEC"), R("KU", a // 16, (a + n) // 16)), R("DF", a, a + n), A.subtract)
             scan(R("D", a, a + n), R("MF", a, a + n), R("DF", a, a + n), R("D", a - 1, a) if a else 0.0, A.mult, A.add)
         for a, n in BH:
             act(R("AB", a, a + n), R("D", a, a + n), AF.Abs)
@@ -380,36 +402,58 @@ def rank_program(g, core, T, topo):
         mm([(t, IDN, R("JB"))], sums(t, MSI, "OO", 0))
         ts(R("T1"), t, -16.0, A.add)
 
-    def qphase():
+    def qphase(r):
+        rs = RD if r else []
         for a, n in QH:
             u, v = I(R("MRK"), R("KU", a // 16, (a + n) // 16)), I(R("MRK"), R("KU", 256 + a // 16, 256 + (a + n) // 16))
-            if a in RC:
-                k = RC.index(a)
+            if a in RC + rs:
+                k = (RC + rs).index(a)
                 qu, qv, b = R("QB", 1024 * k, 1024 * k + n), R("QB", 1024 * k + 512, 1024 * k + 512 + n), R("BE", 0, n)
                 act(qv, v, AF.Identity, -float(CL))
                 act(qu, u, AF.Identity, -float(CL))
                 mm([(b, ID[-1.0], qv)], [(b, IDN, qu)])
                 act(qu, b, AF.Relu)
-                x = R("BG", 0, n)
-                mm([(x, IDF, R("D", a, a + n))], [(x, IDN, R("CC", 0, n))], [(x, IDN, qv)], [(x, IDN, qu)])
+                if a in RC:
+                    x = R("BG", 0, n)
+                    mm([(x, IDF, R("D", a, a + n))], [(x, IDN, R("CC", 0, n))], [(x, IDN, qv)], [(x, IDN, qu)])
+                else:
+                    mm([(b, IDN, qv)], [(b, IDN, qu)])
+                    act(R("QV", a, a + n), b, AF.Identity, float(CL))
             else:
                 act(R("QV", a, a + n), v, AF.Copy)
                 tt(R("QV", a, a + n), u, R("QV", a, a + n), A.max)
         for c, (a, n) in enumerate(AH):
             if a not in RC:
                 addto(R("D", a, a + n), R("QV", a, a + n), "ac%d" % c)
+        signs = [c for c in range(8) if r == 0 or 512 * c in RC]
         for c in range(8):
-            b = R(("BB", "BC")[c % 2])
-            mm([(b, B1, R("AB", 512 * c, 512 * c + 512))])
-            act(R("NS", 512 * c + 1, 512 * c + 513), b, AF.Sign)
+            a, b = 512 * c, ("BB", "BC")[c % 2]
+            if c in signs:
+                mm([(R(b), B1, R("AB", a - 1, a + 511))])
+                act(R("NS", a, a + 512), R(b), AF.Sign)
+            else:
+                mm([(R(b), B25, R("AB", a - 1, a + 511))])
+                mm([(R(b, 0, 512, 16), ID[2.0 ** 24], R("ONE", 0, 32)), (R(b, 0, 512, 16), R24, R("CU", 1 + 32 * c, 33 + 32 * c))])
+                scan(R("EM", a, a + 512), R(b), R("D", a, a + 512), R("EM", a - 1, a) if a else 0.0, A.min, A.add)
         b = R("BA", 256, 512)
         mm([(b, row(15, 1), R("CU", 1, 257))])
         for a, n in EH:
-            act(R("NS", a, a + n, 16), part(b, a // 16, (a + n) // 16), AF.Relu, 0.0, -1.0)
-            x = R("BG", 0, n) if a in RC else R("D", a, a + n)
-            scan(R("EM", a, a + n), R("NS", a, a + n), x, R("EM", a - 1, a) if a else 0.0, A.mult, A.add)
+            if a // 512 in signs:
+                act(R("NS", a, a + n, 16), part(b, a // 16, (a + n) // 16), AF.Relu, 0.0, -1.0)
+                x = R("BG", 0, n) if a in RC else R("D", a, a + n)
+                scan(R("EM", a, a + n), R("NS", a, a + n), x, R("EM", a - 1, a) if a else 0.0, A.mult, A.add)
+
+    def kids(b, at):
+        for a in range(0, P, 512):
+            o, x = R(b, 1 + a, 513 + a), I(R("KDF"), R("KU", at + a // 16, at + a // 16 + 32))
+            if at and a == P - 512:
+                copy(o, x)
+            else:
+                act(o, x, AF.Copy)
+                ops[-1]["late"] = -5000.0
 
     def pairs():
+        gfill(R("UV", ZC, ZC + 1), 1)
         for i in range(16):
             b = R(("BB", "BC")[i % 2], 0, 256)
             mm([(b, row(i, 1), R("KF", 0, 256)), (b, row(i, 0), R("KF", 256, 512))])
@@ -426,23 +470,29 @@ def rank_program(g, core, T, topo):
                 rd += x[1]
                 tot += len(m[d])
                 tr.append(RemoteDMATransfer(dst_ids=[DstId(rid=rid, pnc=pid)], dma_engine_mask=sum(1 << e for e in m[d]), remote_sem=T.sem[rsem], src=x[0], dst=dst[0]))
-        put("g", lambda: g.remote_dma_fused(tr, local_sem=T.sem[lsem]), rd, [(lsem, 0, 1)], 400.0, 1400.0, lsem, -tot)
+        put("g", lambda: g.remote_dma_fused(tr, local_sem=T.sem[lsem]), rd, [(lsem, 0, 1)], 400.0, 2900.0 if lsem == "lk0" else 1400.0, lsem, -tot)
         act(dst, src(me), AF.Copy)
         tot = sum(len(masks(s)[me]) for s in range(N) if s != me)
         put("n", None, [(lsem, 0, 1)], [(buf, base + CAP * s, base + CAP * s + CAP) for s in range(N) if s != me], 1.0, NET - 1800.0, rsem, tot)
 
     def keys(r):
-        ts(R("ZI"), I(R("EM"), R("T1")), float(2 ** 30), A.min, -float(2 ** 30), A.max)
-        ts(R("Z8"), R("ZI"), 255, A.bitwise_and)
-        copy(R("ZB"), R("Z8"))
+        ts(R("ZI"), I(R("EM", 0, P), R("T1")), float(2 ** 30), A.min, -float(2 ** 30), A.max)
+        for k in range(2):
+            ts(R("Z8", k, 512, 2), R("ZI", k, 512, 2), 255, A.bitwise_and)
+            ops[-1]["w"] = [("Z8", k, k + 1)]
+        for k in range(2):
+            copy(R("ZB", k, 512, 2), R("Z8", k, 512, 2))
+            ops[-1]["r"], ops[-1]["w"] = [("Z8", k, k + 1)], [("ZB", k, k + 1)]
         h = R("BD", 0, 32)
-        mm(sums(h, MSW, "ZB", 0))
+        mm(sums(h, MSW, "ZB", 0)[0::2], sums(h, MSW, "ZB", 0)[1::2])
+        for k in range(2):
+            ops[k - 2]["r"] = MSW[1] + [("ZB", k, k + 1)]
         copy(R("HI"), h)
         ts(R("OW"), R("HI"), 3, A.bitwise_and)
-        tt(R("OHB", 1, 145), I(R("OW"), R("REP", 0, 9)), OC, A.is_equal)
+        tt(R("OHB", 1, 145), I(R("OW"), R("REP", 0, 9)), part(OC, 0, 144), A.is_equal)
         k = R("BF", 0, 136)
         mm([(k, IDN, PADC)] + [(R("BF", 34 * o + 2, 34 * o + 34), ID[c], R("INV", a, a + 32)) for o in range(N) for c, a in ((-1024.0, 1), (1024.0, 0))],
-           [(k, TRB, R("OHB", 1, 137)), (k, TGE, R("OHB", 0, 136)), (k, ID[-8192.0], R("OHB", 0, 136))])
+           [(k, TRB, R("OHB", 1, 137)), (k, R("TGB"), R("OHB", 0, 136))])
         scan(R("RK"), RS, k, 0.0, A.mult, A.add)
         tt(R("R2", 0, 66), R("RK", 2, 68), R("RK", 70, 136), A.max)
         tt(R("RQ"), R("R2", 0, 32), R("R2", 34, 66), A.max)
@@ -451,7 +501,7 @@ def rank_program(g, core, T, topo):
         fused(lambda d: R("SND", 512 * d, 512 * d + CAP), "ARR", 256 * r, "lk%d" % r, "ka%d" % r,
               R("RPL", RW * r, RW * r + RW)[1])
         gfill(R("NXT", 0, 256), 0)
-        act(R("LA"), I(R("EM"), R("T1")), AF.Identity, RND, 1.0 / CL)
+        act(R("LA"), I(R("EM", 0, P), R("T1")), AF.Identity, RND, 1.0 / CL)
         act(R("LR"), R("LA"), AF.Identity, -RND)
         t = R("BE")
         mm([(t, B1, R("JK")), (t, BI, R("OO")), (t, BL, R("LR"))])
@@ -499,16 +549,20 @@ def rank_program(g, core, T, topo):
         ts(R("RR"), pa, M11, A.add, M11, A.subtract)
         tt(R("P1"), pb, R("RR"), A.subtract)
         yp = relay(R("YP"), R("P1"))
-        ts(R("PU"), yp, SGN, A.mult, -1.0, A.add)
-        tt(R("NQ"), I(R("STO"), R("PU")), arr, A.not_equal)
         s, n = R("BA", 0, 256), R("BD", 0, 256)
-        mm([(s, ID[4096.0], R("ONE")), (s, BP8, R("NEG"))], [(s, BN4, R("NQ"))])
+        nq = R("NQ") if r else R("ONE")
+        if r:
+            ts(R("PU"), yp, SGN, A.mult, -1.0, A.add)
+            tt(nq, I(R("STO"), R("PU")), arr, A.not_equal)
+            mm([(s, ID[4096.0], R("ONE")), (s, BP8, R("NEG"))], [(s, BN4, nq)])
+        else:
+            mm([(s, ID[4096.0], R("ONE")), (s, BN4, nq)], [(s, BP8, R("NEG"))])
         copy(R("R1"), R("P1"))
         act(R("BE", 0, 256), R("P1"), AF.Identity, 0.0, -1.0)
         tt(R("PMR"), s, R("P1"), A.max)
         relay(R("YM"), R("PMR"))
         tt(R("ED"), R("YM"), R("BE", 0, 256), A.is_equal)
-        eo = [[(n, ID[4096.0], R("ONE")), (n, BP8, R("NEG")), (n, BN4, R("NQ"))]]
+        eo = [[(n, ID[4096.0], R("ONE")), (n, BP8, R("NEG")), (n, BN4, nq)]]
         lo = 0
         es = []
         act(R("YB", 0, 16), R("YM", 15, 256, 16), AF.Identity, 0.5, NSG)
@@ -557,40 +611,41 @@ def rank_program(g, core, T, topo):
         mm([(R("BG", 0, 16), B1, R("KB"))])
         act(R("X3"), R("BG", 0, 16), AF.Identity, 512.0, -16384.0, R("TOB", 0, 1))
         act(R("F0"), IQ, AF.Relu, R("TOB", 0, 1), 16384.0)
-        act(R("FF"), R("F0"), AF.Identity, 1.0)
         act(R("FA"), R("F0"), AF.Relu, 0.5, -1.0)
         copy(I(R("NXT"), R("OF2")), R("T2"))
+        ts(R("FF"), IB, R("TOB", 0, 1), A.add, 1.0, A.max)
         scan(R("PP"), R("FF"), R("NXT", 0, 256), 0.0, A.add, A.max)
         ts(R("CT"), relay(R("YQ"), R("PP")), SGN, A.mult, float(ZC), A.min)
         act(R("NEG"), R("NXT", 0, 256), AF.Relu, 1.0, -1.0)
         mm([(R("BH", 0, 256), IDN, R("FA"))], [(R("BH", 0, 256), IDN, R("NEG"))])
-        act(R("MF", 0, P, 16), R("BH", 0, 256), AF.Relu, -2.0, 2.0)
         if r < RO - 1:
-            copy(R("GU"), I(R("UV"), R("CT")))
-            y = relay(R("YU"), R("GU"))
-            ts(R("FUV", 16, 32), y, SG12, A.mult, -0.5, A.add)
-            ts(R("WI"), y, SGN, A.mult, -1.0, A.add)
-            ts(R("UI"), R("WI"), 4095, A.bitwise_and)
-            copy(R("FUV", 0, 16), R("UI"))
+            act(R("MF", 0, P, 16), R("BH", 0, 256), AF.Relu, -2.0, 2.0)
         else:
+            act(R("OUTF", 512, 768), R("BH", 0, 256), AF.Sign, 1.5, -1.0)
             ts(R("ZI", 0, 256), I(R("UV"), R("CT")), -1.0, A.add)
             ts(R("Z8", 0, 256), R("ZI", 0, 256), 4095, A.bitwise_and)
             copy(R("OUTF", 0, 256), R("Z8", 0, 256))
             act(R("GU"), I(R("UV"), R("CT")), AF.Identity, -0.5, 2.0 ** -12)
             act(R("YU"), R("GU"), AF.Identity, RND)
             act(R("OUTF", 256, 512), R("YU"), AF.Identity, -RND)
-            act(R("OUTF", 512, 768), R("MF", 0, P, 16), AF.Identity, 1.0, -1.0)
             for k, (q, y) in enumerate((("y", T.yu), ("s", T.yv), ("y", T.ys))):
                 dma(q, "st%d" % (k + 1), H(y[:]), R("OUTF", 256 * k, 256 * k + 256, p=(0, 128, 16)), 64)
 
     for r in range(RO):
-        vphase()
+        vphase(r)
         comp()
-        qphase()
-        pairs()
+        qphase(r)
+        if r < RO - 1:
+            kids("UV", 0)
+        else:
+            pairs()
         keys(r)
+        if r < RO - 1:
+            kids("QV", 256)
         owner(r)
         nextfront(r)
+        if r == 0:
+            rows()
 
     n = len(ops)
 
@@ -636,7 +691,16 @@ def rank_program(g, core, T, topo):
             for y, d in arcs[x]:
                 rank[y] = max(rank[y], rank[x] + d)
         at, end, busy, dfree = [0.0] * n, [0.0] * n, [[] for _ in range(6)], 0.0
-        for x in sorted(range(n), key=lambda x: (0, x) if x < NLOAD else (1 if x < NSET else 2, -rank[x], x)):
+        key = [(0, x) if x < NLOAD else (1, ops[x].get("late", 0.0) - rank[x], x) for x in range(n)]
+        left = [len(p) for p in pred]
+        ready = [x for x in range(n) if not left[x]]
+        while ready:
+            x = min(ready, key=lambda x: key[x])
+            ready.remove(x)
+            for y in succ[x]:
+                left[y] -= 1
+                if not left[y]:
+                    ready.append(y)
             h = hs[0][x]
             t = max([end[y] + d for y, d in arcs[x]] + [0.0])
             lst = busy[qn[x]]

import math
from concourse.bass import DstId, RemoteDMATransfer
from concourse.mybir import AluOpType, ActivationFunctionType

A = AluOpType
AF = ActivationFunctionType
W, F, FC, CAP, TS, RO = 3456, 256, 512, 64, 2048, 3
P = 16 * F
RND = 1.5 * 2 ** 23
M11 = 1.5 * 2 ** 34
CL = 393216
HALF = W // 2
CH = QH = [(512 * c, 512) for c in range(8)]
AH = [(0, 1024), (1024, 1024), (2048, 1024), (3072, 512), (3584, 512)]
EH = AH
BH = AH
RC = [3584]
RD = [3072]
EV = 13
RW = 272
DUMP = 4128
ZC = P + 1


def shapes(kind, dtype, text):
    return {w.split(":")[0]: (kind, [128, int(w.split(":")[1])], dtype) for w in text.split()}


SCRATCH = {}
SCRATCH.update(shapes("sbuf", "int32", "KID:3456 FUI:32 FSI:256 ZI:512 Z8:512 HI:32 OW:32 CI:64"))
SCRATCH.update(shapes("sbuf", "uint16", "FUV:32 KU:512 OPU:16 JT:32 T1:32 OFF:32 PU:16 R1:256 SU:16 OF2:16 CT:16 OP2:2 REP:10 JT2:16 KS2:16 OFS:16"))
SCRATCH.update(shapes("sbuf", "float16", "KF:512 TGB:128"))
SCRATCH.update(shapes("sbuf", "bfloat16", "VEC:3456 FSB:256 LASTF:256 EQ:256 MF:4112 VV:4112 CU:264 NS:4112 AP:256 CD:264 SEL:4096 "
                      "JW:4384 JK:512 YJ:512 JB:32 OO:512 LR:512 ZB:512 OHB:160 INV:40 STO:2320 NQ:256 NEG:256 ED:256 YN:256 "
                      "NK:256 YK:272 LN:24 KB:16 SNT:40 JW2:320 JK2:256 YJ2:256 JB2:16 OO2:256 SG:256 PR:256 LR2:256 "
                      "CM:7168 RL:512 SND:4096 ARR:768 NEW:768 RPL:816 ONE:256 J1:256 FF:256 FA:256 QB:2048 CC:512"))
SCRATCH.update(shapes("sbuf", "float32", "MRK:3456 KDF:3456 QV:4112 D:4640 UV:4112 SC:264 XX:256 YX:256 XC:256 LA:512 T0:512 "
                      "RK:136 R2:72 RR:256 P1:256 T2:256 YP:256 PMR:256 YM:256 PP:256 YQ:256 GU:256 YU:256 F0:256 "
                      "CF:1152 CR:1536 SM:576"))
VIEW = {}
for _w in ("RQ:32 S1:16 S2:16 S3:16 PF:16 SE:32 DU:16 X1:16 NR:16 GF:16 X3:16 O3:32 TH:32 O4:32 SLT:32 SC2:40 X2:32 Y2:32 XC2:32 "
           "TOB:8 YB:32").split():
    _n, _k = _w.split(":")
    VIEW[_n] = ("SM", sum(x[2] for x in VIEW.values()), int(_k))
SAME = {"DF": "VV", "AB": "VV", "EM": "QV", "NXT": "D", "EO": "NS"}
BANKS = ("BA", "BB", "BC", "BD", "BE", "BF", "BG", "BH")
SCRATCH.update({b: ("psum", [128, 512], "float32") for b in BANKS})
SEMAPHORES = ["qv", "qs", "qt", "qg"] + ["ld%d" % k for k in range(9)] + ["st%d" % k for k in range(4)] + ["ac%d" % k for k in range(len(AH))] + \
             ["%s%d" % (s, r) for s in ("ka", "ra", "lk", "lr") for r in range(RO)]
SIZE = {"int32": 4, "float32": 4, "uint16": 2, "float16": 2, "bfloat16": 2}
WAKE, NET, DMA0, DMAB, DMAL = 120.0, 2150.0, 2000.0, 0.55, 0.48
PACE = ((0.83, 0.6, 1.56, 3.0, 50.0), (1.2, 0.95, 2.0, 5.5, 30.0), (0.83, 0.55, 1.15, 2.0, 40.0))
WEIGHT = (1.0, 0.5, 1.0)
TRIES, HEAT, SEED = 55000, 30.0, 17
ORDER = {}


def lasts(q, c, pace):
    if not isinstance(c, tuple):
        return c
    return c[0] + pace[0] * (c[1] + pace[2] * c[2] + pace[3] * c[3]) + pace[1] * c[4] + (pace[4] if q in "vs" else 0.0) + (15.0 if q == "s" else 0.0)


def rank_program(g, core, T, topo):
    me = T.rank_of(core)
    if me is None:
        return
    cores = list(T.cores)
    N = len(cores)

    def masks(src):
        s = cores[src]
        out = [d for d in range(N) if d != src and topo.chip(cores[d]) != topo.chip(s)]
        on = [d for d in range(N) if d != src and topo.chip(cores[d]) == topo.chip(s)]
        res = {}
        used = []
        for ds in (out, on):
            if ds:
                lst = [e for e in topo.engines(s, cores[ds[0]]) if e not in used]
                if ds is on and out:
                    lst = lst[::max(1, len(lst) // (len(on) * len(res[out[0]])))]
                n = 1
                while n * 2 * len(ds) <= len(lst):
                    n *= 2
                for x, d in enumerate(ds):
                    res[d] = lst[x * n:(x + 1) * n]
                    used = used + res[d]
        return res

    ops = []

    def put(q, fn, reads, writes, hold, lat=0.0, sem=None, inc=1, chained=False, load=0.0):
        w = [(x[0], 0, 512) if x[0] in BANKS else x for x in writes]
        r = [(x[0], 0, 512) if x[0] in BANKS else x for x in reads]
        ops.append({"q": q, "fn": fn, "r": r, "w": w, "hold": [lasts(q, hold, p) for p in PACE], "lat": lat, "sem": sem or "q" + q,
                    "inc": inc, "ch": chained, "load": load})

    def R(name, lo=None, hi=None, step=None, p=None):
        if name in ("DF", "AB"):
            lo, hi = lo + 16, hi + 16
        if name == "OUTF":
            name, lo, hi = ("XX", "YX", "XC")[lo // 256], 0, 256
        name = SAME.get(name, name)
        if name in VIEW:
            name, at, n = VIEW[name]
            lo, hi = (at, at + n) if lo is None else (at + lo, at + hi)
        t = T[name]
        if lo is None:
            lo, hi = 0, t.shape[1]
        if p is not None:
            ap = t[p[0]:p[1]:p[2], lo:hi] if len(p) > 2 else t[p[0]:p[1], lo:hi]
        else:
            ap = t[:, lo:hi] if step is None else t[:, lo:hi:step]
        return (ap, [(name, lo, hi)], len(range(lo, hi, step or 1)), SIZE[SCRATCH[name][2]], name in BANKS, False)

    def I(win, off):
        return (win[0].indirect(off[0]), win[1] + off[1], 16 * off[2], win[3], False, True)

    def H(t):
        return (t, [], 0, 4, False, False)

    def rg(*xs):
        return [r for x in xs if isinstance(x, tuple) for r in x[1]]

    def va(x):
        return x[0] if isinstance(x, tuple) else x

    def cost(out, *ins, both=False):
        if out[5]:
            return (50, 0, 0, out[2], 0)
        if ins and ins[0][5]:
            return (50, 0, out[2], 0, 0)
        f = 0.5 if all(x[3] == 2 for x in (out,) + ins) else 1.0
        if both and not any(x[4] for x in ins):
            f *= 2
        return (0, max(64, out[2] * f), 0, 0, 0)

    def copy(out, in_):
        put("v", lambda: g.vector.tensor_copy(out=out[0], in_=in_[0]), rg(in_) + out[1][1:], out[1][:1], cost(out, in_))

    def tt(out, a, b, o):
        put("v", lambda: g.vector.tensor_tensor(out=out[0], in0=a[0], in1=b[0], op=o), rg(a, b), out[1], cost(out, a, b, both=True))

    def ts(out, a, s1, o1, s2=None, o2=None):
        if o2 is None:
            put("v", lambda: g.vector.tensor_scalar(out=out[0], in0=a[0], scalar1=va(s1), scalar2=None, op0=o1), rg(a, s1), out[1], cost(out, a))
        else:
            put("v", lambda: g.vector.tensor_scalar(out=out[0], in0=a[0], scalar1=va(s1), scalar2=va(s2), op0=o1, op1=o2), rg(a, s1, s2), out[1], cost(out, a))

    def scan(out, d0, d1, init, o1, o2):
        put("v", lambda: g.vector.tensor_tensor_scan(out=out[0], data0=d0[0], data1=d1[0], initial=va(init), op0=o1, op1=o2), rg(d0, d1, init), out[1], cost(out, d0, d1))

    def fill(out, c):
        put("v", lambda: g.vector.memset(out[0], c), [], out[1], cost(out))

    def act(out, in_, f, bias=0.0, scale=1.0, acc=None):
        c = (65, 0, out[2], 0, 0) if in_[5] else (0, max(64, out[2]), 0, 0, 0)
        if acc is None:
            put("s", lambda: g.scalar.activation(out=out[0], in_=in_[0], func=f, bias=va(bias), scale=va(scale)), rg(in_, bias, scale), out[1], c)
        else:
            put("s", lambda: g.scalar.activation(out=out[0], in_=in_[0], func=f, bias=bias, scale=scale, accum_out=acc[0]), rg(in_), out[1] + acc[1], c)

    def mm(*parts):
        for x, part in enumerate(parts):
            def fn(part=part, first=(x == 0), last=(x == len(parts) - 1)):
                ins = None
                for k, (o, l, r) in enumerate(part):
                    ins = g.tensor.matmul(out=o[0], lhsT=l[0], rhs=r[0], start=(first and k == 0), stop=(last and k == len(part) - 1))
                return ins
            put("t", fn, rg(*[y for p in part for y in p[1:]]), part[0][0][1], (0, 0, 0, 0, sum(max(64, p[0][2]) * (p[2][3] ** 2 // 4) for p in part)), chained=(x > 0))

    def iota(out, pat, base, cm, flag=True):
        if flag:
            put("g", lambda: g.iota(out[0], pat, base, cm, allow_small_or_imprecise_dtypes=True), [], out[1], (130, 2 * out[2], 0, 0, 0))
        else:
            put("g", lambda: g.iota(out[0], pat, base, cm), [], out[1], (130, 2 * out[2], 0, 0, 0))

    def gfill(out, c):
        iota(out, [[0, out[2]]], c, 0)

    queues = {"v": g.vector, "s": g.scalar, "t": g.tensor, "g": g, "y": g.sync}

    def dma(q, sem, out, in_, load):
        put(q, lambda: queues[q].dma_start(out=out[0], in_=in_[0]), in_[1], out[1], 60.0, DMA0 - 500.0, sem, 16, load=load * DMAL + 1.0)

    def addto(out, in_, sem, after=()):
        put("g", lambda: g.dma_start(out=out[0], in_=in_[0], accum_op=A.add), in_[1] + list(after), out[1], 600.0, DMA0, sem, 16, load=4 * out[2] * DMAB)

    free = {"CI": 0, "CF": 0, "CM": 0, "CR": 0}

    def new(buf, n):
        lo = free[buf]
        free[buf] = lo + (n + 15) // 16 * 16
        return R(buf, lo, lo + n)

    def part(m, a, b, step=None):
        return R(m[1][0][0], m[1][0][1] + a, m[1][0][1] + b, step)

    def win(m, i):
        return part(m, 15 - i, 143 - i)

    def L(name):
        x = R(name)
        return (x[0], [(name, 0, W + 2)]) + x[2:]

    dma("y", "ld0", R("FUI", 0, 16), H(T.fu[:]), 64)
    dma("s", "ld1", R("FUI", 16, 32), H(T.fv[:]), 64)
    dma("s", "ld2", R("FSI", 0, 256, p=(0, 8)), H(T.fs[:]), 64)
    for k, (b, x) in enumerate((("KID", T.kids), ("VEC", T.vec))):
        for q, lo in (("y", 0), ("s", 64)):
            dma(q, "ld%d" % (3 + 2 * k + lo // 64), (T[b][lo:lo + 64, :], [(b, W + lo // 64, W + lo // 64 + 1)]), H(x[lo:lo + 64, :]),
                SIZE[SCRATCH[b][2]] * HALF)
    pI = new("CI", 1); CG = new("CF", 144); CMF = new("CF", 144); PX = new("CF", 1)
    iota(pI, [[0, 1]], 0, 1, False)
    iota(CG, [[1, 9], [0, 16]], 0, 0)
    iota(CMF, [[0, 9], [1, 16]], 0, 0)
    iota(PX, [[0, 1]], 0, 1)
    NLOAD = len(ops)
    gfill(R("MRK", 0, HALF), CL)
    gfill(R("MRK", HALF, W), CL)
    for k in range(2):
        addto(R("MRK", HALF * k, HALF * k + HALF), H(T.mark[:, HALF * k:HALF * k + HALF]), "ld%d" % (7 + k), L("KID")[1])

    pmI = new("CI", 1); pgI = new("CI", 1); PM = new("CF", 1); PG = new("CF", 1)
    ts(pmI, pI, 15, A.bitwise_and)
    ts(pgI, pI, 4, A.arith_shift_right)
    copy(PM, pmI); copy(PG, pgI)
    BLK = new("CM", 144); MST = new("CM", 144); R8 = new("CM", 128)
    ts(BLK, CG, PG, A.is_equal)
    ts(MST, CMF, 15.0, A.is_equal)
    tt(MST, MST, BLK, A.mult)
    ts(R8, part(CG, 0, 128), PX, A.is_equal)
    fill(R("MF", 0, P), 1.0)
    gfill(R("MF", P, P + 16), 0)
    ts(R("FSB", 0, 256, p=(0, 8)), R("FSI", 0, 256, p=(0, 8)), -1.0, A.mult, 1.0, A.add)
    r0 = R8[1][0][1]
    mm([(R("BA", 0, 256), R("CM", r0, r0 + 128, p=(0, 8)), R("FSB", 0, 256, p=(0, 8)))])
    copy(R("MF", 0, P, 16), R("BA", 0, 256))
    copy(R("FUV"), R("FUI"))
    WC = new("CF", 1); W4 = new("CF", 1); SGN = new("CF", 1); SG16 = new("CF", 1); SGH = new("CF", 1); NSG = new("CF", 1); SG12 = new("CF", 1)
    ts(WC, PM, -14.0, A.mult, 255.0, A.add)
    ts(W4, PM, -3.5, A.mult, 63.75, A.add)
    ts(SGH, PM, 15.0, A.is_equal, -0.5, A.add)
    for x, c in ((SGN, 2.0), (SG16, 32.0), (NSG, -2.0), (SG12, 2.0 ** -11)):
        ts(x, SGH, c, A.mult)

    def scaled(src, by, n=128, m=None):
        m = m or new("CM", n)
        act(m, part(src, 0, n), AF.Identity, 0.0, by)
        return m
    B1 = part(BLK, 0, 128)

    def masked(o, sign, base):
        m = new("CM", 128)
        put("g", lambda: g.affine_select(m[0], B1[0], [[sign, 128]], o, 0.0, base, -sign), B1[1], m[1], (170, 256, 0, 0, 0))
        return m

    def select(out, in_, pat, o, c, base, cm, after=()):
        put("g", lambda: g.affine_select(out[0], in_[0], pat, o, c, base, cm), in_[1] + list(after), out[1], (170, 2 * out[2], 0, 0, 0))
        return out

    def line(a, c, base):
        return select(new("CM", 128), a, [[1, 128]], A.not_equal, c, base, -1)
    IDN = masked(A.is_equal, 1, 0); TRS = masked(A.is_gt, 1, 0); TGE = masked(A.is_ge, -1, 0)
    TRI = masked(A.is_ge, 1, 0); TGT = masked(A.is_gt, -1, 0)
    A0 = line(TRS, 64.0, -1); A1 = line(B1, 64.0, 15)
    select(A0, A0, [[-16, 8], [0, 16]], A.is_ge, 0.0, 0, 1)
    select(A1, A1, [[16, 8], [0, 16]], A.is_gt, 0.0, 16, -1)
    A0C = line(A0, -128.0, 0); TRX = line(TRS, -4096.0, 0); TRB = line(TRS, 2048.0, 0)
    ts(R("TGB"), IDN, -2048.0, A.mult)
    tt(R("TGB"), R("TGB"), TGE, A.add)
    MSL = scaled(MST, -float(2 ** 36), 144); MS = scaled(MST, 0.0625, 144); MSW = scaled(MST, WC, 144); MSI = scaled(MST, PM, 144)
    BW4 = scaled(BLK, W4); BI = scaled(BLK, PM); BL = scaled(BLK, -0.0625); BN8 = scaled(BLK, -8192.0); BN4 = scaled(BLK, -4096.0)
    BP8 = scaled(BLK, 8192.0); BP17 = scaled(BLK, float(2 ** 17))
    ID = {}
    for c in (2.0 ** 24, -1.0, float(RW), 94.0, 128.0, float(DUMP), 1024.0, -1024.0, 4096.0, 8192.0, -8192.0, 0.5 - me / 4, 1.0 - me / 4):
        ID[c] = scaled(IDN, c)
    NTRS = scaled(TRS, -1.0); NTGE = scaled(TGE, -1.0); NTRI = scaled(TRI, -1.0); NTGT = scaled(TGT, -1.0)
    STRS = scaled(TRS, SGN); STGE = scaled(TGE, SGN); STRI = scaled(TRI, SGN); STGT = scaled(TGT, SGN); SID = scaled(ID[-8192.0], SGN)
    IDF = scaled(IDN, 1.0, 128, new("CF", 128))
    K1 = new("CR", 512); IQ = new("CR", 256); KT1 = new("CR", 32); KD = new("CR", 16); KS = new("CR", 16); ZR = new("CR", 264)
    KH = new("CR", 32); OC = new("CR", 170); QM = new("CF", 170); KT = new("CF", 32)
    RS = new("CM", 136); PADC = new("CM", 136); RS2 = new("CM", 32)
    iota(KT, [[16, 32]], 1, 0)
    act(KT1, KT, AF.Identity, PM)
    act(KD, part(KT1, 0, 16), AF.Identity, float(DUMP - 1))
    act(KS, part(KT1, 0, 16), AF.Identity, float(TS + 16))
    act(KH, KT1, AF.Identity, 0.5)
    gfill(R("ONE"), 1)
    select(RS, R("ONE", 0, 136), [[0, 4], [1, 34]], A.not_equal, 0.0, -1, 0)
    iota(PADC, [[512, 4], [0, 34]], -2048, 0)
    select(PADC, PADC, [[0, 4], [1, 34]], A.is_equal, 0.0, -1, 0)
    iota(OC, [[1, 5], [0, 34]], 0, 0)
    select(OC, OC, [[0, 5], [1, 34]], A.is_ge, -9.0, -2, 0)
    iota(QM, [[0, 5], [1, 34]], -1, 0)
    select(QM, QM, [[0, 5], [1, 34]], A.is_ge, 1.0, -2, 0)
    select(RS2, R("ONE", 0, 32), [[0, 2], [1, 16]], A.not_equal, 0.0, 0, 0)
    copy(R("CU", 1, 2), SGN)
    DK = new("CF", 128)
    ts(DK, part(CMF, 0, 128), PM, A.subtract)
    ts(R("OO", 0, 128), DK, 0.0, A.is_equal, -float(2 ** 40), A.mult)
    ts(R("OO", 128, 256), DK, 1.0, A.is_equal, -2.0, A.mult)
    ts(R("OO", 256, 384), DK, -15.0, A.is_equal, -2.0, A.mult)
    tt(R("OO", 0, 128), R("OO", 0, 128), R("OO", 128, 256), A.add)
    tt(R("OO", 0, 128), R("OO", 0, 128), R("OO", 256, 384), A.add)
    for k in range(4):
        act(R("RL", 128 * k, 128 * k + 128), R("OO", 0, 128), AF.Identity, 1.0)

    def sums(out, m, b, lo):
        return [(out, win(m, i), R(b, lo + i, lo + 16 * out[2], 16)) for i in range(16)]

    def relay(out, in_):
        scan(out, R("RL", 0, out[2]), in_, SGH, A.mult, A.min)
        return part(out, 15, out[2], 16)

    ts(R("REP", 0, 9), relay(R("LA", 256, 400), part(QM, 0, 144)), SGN, A.mult, -1.0, A.add)
    OH = new("CF", 16)
    ts(OH, part(CMF, 0, 16), PM, A.is_equal)

    def row(i, k):
        return R("SEL", 256 * i + 128 * k, 256 * i + 128 * k + 128)
    scaled(BLK, part(OH, 15, 16), 128, row(15, 1))
    B25 = scaled(BLK, 2.0 ** 25); R24 = scaled(row(15, 1), -2.0 ** 24)
    NSET = len(ops)
    C4 = new("CM", 128)
    gfill(C4, 4096)

    def rows():
        for i in range(31):
            select(row(i % 16, i // 16), R("ONE", 0, 128) if i > 15 else C4, [[-16, 8], [0, 16]], A.is_equal, 0.0, -(i % 16), 1, [("ARR", 0, 1)])
    iota(K1, [[1, 512]], 1 - 4096, 0)
    iota(IQ, [[1, 256]], 0, 0)
    IB = new("CM", 256)
    iota(IB, [[16384, 256]], 0, 0)
    iota(R("J1"), [[1, 256]], 1, 0)
    gfill(ZR, 0)
    gfill(R("CU", 0, 1), -1)
    for b, a, c in (("CD", 0, 0), ("VV", 15, 0), ("OHB", 0, 0), ("SNT", 0, 0), ("YK", 15, 0), ("LN", 0, 0), ("INV", 0, 1), ("UV", 0, 1)):
        gfill(R(b, a, a + 1), c)
    gfill(R("UV", ZC + 1, P + 16), 1)
    gfill(R("QV", P, P + 1), 1)
    gfill(R("QV", ZC + 1, P + 16), 1)
    for a in range(0, TS + 272, 464):
        gfill(R("STO", a, a + 464), -1)
    gfill(R("RPL"), 1)
    if RC:
        gfill(R("CC"), CL)

    def vphase(r):
        if r == 0:
            copy(R("KU", 256, 512), I(L("KID"), R("FUV", 16, 32)))
            copy(R("KU", 0, 256), I(L("KID"), R("FUV", 0, 16)))
            for a in range(0, W, 432):
                x = R("KID", a, a + 432)
                copy(R("KDF", a, a + 432), (x[0], L("KID")[1]) + x[2:])
                ops[-1]["late"] = -40000.0
            act(R("QV", ZC, ZC + 1), R("KDF", 0, 1), AF.Copy)
            act(R("UV", ZC, ZC + 1), R("KDF", 0, 1), AF.Copy)
        else:
            copy(R("KU", 256, 512), I(R("QV"), R("CT")))
            copy(R("KU", 0, 256), I(R("UV"), R("CT")))
        act(R("LASTF"), R("MF", 16, P + 16, 16), AF.Identity, 1.0, -1.0)
        gfill(R("JW", 0, 512), 0)
        for o in range(N):
            gfill(R("SND", 512 * o, 512 * o + CAP), -1)
        for c, (a, n) in enumerate(CH):
            act(R("DF", a, a + n), I(L("VEC"), R("KU", 256 + a // 16, 256 + (a + n) // 16)), AF.Copy)
            ops[-1]["up"] = 1000.0 if c < 1 else 0.0
            tt(R("DF", a, a + n), I(L("VEC"), R("KU", a // 16, (a + n) // 16)), R("DF", a, a + n), A.subtract)
            scan(R("D", a, a + n), R("MF", a, a + n), R("DF", a, a + n), R("D", a - 1, a) if a else 0.0, A.mult, A.add)
        for a, n in BH:
            act(R("AB", a, a + n), R("D", a, a + n), AF.Abs)
        for a, n in AH:
            b = R("BA", a // 16, (a + n) // 16)
            mm([(b, win(MSL, 15), R("LASTF", a // 16, (a + n) // 16))] + sums(b, MST, "AB", a))
        act(R("CU", 2, 258), R("BA", 0, 256), AF.Sign, 0.5, -1.0)

    def comp():
        ts(R("KF"), R("KU"), -float(HALF), A.add)
        tt(R("EQ"), R("KF", 0, 256), R("KF", 256, 512), A.is_equal)
        z, b = R("BD", 0, 256), R("BE", 0, 256)
        mm([(b, ID[128.0], R("EQ"))], [(b, A0C, R("CU", 2, 258)), (b, A1, R("CU", 1, 257)), (b, TGE, R("CU", 0, 256))])
        mm([(z, ID[94.0], R("ONE"))], [(z, A0, R("CU", 2, 258)), (z, A1, R("CU", 1, 257)), (z, TGE, R("CU", 0, 256))])
        act(R("AP"), b, AF.Relu, -8192.0, 256.0)
        tt(R("CD", 1, 257), z, R("AP"), A.is_gt)
        mm([(R("BF", 0, 257), B1, R("CD", 0, 257))])
        x = R("BG", 0, 256)
        mm([(x, IDN, R("J1")), (x, ID[float(DUMP)], R("ONE"))], [(x, BN8, R("CD", 1, 257))])
        mm([(R("BH", 0, 256), TRX, R("CD", 1, 257))])
        scan(R("SC", 0, 257), R("BF", 0, 257), part(ZR, 0, 257), 1.0, A.add, A.add)
        tt(R("XX"), x, R("SC", 0, 256), A.max)
        ts(R("OPU"), relay(R("YX"), R("XX")), SGN, A.mult, -1.0, A.add)
        copy(I(R("JW", 0, DUMP + 256), R("OPU")), R("J1"))
        scan(R("JK"), R("JW", 0, 512), R("JW", 0, 512), 1.0, A.max, A.max)
        y = relay(R("YJ"), R("JK"))
        ts(R("JT"), y, SGN, A.mult, -1.0, A.add)
        act(R("JB"), y, AF.Identity, 0.0, SG16)
        tt(R("XC"), R("BH", 0, 256), R("SC", 0, 256), A.add)
        act(R("INV", 1, 33), KH, AF.Sign, R("SC", 256, 257), -1.0)
        tt(R("OO"), I(R("XC"), R("JT")), K1, A.is_equal)
        t = R("BD", 0, 32)
        mm([(t, IDN, R("JB"))], sums(t, MSI, "OO", 0))
        ts(R("T1"), t, -16.0, A.add)

    def qphase(r):
        rs = RD if r else []
        for a, n in QH:
            u, v = I(R("MRK"), R("KU", a // 16, (a + n) // 16)), I(R("MRK"), R("KU", 256 + a // 16, 256 + (a + n) // 16))
            if a in RC + rs:
                k = (RC + rs).index(a)
                qu, qv, b = R("QB", 1024 * k, 1024 * k + n), R("QB", 1024 * k + 512, 1024 * k + 512 + n), R("BE", 0, n)
                act(qv, v, AF.Identity, -float(CL))
                act(qu, u, AF.Identity, -float(CL))
                mm([(b, ID[-1.0], qv)], [(b, IDN, qu)])
                act(qu, b, AF.Relu)
                if a in RC:
                    x = R("BG", 0, n)
                    mm([(x, IDF, R("D", a, a + n))], [(x, IDN, R("CC", 0, n))], [(x, IDN, qv)], [(x, IDN, qu)])
                else:
                    mm([(b, IDN, qv)], [(b, IDN, qu)])
                    act(R("QV", a, a + n), b, AF.Identity, float(CL))
            else:
                act(R("QV", a, a + n), v, AF.Copy)
                tt(R("QV", a, a + n), u, R("QV", a, a + n), A.max)
        for c, (a, n) in enumerate(AH):
            if a not in RC:
                addto(R("D", a, a + n), R("QV", a, a + n), "ac%d" % c)
        signs = [c for c in range(8) if r == 0 or 512 * c in RC]
        for c in range(8):
            a, b = 512 * c, ("BB", "BC")[c % 2]
            if c in signs:
                mm([(R(b), B1, R("AB", a - 1, a + 511))])
                act(R("NS", a, a + 512), R(b), AF.Sign)
            else:
                mm([(R(b), B25, R("AB", a - 1, a + 511))])
                mm([(R(b, 0, 512, 16), ID[2.0 ** 24], R("ONE", 0, 32)), (R(b, 0, 512, 16), R24, R("CU", 1 + 32 * c, 33 + 32 * c))])
                scan(R("EM", a, a + 512), R(b), R("D", a, a + 512), R("EM", a - 1, a) if a else 0.0, A.min, A.add)
        b = R("BA", 256, 512)
        mm([(b, row(15, 1), R("CU", 1, 257))])
        for a, n in EH:
            if a // 512 in signs:
                act(R("NS", a, a + n, 16), part(b, a // 16, (a + n) // 16), AF.Relu, 0.0, -1.0)
                x = R("BG", 0, n) if a in RC else R("D", a, a + n)
                scan(R("EM", a, a + n), R("NS", a, a + n), x, R("EM", a - 1, a) if a else 0.0, A.mult, A.add)

    def kids(b, at):
        for a in range(0, P, 512):
            o, x = R(b, 1 + a, 513 + a), I(R("KDF"), R("KU", at + a // 16, at + a // 16 + 32))
            if at and a == P - 512:
                copy(o, x)
            else:
                act(o, x, AF.Copy)
                ops[-1]["late"] = -5000.0

    def pairs():
        gfill(R("UV", ZC, ZC + 1), 1)
        for i in range(16):
            b = R(("BB", "BC")[i % 2], 0, 256)
            mm([(b, row(i, 1), R("KF", 0, 256)), (b, row(i, 0), R("KF", 256, 512))])
            act(R("UV", 1 + i, 1 + P, 16), b, AF.Identity, float(4097 * HALF + 1))

    def fused(src, buf, base, lsem, rsem, ready=()):
        m = masks(me)
        tr, rd, tot = [], list(ready), 0
        dst = R(buf, base + CAP * me, base + CAP * me + CAP)
        for d in range(N):
            if d != me:
                rid, pid = topo.addr(cores[d])[:2]
                x = src(d)
                rd += x[1]
                tot += len(m[d])
                tr.append(RemoteDMATransfer(dst_ids=[DstId(rid=rid, pnc=pid)], dma_engine_mask=sum(1 << e for e in m[d]), remote_sem=T.sem[rsem], src=x[0], dst=dst[0]))
        put("g", lambda: g.remote_dma_fused(tr, local_sem=T.sem[lsem]), rd, [(lsem, 0, 1)], 400.0, 2900.0 if lsem == "lk0" else 1400.0, lsem, -tot)
        act(dst, src(me), AF.Copy)
        tot = sum(len(masks(s)[me]) for s in range(N) if s != me)
        put("n", None, [(lsem, 0, 1)], [(buf, base + CAP * s, base + CAP * s + CAP) for s in range(N) if s != me], 1.0, NET - 1800.0, rsem, tot)

    def keys(r):
        ts(R("ZI"), I(R("EM", 0, P), R("T1")), float(2 ** 30), A.min, -float(2 ** 30), A.max)
        for k in range(2):
            ts(R("Z8", k, 512, 2), R("ZI", k, 512, 2), 255, A.bitwise_and)
            ops[-1]["w"] = [("Z8", k, k + 1)]
        for k in range(2):
            copy(R("ZB", k, 512, 2), R("Z8", k, 512, 2))
            ops[-1]["r"], ops[-1]["w"] = [("Z8", k, k + 1)], [("ZB", k, k + 1)]
        h = R("BD", 0, 32)
        mm(sums(h, MSW, "ZB", 0)[0::2], sums(h, MSW, "ZB", 0)[1::2])
        for k in range(2):
            ops[k - 2]["r"] = MSW[1] + [("ZB", k, k + 1)]
        copy(R("HI"), h)
        ts(R("OW"), R("HI"), 3, A.bitwise_and)
        tt(R("OHB", 1, 145), I(R("OW"), R("REP", 0, 9)), part(OC, 0, 144), A.is_equal)
        k = R("BF", 0, 136)
        mm([(k, IDN, PADC)] + [(R("BF", 34 * o + 2, 34 * o + 34), ID[c], R("INV", a, a + 32)) for o in range(N) for c, a in ((-1024.0, 1), (1024.0, 0))],
           [(k, TRB, R("OHB", 1, 137)), (k, R("TGB"), R("OHB", 0, 136))])
        scan(R("RK"), RS, k, 0.0, A.mult, A.add)
        tt(R("R2", 0, 66), R("RK", 2, 68), R("RK", 70, 136), A.max)
        tt(R("RQ"), R("R2", 0, 32), R("R2", 34, 66), A.max)
        copy(R("OFF"), R("RQ"))
        copy(I(R("SND"), R("OFF")), R("ZB"))
        fused(lambda d: R("SND", 512 * d, 512 * d + CAP), "ARR", 256 * r, "lk%d" % r, "ka%d" % r,
              R("RPL", RW * r, RW * r + RW)[1])
        gfill(R("NXT", 0, 256), 0)
        act(R("LA"), I(R("EM", 0, P), R("T1")), AF.Identity, RND, 1.0 / CL)
        act(R("LR"), R("LA"), AF.Identity, -RND)
        t = R("BE")
        mm([(t, B1, R("JK")), (t, BI, R("OO")), (t, BL, R("LR"))])
        act(R("T0"), t, AF.Identity, -14.0)
        gfill(R("JW2", 0, 256), 0)
        copy(R("O3"), R("OW"))
        act(R("TH"), R("O3"), AF.Identity, 64.0, 512.0)
        act(R("O4"), R("O3"), AF.Identity, -256.0, -448.0)
        tt(R("SNT", 1, 33), R("RQ"), R("TH"), A.is_lt)
        tt(R("SLT"), R("RQ"), R("O4"), A.add)
        b, x, t = R("BG", 0, 33), R("BG", 64, 96), R("BG", 96, 128)
        mm([(x, IDN, R("J1", 0, 32)), (x, ID[float(RW)], R("ONE", 0, 32))],
           [(b, B1, R("SNT", 0, 33)), (x, BN8, R("SNT", 1, 33)), (t, TRX, R("SNT", 1, 33))])
        scan(R("SC2", 0, 33), b, part(ZR, 0, 33), 1.0, A.add, A.add)
        tt(R("X2"), x, R("SC2", 0, 32), A.max)
        ts(R("OP2"), relay(R("Y2"), R("X2")), SGN, A.mult, -1.0, A.add)
        tt(R("XC2"), t, R("SC2", 0, 32), A.add)
        copy(I(R("JW2"), R("OP2")), R("J1", 0, 32))
        scan(R("JK2"), R("JW2", 0, 256), R("JW2", 0, 256), 1.0, A.max, A.max)
        y = relay(R("YJ2"), R("JK2"))
        ts(R("JT2"), y, SGN, A.mult, -1.0, A.add)
        act(R("JB2"), y, AF.Identity, 0.0, SG16)
        tt(R("OO2"), I(R("XC2"), R("JT2")), part(K1, 0, 256), A.is_equal)
        act(R("SG"), I(R("SLT"), R("JT2")), AF.Copy)
        tt(R("PR"), R("OO2"), R("SG"), A.mult)
        t = R("BG", 0, 16)
        mm([(t, IDN, R("JB2"))], sums(t, MSI, "OO2", 0))
        ts(R("KS2"), t, -16.0, A.add)
        t = R("BF", 0, 16)
        mm(sums(t, MST, "PR", 0))
        ts(R("OFS"), t, 256.0, A.add)
        act(R("SG"), I(R("LR"), R("KS2")), AF.Relu, -1.0)
        act(R("LR2"), R("SG"), AF.Identity, 1.0)
        act(R("T2"), I(R("T0"), R("KS2")), AF.Copy)
        t = R("BG", 0, 16)
        mm(sums(t, MS, "LR2", 0))
        act(R("LN", 1, 17), t, AF.Copy)

    def owner(r):
        b = 256 * r
        arr = R("ARR", b, b + 256)
        pa, pb = R("BH", 0, 256), R("BH", 256, 512)
        mm([(pa, ID[-1024.0], R("ONE")), (pa, ID[0.5 - me / 4], R("ONE")), (pb, ID[1.0 - me / 4], R("ONE"))], [(pa, BW4, arr)], [(pb, BW4, arr)])
        act(R("NEG"), arr, AF.Relu, 0.0, -1.0)
        ts(R("RR"), pa, M11, A.add, M11, A.subtract)
        tt(R("P1"), pb, R("RR"), A.subtract)
        yp = relay(R("YP"), R("P1"))
        s, n = R("BA", 0, 256), R("BD", 0, 256)
        nq = R("NQ") if r else R("ONE")
        if r:
            ts(R("PU"), yp, SGN, A.mult, -1.0, A.add)
            tt(nq, I(R("STO"), R("PU")), arr, A.not_equal)
            mm([(s, ID[4096.0], R("ONE")), (s, BP8, R("NEG"))], [(s, BN4, nq)])
        else:
            mm([(s, ID[4096.0], R("ONE")), (s, BN4, nq)], [(s, BP8, R("NEG"))])
        copy(R("R1"), R("P1"))
        act(R("BE", 0, 256), R("P1"), AF.Identity, 0.0, -1.0)
        tt(R("PMR"), s, R("P1"), A.max)
        relay(R("YM"), R("PMR"))
        tt(R("ED"), R("YM"), R("BE", 0, 256), A.is_equal)
        eo = [[(n, ID[4096.0], R("ONE")), (n, BP8, R("NEG")), (n, BN4, nq)]]
        lo = 0
        es = []
        act(R("YB", 0, 16), R("YM", 15, 256, 16), AF.Identity, 0.5, NSG)
        act(R("YB", 16, 32), R("YM", 15, 256, 16), AF.Identity, 0.5, SGN)
        for m in range(15):
            k = 240 - 16 * m
            o = R("BD", 16 * m + 16, 256)
            if m < EV:
                ts(R("EO", lo, lo + k), R("R1", 16 * m + 16, 256), SGN, A.mult, R("YM", 16 * m + 15, 16 * m + 16), A.is_equal)
                eo.append([(o, BP17, R("EO", lo, lo + k))])
                lo += k
            else:
                act(R("EO", lo, lo + k), R("P1", 16 * m + 16, 256), AF.Sign, R("YB", m, m + 1))
                act(R("EO", lo + k, lo + 2 * k), R("P1", 16 * m + 16, 256), AF.Sign, R("YB", 16 + m, 17 + m), -1.0)
                es.append([(o, BP17, R("EO", lo, lo + k)), (o, BP17, R("EO", lo + k, lo + 2 * k))])
                lo += 2 * k
        eo.insert(6, [(n, BP17, R("ED"))])
        for x, e in enumerate(es):
            eo.insert(5 + 2 * x, e)
        mm(*eo)
        ts(R("NEW", b, b + 256), n, 0.0, A.is_le, 1.0, A.add)
        fused(lambda d: R("NEW", b + CAP * d, b + CAP * d + CAP), "RPL", RW * r, "lr%d" % r, "ra%d" % r)
        act(R("PF"), yp, AF.Abs)
        ts(R("S1"), relay(R("YN"), R("NEW", b, b + 256)), NSG, A.mult, 2.0, A.add)
        tt(R("S2"), R("S1"), KS, A.mult)
        tt(R("S3"), R("S2"), R("PF"), A.max)
        ts(R("SU"), R("S3"), -1.0, A.add)
        copy(I(R("STO"), R("SU")), arr)
        if r == RO - 1:
            dma("y", "st0", H(T.yt[:]), R("STO", 0, TS), 2 * TS)

    def nextfront(r):
        rp = R("RPL", RW * r, RW * r + RW)
        tt(R("NK"), I(rp, R("OFS")), R("LR2"), A.mult)
        n1, n0 = relay(R("YK", 16, 272), R("NK")), R("YK", 15, 256, 16)
        st, en, du = R("BF", 0, 16), R("BF", 16, 32), R("BF", 32, 48)
        l1, l0 = R("LN", 1, 17), R("LN", 0, 16)
        mm([(st, NTRS, l1), (st, NTGE, l0), (en, NTRI, l1), (en, NTGT, l0), (du, ID[8192.0], l1)],
           [(st, STRS, n1), (st, STGE, n0), (en, STRI, n1), (en, STGT, n0), (du, SID, n1)])
        scan(R("SE"), RS2, R("BF", 0, 32), 0.0, A.mult, A.add)
        tt(R("DU"), du, KD, A.add)
        tt(R("X1"), R("SE", 0, 16), R("DU"), A.max)
        copy(R("OF2"), R("X1"))
        ts(R("GF"), R("SE", 16, 32), 256.0, A.is_le, -1.0 / 8192, A.mult)
        tt(R("KB"), du, R("GF"), A.mult)
        mm([(R("BG", 0, 16), B1, R("KB"))])
        act(R("X3"), R("BG", 0, 16), AF.Identity, 512.0, -16384.0, R("TOB", 0, 1))
        act(R("F0"), IQ, AF.Relu, R("TOB", 0, 1), 16384.0)
        act(R("FA"), R("F0"), AF.Relu, 0.5, -1.0)
        copy(I(R("NXT"), R("OF2")), R("T2"))
        ts(R("FF"), IB, R("TOB", 0, 1), A.add, 1.0, A.max)
        scan(R("PP"), R("FF"), R("NXT", 0, 256), 0.0, A.add, A.max)
        ts(R("CT"), relay(R("YQ"), R("PP")), SGN, A.mult, float(ZC), A.min)
        act(R("NEG"), R("NXT", 0, 256), AF.Relu, 1.0, -1.0)
        mm([(R("BH", 0, 256), IDN, R("FA"))], [(R("BH", 0, 256), IDN, R("NEG"))])
        if r < RO - 1:
            act(R("MF", 0, P, 16), R("BH", 0, 256), AF.Relu, -2.0, 2.0)
        else:
            act(R("OUTF", 512, 768), R("BH", 0, 256), AF.Sign, 1.5, -1.0)
            ts(R("ZI", 0, 256), I(R("UV"), R("CT")), -1.0, A.add)
            ts(R("Z8", 0, 256), R("ZI", 0, 256), 4095, A.bitwise_and)
            copy(R("OUTF", 0, 256), R("Z8", 0, 256))
            act(R("GU"), I(R("UV"), R("CT")), AF.Identity, -0.5, 2.0 ** -12)
            act(R("YU"), R("GU"), AF.Identity, RND)
            act(R("OUTF", 256, 512), R("YU"), AF.Identity, -RND)
            for k, (q, y) in enumerate((("y", T.yu), ("s", T.yv), ("y", T.ys))):
                dma(q, "st%d" % (k + 1), H(y[:]), R("OUTF", 256 * k, 256 * k + 256, p=(0, 128, 16)), 64)

    for r in range(RO):
        vphase(r)
        comp()
        qphase(r)
        if r < RO - 1:
            kids("UV", 0)
        else:
            pairs()
        keys(r)
        if r < RO - 1:
            kids("QV", 256)
        owner(r)
        nextfront(r)
        if r == 0:
            rows()

    n = len(ops)

    def depends(wide):
        recs = {}
        pred = []
        for x, o in enumerate(ops):
            ps = set()
            rw = [o["r"], o["w"]]
            for k in range(2):
                rw[k] = [(b, lo // wide[b] * wide[b], -(-hi // wide[b]) * wide[b]) if b in wide else (b, lo, hi) for b, lo, hi in rw[k]]
                for (b, lo, hi) in rw[k]:
                    for rec in recs.get(b, []):
                        if rec[0] < hi and lo < rec[1] and (k or rec[2] or (b in BANKS and ops[rec[3]]["q"] != o["q"])):
                            ps.add(rec[3])
            pred.append(ps)
            for (b, lo, hi) in rw[1]:
                recs[b] = [r for r in recs.get(b, []) if b in wide or not (lo <= r[0] and r[1] <= hi)] + [(lo, hi, True, x)]
            for (b, lo, hi) in rw[0]:
                recs.setdefault(b, []).append((lo, hi, False, x))
        return pred

    def chained(y, x):
        return ops[x]["ch"] and ops[y]["q"] == "t" and ops[y]["w"] == ops[x]["w"]

    def arrange():
        pred = [a | b for a, b in zip(depends({}), depends({"ARR": 256, "NEW": 256, "RPL": RW, "SND": 4096}))]
        for x in range(n):
            pred[x] = set(y for y in pred[x] if ops[x]["q"] != "g" or ops[y]["q"] != "g" or not ops[x]["w"] or not ops[y]["w"]
                          or ops[x]["w"][0][0] != "SND" or ops[y]["w"][0][0] != "SND")
        succ = [set() for _ in range(n)]
        for x in range(n):
            for y in pred[x]:
                succ[y].add(x)
        hs = [[o["hold"][m] for o in ops] for m in range(len(PACE))]
        lat = [o["lat"] for o in ops]
        load = [o["load"] for o in ops]
        arcs = [[(y, 0.0 if chained(y, x) else WAKE) for y in pred[x]] for x in range(n)]
        qn = ["vstgyn".index(o["q"]) for o in ops]
        rank = [0.0] * n
        for x in range(n - 1, -1, -1):
            rank[x] += hs[0][x] + lat[x] + load[x] + ops[x].get("up", 0.0)
            for y, d in arcs[x]:
                rank[y] = max(rank[y], rank[x] + d)
        at, end, busy, dfree = [0.0] * n, [0.0] * n, [[] for _ in range(6)], 0.0
        key = [(0, x) if x < NLOAD else (1, ops[x].get("late", 0.0) - rank[x], x) for x in range(n)]
        left = [len(p) for p in pred]
        ready = [x for x in range(n) if not left[x]]
        while ready:
            x = min(ready, key=lambda x: key[x])
            ready.remove(x)
            for y in succ[x]:
                left[y] -= 1
                if not left[y]:
                    ready.append(y)
            h = hs[0][x]
            t = max([end[y] + d for y, d in arcs[x]] + [0.0])
            lst = busy[qn[x]]
            a = 0
            while a < len(lst) and lst[a][1] <= t:
                a += 1
            while a < len(lst) and lst[a][0] < t + h:
                t = lst[a][1]
                a += 1
            lst.insert(a, (t, t + h))
            at[x] = t
            end[x] = t + h + lat[x] + load[x]
            if load[x] and x < NSET:
                dfree = max(t + lat[x] / 2, dfree) + load[x]
                end[x] = dfree + lat[x] / 2
        seq = sorted(range(n), key=lambda x: (at[x], x))

        def run(m, st, lo):
            h = hs[m]
            end, fre, dma_ = st
            fr = [0.0] * 6
            df = dma_[seq[lo - 1]] if lo else 0.0
            seen = 0
            k = lo - 1
            while k >= 0 and seen & 15 != 15:
                x = seq[k]
                if not seen >> qn[x] & 1:
                    seen |= 1 << qn[x]
                    fr[qn[x]] = fre[x]
                k -= 1
            for k in range(lo, n):
                x = seq[k]
                t = fr[qn[x]]
                for y, d in arcs[x]:
                    u = end[y] + d
                    if u > t:
                        t = u
                fre[x] = fr[qn[x]] = t + h[x]
                if load[x]:
                    df = max(t + lat[x] / 2, df) + load[x]
                    end[x] = df + lat[x] / 2
                else:
                    end[x] = t + h[x] + lat[x]
                dma_[x] = df
            return max(end[x] for x in seq[-60:])
        cur = [[[0.0] * n for _ in range(3)] for _ in PACE]
        val = sum(w * run(m, cur[m], 0) for m, w in enumerate(WEIGHT))
        least, keep = val, list(seq)

        def tight(m):
            end, fre = cur[m][0], cur[m][1]
            before, last = [None] * n, [None] * 6
            for x in seq:
                before[x], last[qn[x]] = last[qn[x]], x
            x = max(seq[-60:], key=lambda x: end[x])
            res = []
            while x is not None and x >= NLOAD:
                t = fre[x] - hs[m][x]
                y = next((y for y, d in arcs[x] if end[y] + d >= t - 0.01), None)
                if y is None:
                    y = before[x]
                    if y is not None and y >= NLOAD:
                        res += [(x, -1), (y, 1)]
                x = y
            return res
        z = SEED
        hot = []
        for it in range(TRIES):
            if it % 40 == 0:
                hot = tight(it // 40 % len(PACE))
            z = (z * 1103515245 + 12345) % 2147483648
            if z >> 10 & 3 and hot:
                x, step = hot[(z >> 12) % len(hot)]
                a = seq.index(x)
            else:
                a = NLOAD + (z >> 12) % (n - NLOAD)
                step = 1 if z >> 9 & 1 else -1
            z = (z * 1103515245 + 12345) % 2147483648
            far = 1 + (z >> 8) % 4
            x = seq[a]
            near = succ[x] if step > 0 else pred[x]
            b = a
            while far and NLOAD <= b + step < n and seq[b + step] not in near:
                b += step
                if qn[seq[b]] == qn[x]:
                    far -= 1
            while b != a and qn[seq[b]] != qn[x]:
                b -= step
            if b == a:
                continue
            seq.insert(b, seq.pop(a))
            lo = min(a, b)
            new_ = [[list(y) for y in c] for c in cur]
            v = sum(w * run(m, new_[m], lo) for m, w in enumerate(WEIGHT))
            z = (z * 1103515245 + 12345) % 2147483648
            if v <= val - HEAT * (1 - it / TRIES) * math.log((z + 1) / 2147483648):
                val, cur = v, new_
                if v < least:
                    least, keep = v, list(seq)
            else:
                seq.insert(a, seq.pop(b))
        return keep

    if n not in ORDER:
        ORDER[n] = arrange()

    pred = depends({})
    count = {}
    known = {q: {} for q in queues}
    waited = {}
    token = {}
    for x in ORDER[n]:
        o = ops[x]
        q = o["q"]
        s = o["sem"]
        count[s] = count.get(s, 0) + abs(o["inc"])
        if q == "n":
            token[x] = (s, count[s], {s: count[s]})
            continue
        best = {}
        for y in pred[x]:
            if chained(y, x):
                continue
            a, v, clk = token[y]
            if known[q].get(a, 0) < v and best.get(a, (0, None))[0] < v:
                best[a] = (v, clk)
        for a in sorted(best, key=lambda a: -sum(best[a][1].values())):
            v, clk = best[a]
            if known[q].get(a, 0) >= v:
                continue
            queues[q].wait_ge(T.sem[a], v)
            waited[a] = max(waited.get(a, 0), v)
            known[q][a] = v
            for b, u in clk.items():
                known[q][b] = max(known[q].get(b, 0), u)
        ins = o["fn"]()
        if o["inc"] > 0:
            ins.then_inc(T.sem[s], o["inc"])
        clk = dict(known[q])
        clk[s] = count[s]
        token[x] = (s, count[s], clk)
    for s in sorted(count):
        if waited.get(s, 0) < count[s]:
            g.wait_ge(T.sem[s], count[s])
